import numpy as np
import ml_dtypes


def mxq(x, axis, fmt="e4m3"):
    dtype, down = {"e4m3": (ml_dtypes.float8_e4m3fn, 7), "e5m2": (ml_dtypes.float8_e5m2, 14)}[fmt]
    v = np.moveaxis(np.asarray(x, np.float32).astype(ml_dtypes.bfloat16).astype(np.float64), axis, -1)
    blocks = v.reshape(v.shape[:-1] + (-1, 32))
    amax = np.abs(blocks).max(-1, keepdims=True)
    byte = np.maximum(np.where(amax > 0, np.frexp(amax)[1] - 1 + 127, 0) - down, 1)
    scale = np.exp2(byte - 127.0)
    codes = (blocks / scale).astype(np.float32).astype(dtype).astype(np.float64)
    return np.moveaxis((codes * scale).reshape(v.shape), -1, axis)


WIDE = False


def mx_kscale(k):
    if not WIDE:
        return np.ones(k)
    levels = np.array([10, -10, 5, -5, 0])
    if k % 512:
        return np.exp2(np.random.permutation(np.resize(levels, k // 32))).repeat(32)
    a = np.empty((k // 512, 16))
    for p in range(k // 512):
        a[p, :8] = np.random.permutation(np.resize(levels, 8))
        for g in range(8):
            far = levels[np.abs(levels - a[p, g]) >= 10]
            a[p, g + 8] = far[np.random.randint(len(far))]
    return np.exp2(a.ravel()).repeat(32)


def f64(x):
    return np.asarray(x).astype(np.float64)


def striped(idx):
    return np.tile(idx.reshape(-1, 16).T, (8, 1)).astype(np.uint16)


def unstriped(offs):
    return offs[:16].T.reshape(-1).astype(np.int64)


def pack_weight(w):
    k, n = w.shape
    w = f64(np.asarray(w, np.float32).astype(ml_dtypes.bfloat16)).reshape(k // 32, 32, n)
    amax = np.abs(w).max(1)
    byte = np.clip(np.where(amax > 0, np.frexp(amax)[1] - 1 + 127 - 7, 1), 1, 254)
    scaled = (w * np.exp2(127.0 - byte)[:, None, :]).reshape(k, n).astype(np.float32)
    words = np.ascontiguousarray(scaled.reshape(k // 512, 128, 4, n).transpose(0, 1, 3, 2)).astype(ml_dtypes.float8_e4m3fn).view(np.uint8)
    return words, np.ascontiguousarray(byte.astype(np.uint8).reshape(k // 512, 16, n))


def unpack_weight(words, scales):
    g, p, n, _ = words.shape
    vals = np.ascontiguousarray(words).view(ml_dtypes.float8_e4m3fn).astype(np.float64) * np.repeat(np.exp2(scales.astype(np.float64) - 127.0), 8, axis=1)[..., None]
    return vals.transpose(0, 1, 3, 2).reshape(g * 512, n)


def planes(y):
    n, m = y.shape
    v = y.astype(np.float32).astype(ml_dtypes.bfloat16).astype(np.float64).reshape(n // 32, 32, m)
    top = np.abs(v).max(1)
    byte = np.clip(np.where(top > 0, np.frexp(top)[1] - 1 + 127 - 7, 1), 1, 254)
    codes = (v * np.exp2(127.0 - byte)[:, None, :]).reshape(n, m).astype(np.float32).astype(ml_dtypes.float8_e4m3fn).view(np.uint8)
    words = codes.reshape(n // 512, 128, 4, m).transpose(0, 1, 3, 2)
    return np.ascontiguousarray(words), np.ascontiguousarray(byte.astype(np.uint8).reshape(n // 512, 16, m))


K, T, S, N, R = 512, 4096, 1024, 512, 256


def setup_inputs():
    n = np.random.standard_normal
    s = mx_kscale(K)[:, None]
    packed_xT = pack_weight(n((K, T)) * s)
    return {
        "x_words": packed_xT[0],
        "x_scales": packed_xT[1],
        "w1": (n((K, N)) / np.sqrt(K) / s).astype(np.float32),
        "gam": (np.random.uniform(0.5, 1.5, (N, R))).astype(np.float32),
        "bet": (0.5 * n((N, R))).astype(np.float32),
        "offs": striped(np.random.permutation(T)[:S]),
        "lab": striped(np.random.permutation(np.concatenate([np.arange(R), np.random.randint(0, R, S - R)]))),
    }


def reference(x_words, x_scales, w1, gam, bet, offs, lab):
    xq = unpack_weight(x_words, x_scales)[:, unstriped(offs)]
    y = mxq(f64(w1), 0, "e4m3").T @ xq
    my = y.mean(axis=1, keepdims=True)
    dy = y - my
    qy = (dy) ** 2
    sy = np.sqrt(qy.mean(axis=1, keepdims=True) + 1e-4)
    out_0 = (dy / sy) * f64(gam)[:, unstriped(lab)] + f64(bet)[:, unstriped(lab)]
    return (out_0,) + planes(out_0)

@@ -1,0 +1,203 @@
+from contextlib import ExitStack
+
+import concourse.mybir as mybir
+
+F32 = mybir.dt.float32
+BF16 = mybir.dt.bfloat16
+U32 = mybir.dt.uint32
+I32 = mybir.dt.int32
+U16 = mybir.dt.uint16
+U8 = mybir.dt.uint8
+FP8X4 = mybir.dt.float8_e4m3fn_x4
+ACT = mybir.ActivationFunctionType
+ALU = mybir.AluOpType
+
+K, T, S, N, R = 512, 4096, 1024, 512, 256
+P = 128
+PACK = 4
+HALF = 512
+TABLE_W = 528
+EPS = 1e-4
+EARLY = (0, 1)
+FUSED = (2, 3)
+CHUNKS = (256, 256, 256, 128, 128)
+FLOPS = 2 * K * N * S
+
+
+def tile_picked_yspade_none_po_kernel(
+    tc, x_words, x_scales, w1, gam, bet, offs, lab, out_0, out_1, out_2
+):
+    nc = tc.nc
+    with ExitStack() as ctx:
+        keep = ctx.enter_context(tc.tile_pool(name="keep", bufs=1))
+        ring = ctx.enter_context(tc.tile_pool(name="ring", bufs=4))
+        psum = ctx.enter_context(tc.psum_pool(name="psum", bufs=1))
+
+        lab_t = keep.tile([P, S // 16], U16, name="lab_t")
+        offs_t = keep.tile([P, S // 16], U16, name="offs_t")
+        gam_t = [keep.tile([P, TABLE_W], F32, name=f"gam{t}") for t in range(PACK)]
+        bet_t = [keep.tile([P, TABLE_W], F32, name=f"bet{t}") for t in range(PACK)]
+        xw = keep.tile([P, T], U32, name="xw")
+        xs = keep.tile([P, T], U8, name="xs")
+        w_raw = [keep.tile([P, PACK, N // 2], F32, name=f"w_raw{h}") for h in range(2)]
+        gam_rows = gam.rearrange("(p t) r -> p t r", t=PACK)
+        bet_rows = bet.rearrange("(p t) r -> p t r", t=PACK)
+        w_rows = w1.rearrange("(p j) n -> p j n", j=PACK)
+
+        nc.vector.memset(xs[:].bitcast(I32), 0)
+        for table in [gam_t[t] for t in EARLY] + [bet_t[t] for t in EARLY]:
+            nc.gpsimd.memset(table[:, R:], 0.0)
+        warm = keep.tile([P, 2], F32, name="warm")
+        nc.gpsimd.memset(warm[:, 0:1], 1.0)
+        nc.scalar.activation(warm[:, 1:2], warm[:, 0:1], ACT.Abs_reciprocal_sqrt)
+
+        nc.sync.dma_start(lab_t[:], lab)
+        for t in EARLY[:2]:
+            nc.sync.dma_start(gam_t[t][:, :R], gam_rows[:, t, :])
+        nc.sync.dma_start(offs_t[:], offs)
+        nc.sync.dma_start(xw[:].bitcast(I32), x_words[0].rearrange("p n t -> p (n t)").bitcast(I32))
+        for q in range(4):
+            nc.scalar.dma_start(xs[32 * q : 32 * q + 4, :].bitcast(I32), x_scales[0, 4 * q : 4 * q + 4, :].bitcast(I32))
+        for h in range(2):
+            nc.sync.dma_start(w_raw[h][:], w_rows[:, :, h * (N // 2) : (h + 1) * (N // 2)])
+        for t in EARLY:
+            nc.sync.dma_start(bet_t[t][:, :R], bet_rows[:, t, :])
+        for t in FUSED:
+            nc.sync.dma_start(gam_t[t][:, :R], gam_rows[:, t, :])
+            nc.sync.dma_start(bet_t[t][:, :R], bet_rows[:, t, :])
+
+        def entries(lst, lo, hi):
+            return lst[:, lo // 16 : hi // 16]
+
+        def look_up(table, picked):
+            for lo in range(0, S, HALF):
+                nc.vector.tensor_copy(picked[:, lo : lo + HALF], table[:].indirect(entries(lab_t, lo, lo + HALF)))
+
+        g_px = keep.tile([P, len(EARLY), S], F32, name="g_px")
+        for i, t in enumerate(EARLY):
+            look_up(gam_t[t], g_px[:, i, :])
+
+        x_codes = []
+        x_bytes = []
+        for h in range(2):
+            x_codes.append(keep.tile([P, HALF], U32, name=f"x_codes{h}", align_bytes=64))
+            x_bytes.append(keep.tile([P, HALF], U8, name=f"x_bytes{h}", align_bytes=64))
+            picks = entries(offs_t, h * HALF, (h + 1) * HALF)
+            nc.vector.tensor_copy(x_codes[h][:], xw[:].indirect(picks))
+            nc.vector.tensor_copy(x_bytes[h][:], xs[:].indirect(picks))
+
+        w_bf = keep.tile([P, PACK, P, PACK], BF16, name="w_bf", tag="stage", align_bytes=64)
+        for h in range(2):
+            nc.scalar.copy(
+                w_bf[:, :, h * (P // 2) : (h + 1) * (P // 2), :].rearrange("p t m j -> p m j t"),
+                w_raw[h][:].rearrange("p j (m t) -> p m j t", t=PACK),
+            )
+        w_codes = keep.tile([P, N], U32, name="w_codes", align_bytes=64)
+        w_scales = keep.tile([P, N], U8, name="w_scales", align_bytes=64)
+        nc.vector.quantize_mx(
+            out=w_codes[:].bitcast(FP8X4), scales=w_scales[:], in_=w_bf[:].rearrange("p t m j -> p (t m j)")
+        )
+        b_px = keep.tile([P, len(EARLY), S], F32, name="b_px", tag="stage", align_bytes=64)
+        for i, t in enumerate(EARLY):
+            look_up(bet_t[t], b_px[:, i, :])
+
+        order = FUSED[:1] + EARLY + FUSED[1:]
+        y = {}
+        for t in order:
+            for h in range(2):
+                y[t, h] = psum.tile([P, HALF], F32, name=f"y{t}{h}")
+                nc.tensor.matmul_mx(
+                    out=y[t, h][:],
+                    lhsT=w_codes[:, t * P : (t + 1) * P].bitcast(FP8X4),
+                    lhsT_scale=w_scales[:, t * P : (t + 1) * P],
+                    rhs=x_codes[h][:].bitcast(FP8X4),
+                    rhs_scale=x_bytes[h][:],
+                    start=True,
+                    stop=True,
+                )
+
+        def col(name):
+            return keep.tile([P, 1], F32, name=name)
+
+        starts = [sum(CHUNKS[:c]) for c in range(len(CHUNKS))]
+        res = [keep.tile([P, PACK, width], F32, name=f"res{c}") for c, width in enumerate(CHUNKS)]
+        out_codes = keep.tile([P, S], U32, name="out_codes", align_bytes=64)
+        out_scales = keep.tile([P, S], U8, name="out_scales", align_bytes=64)
+        out_rows = out_0.rearrange("(p t) j -> p t j", t=PACK)
+        word_rows = out_1[0].rearrange("p n t -> p (n t)").bitcast(I32)
+
+        def mean_of(t, y_sb):
+            sums = [col(f"sum{t}{h}") for h in range(2)]
+            for h in range(2):
+                nc.scalar.activation(y_sb[:, h * HALF : (h + 1) * HALF], y[t, h][:], ACT.Copy, accum_out=sums[h][:])
+            part_mean = col(f"pm{t}")
+            nc.scalar.activation(part_mean[:], sums[0][:], ACT.Copy, scale=-1.0 / S)
+            neg_mean = col(f"nm{t}")
+            nc.scalar.activation(neg_mean[:], sums[1][:], ACT.Identity, scale=-1.0 / S, bias=part_mean[:])
+            return neg_mean
+
+        def rstd_of(t, y_sb, neg_mean):
+            sq = col(f"sq{t}")
+            junk = ring.tile([P, S], BF16, name="junk")
+            nc.scalar.activation(junk[:], y_sb[:], ACT.Square, bias=neg_mean[:], accum_out=sq[:])
+            rstd = col(f"rs{t}")
+            nc.scalar.activation(rstd[:], sq[:], ACT.Abs_reciprocal_sqrt, scale=1.0 / S, bias=EPS)
+            return rstd
+
+        def finish(c):
+            cols = slice(starts[c], starts[c] + CHUNKS[c])
+            nc.sync.dma_start(out_rows[:, :, cols], res[c][:])
+            res_bf = keep.tile([P, CHUNKS[c], PACK], BF16, name=f"res_bf{c}", align_bytes=64)
+            nc.scalar.copy(
+                res_bf[:].rearrange("p (c i) t -> p c t i", i=4), res[c][:].rearrange("p t (c i) -> p c t i", i=4)
+            )
+            nc.vector.quantize_mx(
+                out=out_codes[:, cols].bitcast(FP8X4),
+                scales=out_scales[:, cols],
+                in_=res_bf[:].rearrange("p n t -> p (n t)"),
+            )
+            nc.sync.dma_start(word_rows[:, cols], out_codes[:, cols].bitcast(I32))
+
+        for t in order:
+            scaled = keep.tile([P, S], F32, name=f"scaled{t}")
+            y_sb = keep.tile([P, S], F32, name=f"y_sb{t}")
+            neg_mean = mean_of(t, y_sb)
+            rstd = rstd_of(t, y_sb, neg_mean)
+            if t in EARLY:
+                i = EARLY.index(t)
+                for h in range(2):
+                    cols = slice(h * HALF, (h + 1) * HALF)
+                    nc.vector.scalar_tensor_tensor(
+                        scaled[:, cols], y[t, h][:], neg_mean[:], g_px[:, i, cols], ALU.add, ALU.mult
+                    )
+                for c, width in enumerate(CHUNKS):
+                    cols = slice(starts[c], starts[c] + width)
+                    nc.vector.scalar_tensor_tensor(
+                        res[c][:, t, :], scaled[:, cols], rstd[:], b_px[:, i, cols], ALU.mult, ALU.add
+                    )
+                continue
+            gain = keep.tile([P, TABLE_W], F32, name=f"gain{t}")
+            shift = keep.tile([P, TABLE_W], F32, name=f"shift{t}")
+            nc.gpsimd.memset(gain[:, R:], 0.0)
+            nc.gpsimd.memset(shift[:, R:], 0.0)
+            nc.scalar.activation(gain[:, :R], gam_t[t][:, :R], ACT.Copy, scale=rstd[:])
+            nc.vector.scalar_tensor_tensor(shift[:, :R], gain[:, :R], neg_mean[:], bet_t[t][:, :R], ALU.mult, ALU.add)
+            last = t == order[-1]
+            pieces = list(zip(starts, CHUNKS)) if last else [(0, HALF), (HALF, HALF)]
+            for lo, width in pieces:
+                cols = slice(lo, lo + width)
+                nc.vector.tensor_tensor(
+                    scaled[:, cols], gain[:].indirect(entries(lab_t, lo, lo + width)), y_sb[:, cols], ALU.mult
+                )
+                for c in range(len(CHUNKS)):
+                    if lo <= starts[c] < lo + width:
+                        cols = slice(starts[c], starts[c] + CHUNKS[c])
+                        nc.vector.tensor_tensor(
+                            res[c][:, t, :], shift[:].indirect(entries(lab_t, cols.start, cols.stop)), scaled[:, cols], ALU.add
+                        )
+                        if last:
+                            finish(c)
+
+        for q in range(4):
+            queue = nc.sync if q % 2 else nc.scalar
+            queue.dma_start(out_2[0, 4 * q : 4 * q + 4, :].bitcast(I32), out_scales[32 * q : 32 * q + 4, :].bitcast(I32))

@@ -16,10 +16,9 @@ K, T, S, N, R = 512, 4096, 1024, 512, 256
 P = 128
 PACK = 4
 HALF = 512
-TABLE_W = 528
+TABLE_W = 1376
 EPS = 1e-4
-EARLY = (0, 1)
-FUSED = (2, 3)
+EARLY = 2
 CHUNKS = (256, 256, 256, 128, 128)
 FLOPS = 2 * K * N * S
 
@@ -45,14 +44,12 @@ def tile_picked_yspade_none_po_kernel(
         w_rows = w1.rearrange("(p j) n -> p j n", j=PACK)
 
         nc.vector.memset(xs[:].bitcast(I32), 0)
-        for table in [gam_t[t] for t in EARLY] + [bet_t[t] for t in EARLY]:
-            nc.gpsimd.memset(table[:, R:], 0.0)
         warm = keep.tile([P, 2], F32, name="warm")
-        nc.gpsimd.memset(warm[:, 0:1], 1.0)
+        nc.vector.memset(warm[:, 0:1], 1.0)
         nc.scalar.activation(warm[:, 1:2], warm[:, 0:1], ACT.Abs_reciprocal_sqrt)
 
         nc.sync.dma_start(lab_t[:], lab)
-        for t in EARLY[:2]:
+        for t in range(EARLY):
             nc.sync.dma_start(gam_t[t][:, :R], gam_rows[:, t, :])
         nc.sync.dma_start(offs_t[:], offs)
         nc.sync.dma_start(xw[:].bitcast(I32), x_words[0].rearrange("p n t -> p (n t)").bitcast(I32))
@@ -60,31 +57,22 @@ def tile_picked_yspade_none_po_kernel(
             nc.scalar.dma_start(xs[32 * q : 32 * q + 4, :].bitcast(I32), x_scales[0, 4 * q : 4 * q + 4, :].bitcast(I32))
         for h in range(2):
             nc.sync.dma_start(w_raw[h][:], w_rows[:, :, h * (N // 2) : (h + 1) * (N // 2)])
-        for t in EARLY:
-            nc.sync.dma_start(bet_t[t][:, :R], bet_rows[:, t, :])
-        for t in FUSED:
+        for t in range(EARLY, PACK):
             nc.sync.dma_start(gam_t[t][:, :R], gam_rows[:, t, :])
+        for t in range(PACK):
             nc.sync.dma_start(bet_t[t][:, :R], bet_rows[:, t, :])
-
-        def entries(lst, lo, hi):
-            return lst[:, lo // 16 : hi // 16]
 
         def look_up(table, picked):
-            for lo in range(0, S, HALF):
-                nc.vector.tensor_copy(picked[:, lo : lo + HALF], table[:].indirect(entries(lab_t, lo, lo + HALF)))
+            nc.vector.tensor_copy(picked, table[:].indirect(lab_t[:]))
 
-        g_px = keep.tile([P, len(EARLY), S], F32, name="g_px")
-        for i, t in enumerate(EARLY):
-            look_up(gam_t[t], g_px[:, i, :])
+        early = keep.tile([P, EARLY, S], F32, name="early")
+        for t in range(EARLY):
+            look_up(gam_t[t], early[:, t, :])
 
-        x_codes = []
-        x_bytes = []
-        for h in range(2):
-            x_codes.append(keep.tile([P, HALF], U32, name=f"x_codes{h}", align_bytes=64))
-            x_bytes.append(keep.tile([P, HALF], U8, name=f"x_bytes{h}", align_bytes=64))
-            picks = entries(offs_t, h * HALF, (h + 1) * HALF)
-            nc.vector.tensor_copy(x_codes[h][:], xw[:].indirect(picks))
-            nc.vector.tensor_copy(x_bytes[h][:], xs[:].indirect(picks))
+        x_codes = keep.tile([P, S], U32, name="x_codes", align_bytes=64)
+        x_bytes = keep.tile([P, S], U8, name="x_bytes", align_bytes=64)
+        nc.vector.tensor_copy(x_bytes[:], xs[:].indirect(offs_t[:]))
+        nc.vector.tensor_copy(x_codes[:], xw[:].indirect(offs_t[:]))
 
         w_bf = keep.tile([P, PACK, P, PACK], BF16, name="w_bf", tag="stage", align_bytes=64)
         for h in range(2):
@@ -97,21 +85,23 @@ def tile_picked_yspade_none_po_kernel(
         nc.vector.quantize_mx(
             out=w_codes[:].bitcast(FP8X4), scales=w_scales[:], in_=w_bf[:].rearrange("p t m j -> p (t m j)")
         )
-        b_px = keep.tile([P, len(EARLY), S], F32, name="b_px", tag="stage", align_bytes=64)
-        for i, t in enumerate(EARLY):
-            look_up(bet_t[t], b_px[:, i, :])
+        late = keep.tile([P, 2 * PACK - EARLY, S], F32, name="late", tag="stage", align_bytes=64)
+        g_px = [early[:, t, :] if t < EARLY else late[:, t - EARLY, :] for t in range(PACK)]
+        b_px = [late[:, PACK - EARLY + t, :] for t in range(PACK)]
+        for t in range(EARLY, PACK):
+            look_up(gam_t[t], g_px[t])
+        for t in range(PACK):
+            look_up(bet_t[t], b_px[t])
 
-        order = FUSED[:1] + EARLY + FUSED[1:]
-        y = {}
-        for t in order:
+        y = psum.tile([P, PACK, S], F32, name="y")
+        for t in range(PACK):
             for h in range(2):
-                y[t, h] = psum.tile([P, HALF], F32, name=f"y{t}{h}")
                 nc.tensor.matmul_mx(
-                    out=y[t, h][:],
+                    out=y[:, t, h * HALF : (h + 1) * HALF],
                     lhsT=w_codes[:, t * P : (t + 1) * P].bitcast(FP8X4),
                     lhsT_scale=w_scales[:, t * P : (t + 1) * P],
-                    rhs=x_codes[h][:].bitcast(FP8X4),
-                    rhs_scale=x_bytes[h][:],
+                    rhs=x_codes[:, h * HALF : (h + 1) * HALF].bitcast(FP8X4),
+                    rhs_scale=x_bytes[:, h * HALF : (h + 1) * HALF],
                     start=True,
                     stop=True,
                 )
@@ -119,37 +109,46 @@ def tile_picked_yspade_none_po_kernel(
         def col(name):
             return keep.tile([P, 1], F32, name=name)
 
-        starts = [sum(CHUNKS[:c]) for c in range(len(CHUNKS))]
-        res = [keep.tile([P, PACK, width], F32, name=f"res{c}") for c, width in enumerate(CHUNKS)]
+        neg_mean = []
+        squares = keep.tile([P, PACK], F32, name="squares")
+        for t in range(PACK):
+            y_sb = ring.tile([P, S], F32, name="y_sb")
+            sums = [col(f"sum{t}{h}") for h in range(2)]
+            for h in range(2):
+                cols = slice(h * HALF, (h + 1) * HALF)
+                nc.scalar.activation(y_sb[:, cols], y[:, t, cols], ACT.Copy, accum_out=sums[h][:])
+            part_mean = col(f"pm{t}")
+            nc.scalar.activation(part_mean[:], sums[0][:], ACT.Copy, scale=-1.0 / S)
+            neg_mean.append(col(f"nm{t}"))
+            nc.scalar.activation(neg_mean[t][:], sums[1][:], ACT.Identity, scale=-1.0 / S, bias=part_mean[:])
+            junk = ring.tile([P, S], BF16, name="junk")
+            nc.scalar.activation(junk[:], y_sb[:], ACT.Square, bias=neg_mean[t][:], accum_out=squares[:, t : t + 1])
+        rstd = keep.tile([P, PACK], F32, name="rstd")
+        nc.scalar.activation(rstd[:], squares[:], ACT.Abs_reciprocal_sqrt, scale=1.0 / S, bias=EPS)
+
         out_codes = keep.tile([P, S], U32, name="out_codes", align_bytes=64)
         out_scales = keep.tile([P, S], U8, name="out_scales", align_bytes=64)
         out_rows = out_0.rearrange("(p t) j -> p t j", t=PACK)
         word_rows = out_1[0].rearrange("p n t -> p (n t)").bitcast(I32)
 
-        def mean_of(t, y_sb):
-            sums = [col(f"sum{t}{h}") for h in range(2)]
-            for h in range(2):
-                nc.scalar.activation(y_sb[:, h * HALF : (h + 1) * HALF], y[t, h][:], ACT.Copy, accum_out=sums[h][:])
-            part_mean = col(f"pm{t}")
-            nc.scalar.activation(part_mean[:], sums[0][:], ACT.Copy, scale=-1.0 / S)
-            neg_mean = col(f"nm{t}")
-            nc.scalar.activation(neg_mean[:], sums[1][:], ACT.Identity, scale=-1.0 / S, bias=part_mean[:])
-            return neg_mean
-
-        def rstd_of(t, y_sb, neg_mean):
-            sq = col(f"sq{t}")
-            junk = ring.tile([P, S], BF16, name="junk")
-            nc.scalar.activation(junk[:], y_sb[:], ACT.Square, bias=neg_mean[:], accum_out=sq[:])
-            rstd = col(f"rs{t}")
-            nc.scalar.activation(rstd[:], sq[:], ACT.Abs_reciprocal_sqrt, scale=1.0 / S, bias=EPS)
-            return rstd
-
-        def finish(c):
-            cols = slice(starts[c], starts[c] + CHUNKS[c])
-            nc.sync.dma_start(out_rows[:, :, cols], res[c][:])
-            res_bf = keep.tile([P, CHUNKS[c], PACK], BF16, name=f"res_bf{c}", align_bytes=64)
+        lo = 0
+        for c, width in enumerate(CHUNKS):
+            cols = slice(lo, lo + width)
+            lo = lo + width
+            scaled = keep.tile([P, PACK, width], F32, name="scaled", bufs=2)
+            res = keep.tile([P, PACK, width], F32, name=f"res{c}")
+            for t in range(PACK):
+                nc.vector.scalar_tensor_tensor(
+                    scaled[:, t, :], y[:, t, cols], neg_mean[t][:], g_px[t][:, cols], ALU.add, ALU.mult
+                )
+            for t in range(PACK):
+                nc.vector.scalar_tensor_tensor(
+                    res[:, t, :], scaled[:, t, :], rstd[:, t : t + 1], b_px[t][:, cols], ALU.mult, ALU.add
+                )
+            nc.sync.dma_start(out_rows[:, :, cols], res[:])
+            res_bf = keep.tile([P, width, PACK], BF16, name=f"res_bf{c}", align_bytes=64)
             nc.scalar.copy(
-                res_bf[:].rearrange("p (c i) t -> p c t i", i=4), res[c][:].rearrange("p t (c i) -> p c t i", i=4)
+                res_bf[:].rearrange("p (c i) t -> p c t i", i=4), res[:].rearrange("p t (c i) -> p c t i", i=4)
             )
             nc.vector.quantize_mx(
                 out=out_codes[:, cols].bitcast(FP8X4),
@@ -157,46 +156,6 @@ def tile_picked_yspade_none_po_kernel(
                 in_=res_bf[:].rearrange("p n t -> p (n t)"),
             )
             nc.sync.dma_start(word_rows[:, cols], out_codes[:, cols].bitcast(I32))
-
-        for t in order:
-            scaled = keep.tile([P, S], F32, name=f"scaled{t}")
-            y_sb = keep.tile([P, S], F32, name=f"y_sb{t}")
-            neg_mean = mean_of(t, y_sb)
-            rstd = rstd_of(t, y_sb, neg_mean)
-            if t in EARLY:
-                i = EARLY.index(t)
-                for h in range(2):
-                    cols = slice(h * HALF, (h + 1) * HALF)
-                    nc.vector.scalar_tensor_tensor(
-                        scaled[:, cols], y[t, h][:], neg_mean[:], g_px[:, i, cols], ALU.add, ALU.mult
-                    )
-                for c, width in enumerate(CHUNKS):
-                    cols = slice(starts[c], starts[c] + width)
-                    nc.vector.scalar_tensor_tensor(
-                        res[c][:, t, :], scaled[:, cols], rstd[:], b_px[:, i, cols], ALU.mult, ALU.add
-                    )
-                continue
-            gain = keep.tile([P, TABLE_W], F32, name=f"gain{t}")
-            shift = keep.tile([P, TABLE_W], F32, name=f"shift{t}")
-            nc.gpsimd.memset(gain[:, R:], 0.0)
-            nc.gpsimd.memset(shift[:, R:], 0.0)
-            nc.scalar.activation(gain[:, :R], gam_t[t][:, :R], ACT.Copy, scale=rstd[:])
-            nc.vector.scalar_tensor_tensor(shift[:, :R], gain[:, :R], neg_mean[:], bet_t[t][:, :R], ALU.mult, ALU.add)
-            last = t == order[-1]
-            pieces = list(zip(starts, CHUNKS)) if last else [(0, HALF), (HALF, HALF)]
-            for lo, width in pieces:
-                cols = slice(lo, lo + width)
-                nc.vector.tensor_tensor(
-                    scaled[:, cols], gain[:].indirect(entries(lab_t, lo, lo + width)), y_sb[:, cols], ALU.mult
-                )
-                for c in range(len(CHUNKS)):
-                    if lo <= starts[c] < lo + width:
-                        cols = slice(starts[c], starts[c] + CHUNKS[c])
-                        nc.vector.tensor_tensor(
-                            res[c][:, t, :], shift[:].indirect(entries(lab_t, cols.start, cols.stop)), scaled[:, cols], ALU.add
-                        )
-                        if last:
-                            finish(c)
 
         for q in range(4):
             queue = nc.sync if q % 2 else nc.scalar

@@ -18,7 +18,7 @@ PACK = 4
 HALF = 512
 TABLE_W = 1376
 EPS = 1e-4
-EARLY = 2
+POOL_TILES = 2
 CHUNKS = (256, 256, 256, 128, 128)
 FLOPS = 2 * K * N * S
 
@@ -36,62 +36,54 @@ def tile_picked_yspade_none_po_kernel(
         offs_t = keep.tile([P, S // 16], U16, name="offs_t")
         gam_t = [keep.tile([P, TABLE_W], F32, name=f"gam{t}") for t in range(PACK)]
         bet_t = [keep.tile([P, TABLE_W], F32, name=f"bet{t}") for t in range(PACK)]
-        xw = keep.tile([P, T], U32, name="xw")
-        xs = keep.tile([P, T], U8, name="xs")
-        w_raw = [keep.tile([P, PACK, N // 2], F32, name=f"w_raw{h}") for h in range(2)]
+        xw = keep.tile([P, T], U32, name="xw", tag="wide")
+        xs = keep.tile([P, T], U8, name="xs", tag="after_bytes", align_bytes=64)
+        w_raw = keep.tile([P, PACK, N], F32, name="w_raw")
         gam_rows = gam.rearrange("(p t) r -> p t r", t=PACK)
         bet_rows = bet.rearrange("(p t) r -> p t r", t=PACK)
         w_rows = w1.rearrange("(p j) n -> p j n", j=PACK)
 
-        nc.vector.memset(xs[:].bitcast(I32), 0)
+        nc.gpsimd.memset(xs[:, : T // 2].bitcast(I32), 0)
+        nc.vector.memset(xs[:, T // 2 :].bitcast(I32), 0)
         warm = keep.tile([P, 2], F32, name="warm")
         nc.vector.memset(warm[:, 0:1], 1.0)
         nc.scalar.activation(warm[:, 1:2], warm[:, 0:1], ACT.Abs_reciprocal_sqrt)
 
         nc.sync.dma_start(lab_t[:], lab)
-        for t in range(EARLY):
-            nc.sync.dma_start(gam_t[t][:, :R], gam_rows[:, t, :])
+        nc.sync.dma_start(gam_t[0][:, :R], gam_rows[:, 0, :])
+        nc.sync.dma_start(bet_t[0][:, :R], bet_rows[:, 0, :])
+        nc.sync.dma_start(w_raw[:], w_rows)
+        for q in range(4):
+            nc.sync.dma_start(xs[32 * q : 32 * q + 4, :].bitcast(I32), x_scales[0, 4 * q : 4 * q + 4, :].bitcast(I32))
         nc.sync.dma_start(offs_t[:], offs)
         nc.sync.dma_start(xw[:].bitcast(I32), x_words[0].rearrange("p n t -> p (n t)").bitcast(I32))
-        for q in range(4):
-            nc.scalar.dma_start(xs[32 * q : 32 * q + 4, :].bitcast(I32), x_scales[0, 4 * q : 4 * q + 4, :].bitcast(I32))
-        for h in range(2):
-            nc.sync.dma_start(w_raw[h][:], w_rows[:, :, h * (N // 2) : (h + 1) * (N // 2)])
-        for t in range(EARLY, PACK):
+        for t in range(1, PACK):
             nc.sync.dma_start(gam_t[t][:, :R], gam_rows[:, t, :])
-        for t in range(PACK):
             nc.sync.dma_start(bet_t[t][:, :R], bet_rows[:, t, :])
 
-        def look_up(table, picked):
-            nc.vector.tensor_copy(picked, table[:].indirect(lab_t[:]))
+        def look_up(t, gains, shifts):
+            nc.vector.tensor_copy(gains, gam_t[t][:].indirect(lab_t[:]))
+            nc.vector.tensor_copy(shifts, bet_t[t][:].indirect(lab_t[:]))
 
-        early = keep.tile([P, EARLY, S], F32, name="early")
-        for t in range(EARLY):
-            look_up(gam_t[t], early[:, t, :])
-
-        x_codes = keep.tile([P, S], U32, name="x_codes", align_bytes=64)
+        early = keep.tile([P, 2, S], F32, name="early")
+        look_up(0, early[:, 0, :], early[:, 1, :])
         x_bytes = keep.tile([P, S], U8, name="x_bytes", align_bytes=64)
         nc.vector.tensor_copy(x_bytes[:], xs[:].indirect(offs_t[:]))
-        nc.vector.tensor_copy(x_codes[:], xw[:].indirect(offs_t[:]))
 
-        w_bf = keep.tile([P, PACK, P, PACK], BF16, name="w_bf", tag="stage", align_bytes=64)
-        for h in range(2):
-            nc.scalar.copy(
-                w_bf[:, :, h * (P // 2) : (h + 1) * (P // 2), :].rearrange("p t m j -> p m j t"),
-                w_raw[h][:].rearrange("p j (m t) -> p m j t", t=PACK),
-            )
-        w_codes = keep.tile([P, N], U32, name="w_codes", align_bytes=64)
+        w_bf = keep.tile([P, PACK, P, PACK], BF16, name="w_bf", tag="after_quant", align_bytes=64)
+        nc.scalar.copy(w_bf[:].rearrange("p t m j -> p m j t"), w_raw[:].rearrange("p j (m t) -> p m j t", t=PACK))
+        w_codes = keep.tile([P, N], U32, name="w_codes", tag="after_bytes", align_bytes=64)
         w_scales = keep.tile([P, N], U8, name="w_scales", align_bytes=64)
         nc.vector.quantize_mx(
             out=w_codes[:].bitcast(FP8X4), scales=w_scales[:], in_=w_bf[:].rearrange("p t m j -> p (t m j)")
         )
-        late = keep.tile([P, 2 * PACK - EARLY, S], F32, name="late", tag="stage", align_bytes=64)
-        g_px = [early[:, t, :] if t < EARLY else late[:, t - EARLY, :] for t in range(PACK)]
-        b_px = [late[:, PACK - EARLY + t, :] for t in range(PACK)]
-        for t in range(EARLY, PACK):
-            look_up(gam_t[t], g_px[t])
-        for t in range(PACK):
-            look_up(bet_t[t], b_px[t])
+        x_codes = keep.tile([P, S], U32, name="x_codes", tag="after_quant", align_bytes=64)
+        nc.vector.tensor_copy(x_codes[:], xw[:].indirect(offs_t[:]))
+        late = keep.tile([P, PACK - 1, 2, S], F32, name="late", tag="wide")
+        g_px = [early[:, 0, :]] + [late[:, t, 0, :] for t in range(PACK - 1)]
+        b_px = [early[:, 1, :]] + [late[:, t, 1, :] for t in range(PACK - 1)]
+        for t in range(1, PACK):
+            look_up(t, g_px[t], b_px[t])
 
         y = psum.tile([P, PACK, S], F32, name="y")
         for t in range(PACK):
@@ -109,10 +101,17 @@ def tile_picked_yspade_none_po_kernel(
         def col(name):
             return keep.tile([P, 1], F32, name=name)
 
+        res = keep.tile([P, PACK, S], F32, name="res")
+        out_codes = keep.tile([P, S], U32, name="out_codes", align_bytes=64)
+        out_scales = keep.tile([P, S], U8, name="out_scales", align_bytes=64)
+        out_rows = out_0.rearrange("(p t) j -> p t j", t=PACK)
+        word_rows = out_1[0].rearrange("p n t -> p (n t)").bitcast(I32)
+
         neg_mean = []
         squares = keep.tile([P, PACK], F32, name="squares")
+        rstd = keep.tile([P, PACK], F32, name="rstd")
         for t in range(PACK):
-            y_sb = ring.tile([P, S], F32, name="y_sb")
+            y_sb = keep.tile([P, S], F32, name="y_sb", bufs=1)
             sums = [col(f"sum{t}{h}") for h in range(2)]
             for h in range(2):
                 cols = slice(h * HALF, (h + 1) * HALF)
@@ -123,32 +122,43 @@ def tile_picked_yspade_none_po_kernel(
             nc.scalar.activation(neg_mean[t][:], sums[1][:], ACT.Identity, scale=-1.0 / S, bias=part_mean[:])
             junk = ring.tile([P, S], BF16, name="junk")
             nc.scalar.activation(junk[:], y_sb[:], ACT.Square, bias=neg_mean[t][:], accum_out=squares[:, t : t + 1])
-        rstd = keep.tile([P, PACK], F32, name="rstd")
-        nc.scalar.activation(rstd[:], squares[:], ACT.Abs_reciprocal_sqrt, scale=1.0 / S, bias=EPS)
-
-        out_codes = keep.tile([P, S], U32, name="out_codes", align_bytes=64)
-        out_scales = keep.tile([P, S], U8, name="out_scales", align_bytes=64)
-        out_rows = out_0.rearrange("(p t) j -> p t j", t=PACK)
-        word_rows = out_1[0].rearrange("p n t -> p (n t)").bitcast(I32)
+            if t < POOL_TILES:
+                nc.scalar.activation(
+                    rstd[:, t : t + 1], squares[:, t : t + 1], ACT.Abs_reciprocal_sqrt, scale=1.0 / S, bias=EPS
+                )
+                shift = col(f"sh{t}")
+                nc.scalar.activation(shift[:], neg_mean[t][:], ACT.Copy, scale=rstd[:, t : t + 1])
+                normed = keep.tile([P, S], F32, name=f"normed{t}")
+                nc.scalar.activation(normed[:], y_sb[:], ACT.Identity, scale=rstd[:, t : t + 1], bias=shift[:])
+                gained = keep.tile([P, S], F32, name=f"gained{t}")
+                for h in range(2):
+                    cols = slice(h * HALF, (h + 1) * HALF)
+                    nc.gpsimd.tensor_tensor(gained[:, cols], normed[:, cols], g_px[t][:, cols], ALU.mult)
+                for h in range(2):
+                    cols = slice(h * HALF, (h + 1) * HALF)
+                    nc.gpsimd.tensor_tensor(res[:, t, cols], gained[:, cols], b_px[t][:, cols], ALU.add)
+                nc.sync.dma_start(out_rows[:, t, :], res[:, t, :])
+        nc.scalar.activation(
+            rstd[:, POOL_TILES:], squares[:, POOL_TILES:], ACT.Abs_reciprocal_sqrt, scale=1.0 / S, bias=EPS
+        )
 
         lo = 0
         for c, width in enumerate(CHUNKS):
             cols = slice(lo, lo + width)
             lo = lo + width
             scaled = keep.tile([P, PACK, width], F32, name="scaled", bufs=2)
-            res = keep.tile([P, PACK, width], F32, name=f"res{c}")
-            for t in range(PACK):
+            for t in range(POOL_TILES, PACK):
                 nc.vector.scalar_tensor_tensor(
                     scaled[:, t, :], y[:, t, cols], neg_mean[t][:], g_px[t][:, cols], ALU.add, ALU.mult
                 )
-            for t in range(PACK):
+            for t in range(POOL_TILES, PACK):
                 nc.vector.scalar_tensor_tensor(
-                    res[:, t, :], scaled[:, t, :], rstd[:, t : t + 1], b_px[t][:, cols], ALU.mult, ALU.add
+                    res[:, t, cols], scaled[:, t, :], rstd[:, t : t + 1], b_px[t][:, cols], ALU.mult, ALU.add
                 )
-            nc.sync.dma_start(out_rows[:, :, cols], res[:])
+            nc.sync.dma_start(out_rows[:, POOL_TILES:, cols], res[:, POOL_TILES:, cols])
             res_bf = keep.tile([P, width, PACK], BF16, name=f"res_bf{c}", align_bytes=64)
             nc.scalar.copy(
-                res_bf[:].rearrange("p (c i) t -> p c t i", i=4), res[:].rearrange("p t (c i) -> p c t i", i=4)
+                res_bf[:].rearrange("p (c i) t -> p c t i", i=4), res[:, :, cols].rearrange("p t (c i) -> p c t i", i=4)
             )
             nc.vector.quantize_mx(
                 out=out_codes[:, cols].bitcast(FP8X4),

@@ -18,9 +18,11 @@ PACK = 4
 HALF = 512
 TABLE_W = 1376
 EPS = 1e-4
-POOL_TILES = 2
 CHUNKS = (256, 256, 256, 128, 128)
+STORES = {1: 0, 3: 2, 4: 4}
 FLOPS = 2 * K * N * S
+EARLY = 2
+LAST = 3
 
 
 def tile_picked_yspade_none_po_kernel(
@@ -29,14 +31,18 @@ def tile_picked_yspade_none_po_kernel(
     nc = tc.nc
     with ExitStack() as ctx:
         keep = ctx.enter_context(tc.tile_pool(name="keep", bufs=1))
-        ring = ctx.enter_context(tc.tile_pool(name="ring", bufs=4))
         psum = ctx.enter_context(tc.psum_pool(name="psum", bufs=1))
 
         lab_t = keep.tile([P, S // 16], U16, name="lab_t")
         offs_t = keep.tile([P, S // 16], U16, name="offs_t")
-        gam_t = [keep.tile([P, TABLE_W], F32, name=f"gam{t}") for t in range(PACK)]
-        bet_t = [keep.tile([P, TABLE_W], F32, name=f"bet{t}") for t in range(PACK)]
-        xw = keep.tile([P, T], U32, name="xw", tag="wide")
+        gam_early = keep.tile([P, TABLE_W], F32, name="gam_early")
+        bet_early = keep.tile([P, TABLE_W], F32, name="bet_early")
+        gam_first = keep.tile([P, TABLE_W], F32, name="gam_first")
+        gam_second = keep.tile([P, R], F32, name="gam_second", tag="after_gain")
+        bet_raw = keep.tile([P, 2, R], F32, name="bet_raw")
+        gam_last = keep.tile([P, TABLE_W], F32, name="gam_last")
+        bet_last = keep.tile([P, TABLE_W], F32, name="bet_last")
+        xw = keep.tile([P, T], U32, name="xw", tag="after_words")
         xs = keep.tile([P, T], U8, name="xs", tag="after_bytes", align_bytes=64)
         w_raw = keep.tile([P, PACK, N], F32, name="w_raw")
         gam_rows = gam.rearrange("(p t) r -> p t r", t=PACK)
@@ -50,23 +56,27 @@ def tile_picked_yspade_none_po_kernel(
         nc.scalar.activation(warm[:, 1:2], warm[:, 0:1], ACT.Abs_reciprocal_sqrt)
 
         nc.sync.dma_start(lab_t[:], lab)
-        nc.sync.dma_start(gam_t[0][:, :R], gam_rows[:, 0, :])
-        nc.sync.dma_start(bet_t[0][:, :R], bet_rows[:, 0, :])
+        nc.sync.dma_start(gam_early[:, :R], gam_rows[:, EARLY, :])
+        nc.sync.dma_start(bet_early[:, :R], bet_rows[:, EARLY, :])
         nc.sync.dma_start(w_raw[:], w_rows)
         for q in range(4):
             nc.sync.dma_start(xs[32 * q : 32 * q + 4, :].bitcast(I32), x_scales[0, 4 * q : 4 * q + 4, :].bitcast(I32))
         nc.sync.dma_start(offs_t[:], offs)
         nc.sync.dma_start(xw[:].bitcast(I32), x_words[0].rearrange("p n t -> p (n t)").bitcast(I32))
-        for t in range(1, PACK):
-            nc.sync.dma_start(gam_t[t][:, :R], gam_rows[:, t, :])
-            nc.sync.dma_start(bet_t[t][:, :R], bet_rows[:, t, :])
+        nc.sync.dma_start(gam_last[:, :R], gam_rows[:, LAST, :])
+        nc.sync.dma_start(gam_first[:, :R], gam_rows[:, 0, :])
+        nc.sync.dma_start(bet_raw[:], bet_rows[:, 0:2, :])
+        nc.sync.dma_start(gam_second[:], gam_rows[:, 1, :])
+        nc.sync.dma_start(bet_last[:, :R], bet_rows[:, LAST, :])
 
-        def look_up(t, gains, shifts):
-            nc.vector.tensor_copy(gains, gam_t[t][:].indirect(lab_t[:]))
-            nc.vector.tensor_copy(shifts, bet_t[t][:].indirect(lab_t[:]))
+        def picks(lo, hi):
+            return lab_t[:, lo // 16 : hi // 16]
 
-        early = keep.tile([P, 2, S], F32, name="early")
-        look_up(0, early[:, 0, :], early[:, 1, :])
+        halves = [slice(h * HALF, (h + 1) * HALF) for h in range(2)]
+        g_early = keep.tile([P, S], F32, name="g_early")
+        nc.vector.tensor_copy(g_early[:], gam_early[:].indirect(lab_t[:]))
+        b_early = [keep.tile([P, HALF], F32, name="b_early0")[:]]
+        nc.vector.tensor_copy(b_early[0], bet_early[:].indirect(picks(0, HALF)))
         x_bytes = keep.tile([P, S], U8, name="x_bytes", align_bytes=64)
         nc.vector.tensor_copy(x_bytes[:], xs[:].indirect(offs_t[:]))
 
@@ -78,16 +88,20 @@ def tile_picked_yspade_none_po_kernel(
             out=w_codes[:].bitcast(FP8X4), scales=w_scales[:], in_=w_bf[:].rearrange("p t m j -> p (t m j)")
         )
         x_codes = keep.tile([P, S], U32, name="x_codes", tag="after_quant", align_bytes=64)
-        nc.vector.tensor_copy(x_codes[:], xw[:].indirect(offs_t[:]))
-        late = keep.tile([P, PACK - 1, 2, S], F32, name="late", tag="wide")
-        g_px = [early[:, 0, :]] + [late[:, t, 0, :] for t in range(PACK - 1)]
-        b_px = [early[:, 1, :]] + [late[:, t, 1, :] for t in range(PACK - 1)]
-        for t in range(1, PACK):
-            look_up(t, g_px[t], b_px[t])
+        for h in range(2):
+            nc.vector.tensor_copy(
+                x_codes[:, h * HALF : (h + 1) * HALF], xw[:].indirect(offs_t[:, h * HALF // 16 : (h + 1) * HALF // 16])
+            )
+
+        waiting = keep.tile([P, 2, HALF], F32, name="waiting", tag="after_words")
+        b_early.append(waiting[:, 0, :])
+        nc.vector.tensor_copy(b_early[1], bet_early[:].indirect(picks(HALF, S)))
+        g_last = waiting[:, 1, :]
+        nc.vector.tensor_copy(g_last, gam_last[:].indirect(picks(0, HALF)))
 
         y = psum.tile([P, PACK, S], F32, name="y")
-        for t in range(PACK):
-            for h in range(2):
+        for pair in range(2):
+            for h, t in [(h, 2 * pair + 1 - i) for h in range(2) for i in range(2)]:
                 nc.tensor.matmul_mx(
                     out=y[:, t, h * HALF : (h + 1) * HALF],
                     lhsT=w_codes[:, t * P : (t + 1) * P].bitcast(FP8X4),
@@ -107,65 +121,121 @@ def tile_picked_yspade_none_po_kernel(
         out_rows = out_0.rearrange("(p t) j -> p t j", t=PACK)
         word_rows = out_1[0].rearrange("p n t -> p (n t)").bitcast(I32)
 
-        neg_mean = []
-        squares = keep.tile([P, PACK], F32, name="squares")
-        rstd = keep.tile([P, PACK], F32, name="rstd")
-        for t in range(PACK):
-            y_sb = keep.tile([P, S], F32, name="y_sb", bufs=1)
-            sums = [col(f"sum{t}{h}") for h in range(2)]
-            for h in range(2):
-                cols = slice(h * HALF, (h + 1) * HALF)
-                nc.scalar.activation(y_sb[:, cols], y[:, t, cols], ACT.Copy, accum_out=sums[h][:])
-            part_mean = col(f"pm{t}")
-            nc.scalar.activation(part_mean[:], sums[0][:], ACT.Copy, scale=-1.0 / S)
-            neg_mean.append(col(f"nm{t}"))
-            nc.scalar.activation(neg_mean[t][:], sums[1][:], ACT.Identity, scale=-1.0 / S, bias=part_mean[:])
-            junk = ring.tile([P, S], BF16, name="junk")
-            nc.scalar.activation(junk[:], y_sb[:], ACT.Square, bias=neg_mean[t][:], accum_out=squares[:, t : t + 1])
-            if t < POOL_TILES:
-                nc.scalar.activation(
-                    rstd[:, t : t + 1], squares[:, t : t + 1], ACT.Abs_reciprocal_sqrt, scale=1.0 / S, bias=EPS
-                )
-                shift = col(f"sh{t}")
-                nc.scalar.activation(shift[:], neg_mean[t][:], ACT.Copy, scale=rstd[:, t : t + 1])
-                normed = keep.tile([P, S], F32, name=f"normed{t}")
-                nc.scalar.activation(normed[:], y_sb[:], ACT.Identity, scale=rstd[:, t : t + 1], bias=shift[:])
-                gained = keep.tile([P, S], F32, name=f"gained{t}")
-                for h in range(2):
-                    cols = slice(h * HALF, (h + 1) * HALF)
-                    nc.gpsimd.tensor_tensor(gained[:, cols], normed[:, cols], g_px[t][:, cols], ALU.mult)
-                for h in range(2):
-                    cols = slice(h * HALF, (h + 1) * HALF)
-                    nc.gpsimd.tensor_tensor(res[:, t, cols], gained[:, cols], b_px[t][:, cols], ALU.add)
-                nc.sync.dma_start(out_rows[:, t, :], res[:, t, :])
-        nc.scalar.activation(
-            rstd[:, POOL_TILES:], squares[:, POOL_TILES:], ACT.Abs_reciprocal_sqrt, scale=1.0 / S, bias=EPS
-        )
+        y_sb = {t: keep.tile([P, S], F32, name=f"y_sb{t}")[:] for t in range(2)}
+        sums = [[col(f"sum{t}{h}") for h in range(2)] for t in range(PACK)]
 
-        lo = 0
-        for c, width in enumerate(CHUNKS):
-            cols = slice(lo, lo + width)
-            lo = lo + width
-            scaled = keep.tile([P, PACK, width], F32, name="scaled", bufs=2)
-            for t in range(POOL_TILES, PACK):
-                nc.vector.scalar_tensor_tensor(
-                    scaled[:, t, :], y[:, t, cols], neg_mean[t][:], g_px[t][:, cols], ALU.add, ALU.mult
-                )
-            for t in range(POOL_TILES, PACK):
-                nc.vector.scalar_tensor_tensor(
-                    res[:, t, cols], scaled[:, t, :], rstd[:, t : t + 1], b_px[t][:, cols], ALU.mult, ALU.add
-                )
-            nc.sync.dma_start(out_rows[:, POOL_TILES:, cols], res[:, POOL_TILES:, cols])
-            res_bf = keep.tile([P, width, PACK], BF16, name=f"res_bf{c}", align_bytes=64)
-            nc.scalar.copy(
-                res_bf[:].rearrange("p (c i) t -> p c t i", i=4), res[:, :, cols].rearrange("p t (c i) -> p c t i", i=4)
+        def copy_out(t, h):
+            nc.scalar.activation(y_sb[t][:, halves[h]], y[:, t, halves[h]], ACT.Copy, accum_out=sums[t][h][:])
+
+        def moments(t, junk):
+            part_mean = col(f"pm{t}")
+            nc.scalar.activation(part_mean[:], sums[t][0][:], ACT.Copy, scale=-1.0 / S)
+            neg_mean = col(f"nm{t}")
+            nc.scalar.activation(neg_mean[:], sums[t][1][:], ACT.Identity, scale=-1.0 / S, bias=part_mean[:])
+            squares = col(f"sq{t}")
+            nc.scalar.activation(junk, y_sb[t], ACT.Square, bias=neg_mean[:], accum_out=squares[:])
+            rstd = col(f"rstd{t}")
+            nc.scalar.activation(rstd[:], squares[:], ACT.Abs_reciprocal_sqrt, scale=1.0 / S, bias=EPS)
+            return neg_mean, rstd
+
+        def fold_shift(t, gains, factor):
+            table = keep.tile([P, TABLE_W], F32, name=f"shift{t}")
+            nc.vector.scalar_tensor_tensor(table[:, :R], gains, factor, bet_raw[:, t, :], ALU.mult, ALU.add)
+            return table
+
+        def product(t, neg_mean, rstd):
+            out = col(f"c{t}")
+            nc.scalar.activation(out[:], neg_mean[:], ACT.Copy, scale=rstd[:])
+            return out
+
+        for h in range(2):
+            for t in (1, 0):
+                copy_out(t, h)
+
+        raw_gained = keep.tile([P, S], F32, name="raw_gained")
+        gained = [keep.tile([P, S], F32, name=f"gained{t}") for t in range(PACK)]
+        for cols in halves:
+            nc.vector.tensor_tensor(
+                raw_gained[:, cols], gam_first[:].indirect(picks(cols.start, cols.stop)), y_sb[0][:, cols], ALU.mult
             )
+        neg_mean1, rstd = moments(1, keep.tile([P, S], BF16, name="junk")[:])
+        gains = keep.tile([P, TABLE_W], F32, name="gains1")
+        nc.scalar.activation(gains[:, :R], gam_second[:], ACT.Copy, scale=rstd[:])
+        shifts1 = fold_shift(1, gains[:, :R], neg_mean1[:])
+        nc.vector.tensor_tensor(gained[1][:], gains[:].indirect(lab_t[:]), y_sb[1], ALU.mult)
+
+        late = keep.tile([P, 3, S], F32, name="late", tag="after_gain")
+        junk = late[:, 0, :]
+        y_sb[EARLY] = late[:, 1, :]
+        y_sb[LAST] = late[:, 2, :]
+        neg_mean, rstd = moments(0, junk)
+        factor = product(0, neg_mean, rstd)
+        shifts = fold_shift(0, gam_first[:, :R], factor[:])
+        nc.vector.tensor_tensor(res[:, 1, :], shifts1[:].indirect(lab_t[:]), gained[1][:], ALU.add)
+        nc.sync.dma_start(out_rows[:, 1, :], res[:, 1, :])
+        nc.scalar.activation(gained[0][:], raw_gained[:], ACT.Copy, scale=rstd[:])
+        nc.vector.tensor_tensor(res[:, 0, :], shifts[:].indirect(lab_t[:]), gained[0][:], ALU.add)
+        nc.sync.dma_start(out_rows[:, 0, :], res[:, 0, :])
+
+        for h in range(2):
+            copy_out(EARLY, h)
+        neg_mean_early, rstd_early = moments(EARLY, junk)
+        for h in range(2):
+            copy_out(LAST, h)
+        neg_mean, rstd = moments(LAST, junk)
+        factor = product(LAST, neg_mean, rstd)
+        normed = keep.tile([P, S], F32, name="normed")
+        for cols in halves:
+            nc.scalar.activation(normed[:, cols], y_sb[LAST][:, cols], ACT.Identity, scale=rstd[:], bias=factor[:])
+
+        def gain_half(h):
+            cols = halves[h]
+            nc.vector.scalar_tensor_tensor(
+                gained[EARLY][:, cols], y_sb[EARLY][:, cols], neg_mean_early[:], g_early[:, cols], ALU.add, ALU.mult
+            )
+            gains_px = g_last if h == 0 else gam_last[:].indirect(picks(HALF, S))
+            nc.vector.tensor_tensor(gained[LAST][:, cols], gains_px, normed[:, cols], ALU.mult)
+            nc.vector.scalar_tensor_tensor(
+                res[:, EARLY, cols], gained[EARLY][:, cols], rstd_early[:], b_early[h], ALU.mult, ALU.add
+            )
+            nc.sync.dma_start(out_rows[:, EARLY, cols], res[:, EARLY, cols])
+
+        bounds = [sum(CHUNKS[:c]) for c in range(len(CHUNKS) + 1)]
+
+        res_bf = []
+
+        def shift_chunk(c):
+            cols = slice(bounds[c], bounds[c + 1])
+            nc.vector.tensor_tensor(
+                res[:, LAST, cols], bet_last[:].indirect(picks(cols.start, cols.stop)), gained[LAST][:, cols], ALU.add
+            )
+            if c in STORES:
+                run = slice(bounds[STORES[c]], bounds[c + 1])
+                nc.sync.dma_start(out_rows[:, LAST, run], res[:, LAST, run])
+            res_bf.append(keep.tile([P, CHUNKS[c], PACK], BF16, name=f"res_bf{c}", align_bytes=64))
+            nc.scalar.copy(
+                res_bf[c][:].rearrange("p (c i) t -> p c t i", i=4),
+                res[:, :, cols].rearrange("p t (c i) -> p c t i", i=4),
+            )
+
+        def quantise_chunk(c):
+            cols = slice(bounds[c], bounds[c + 1])
             nc.vector.quantize_mx(
                 out=out_codes[:, cols].bitcast(FP8X4),
                 scales=out_scales[:, cols],
-                in_=res_bf[:].rearrange("p n t -> p (n t)"),
+                in_=res_bf[c][:].rearrange("p n t -> p (n t)"),
             )
-            nc.sync.dma_start(word_rows[:, cols], out_codes[:, cols].bitcast(I32))
+            if c in STORES:
+                run = slice(bounds[STORES[c]], bounds[c + 1])
+                nc.sync.dma_start(word_rows[:, run], out_codes[:, run].bitcast(I32))
+
+        for step in range(len(CHUNKS) + 1):
+            if step < len(CHUNKS):
+                if bounds[step] % HALF == 0:
+                    gain_half(bounds[step] // HALF)
+                shift_chunk(step)
+            if step >= 1:
+                quantise_chunk(step - 1)
 
         for q in range(4):
             queue = nc.sync if q % 2 else nc.scalar

@@ -21,6 +21,7 @@ EPS = 1e-4
 CHUNKS = (256, 256, 256, 128, 128)
 STORES = {1: 0, 3: 2, 4: 4}
 FLOPS = 2 * K * N * S
+BEFORE_WORDS = 768
 EARLY = 2
 LAST = 3
 
@@ -60,7 +61,7 @@ def tile_picked_yspade_none_po_kernel(
         nc.sync.dma_start(bet_early[:, :R], bet_rows[:, EARLY, :])
         nc.sync.dma_start(w_raw[:], w_rows)
         for q in range(4):
-            nc.sync.dma_start(xs[32 * q : 32 * q + 4, :].bitcast(I32), x_scales[0, 4 * q : 4 * q + 4, :].bitcast(I32))
+            nc.sync.dma_start(xs[q:P:32, :].bitcast(I32), x_scales[0, q:16:4, :].bitcast(I32))
         nc.sync.dma_start(offs_t[:], offs)
         nc.sync.dma_start(xw[:].bitcast(I32), x_words[0].rearrange("p n t -> p (n t)").bitcast(I32))
         nc.sync.dma_start(gam_last[:, :R], gam_rows[:, LAST, :])
@@ -75,8 +76,8 @@ def tile_picked_yspade_none_po_kernel(
         halves = [slice(h * HALF, (h + 1) * HALF) for h in range(2)]
         g_early = keep.tile([P, S], F32, name="g_early")
         nc.vector.tensor_copy(g_early[:], gam_early[:].indirect(lab_t[:]))
-        b_early = [keep.tile([P, HALF], F32, name="b_early0")[:]]
-        nc.vector.tensor_copy(b_early[0], bet_early[:].indirect(picks(0, HALF)))
+        b_early = [keep.tile([P, BEFORE_WORDS], F32, name="b_early0")[:]]
+        nc.vector.tensor_copy(b_early[0], bet_early[:].indirect(picks(0, BEFORE_WORDS)))
         x_bytes = keep.tile([P, S], U8, name="x_bytes", align_bytes=64)
         nc.vector.tensor_copy(x_bytes[:], xs[:].indirect(offs_t[:]))
 
@@ -93,10 +94,10 @@ def tile_picked_yspade_none_po_kernel(
                 x_codes[:, h * HALF : (h + 1) * HALF], xw[:].indirect(offs_t[:, h * HALF // 16 : (h + 1) * HALF // 16])
             )
 
-        waiting = keep.tile([P, 2, HALF], F32, name="waiting", tag="after_words")
-        b_early.append(waiting[:, 0, :])
-        nc.vector.tensor_copy(b_early[1], bet_early[:].indirect(picks(HALF, S)))
-        g_last = waiting[:, 1, :]
+        waiting = keep.tile([P, S - BEFORE_WORDS + HALF], F32, name="waiting", tag="after_words")
+        b_early.append(waiting[:, HALF:])
+        nc.vector.tensor_copy(b_early[1], bet_early[:].indirect(picks(BEFORE_WORDS, S)))
+        g_last = waiting[:, :HALF]
         nc.vector.tensor_copy(g_last, gam_last[:].indirect(picks(0, HALF)))
 
         y = psum.tile([P, PACK, S], F32, name="y")
@@ -188,17 +189,21 @@ def tile_picked_yspade_none_po_kernel(
         for cols in halves:
             nc.scalar.activation(normed[:, cols], y_sb[LAST][:, cols], ACT.Identity, scale=rstd[:], bias=factor[:])
 
-        def gain_half(h):
-            cols = halves[h]
+        parts = [slice(0, BEFORE_WORDS), slice(BEFORE_WORDS, S)]
+        for cols in halves:
             nc.vector.scalar_tensor_tensor(
                 gained[EARLY][:, cols], y_sb[EARLY][:, cols], neg_mean_early[:], g_early[:, cols], ALU.add, ALU.mult
             )
-            gains_px = g_last if h == 0 else gam_last[:].indirect(picks(HALF, S))
-            nc.vector.tensor_tensor(gained[LAST][:, cols], gains_px, normed[:, cols], ALU.mult)
+        for cols, shifts_px in reversed(list(zip(parts, b_early))):
             nc.vector.scalar_tensor_tensor(
-                res[:, EARLY, cols], gained[EARLY][:, cols], rstd_early[:], b_early[h], ALU.mult, ALU.add
+                res[:, EARLY, cols], gained[EARLY][:, cols], rstd_early[:], shifts_px, ALU.mult, ALU.add
             )
-            nc.sync.dma_start(out_rows[:, EARLY, cols], res[:, EARLY, cols])
+        nc.sync.dma_start(out_rows[:, EARLY, :], res[:, EARLY, :])
+
+        def gain_quarter(lo):
+            cols = slice(lo, lo + HALF // 2)
+            gains_px = g_last[:, cols] if lo < HALF else gam_last[:].indirect(picks(cols.start, cols.stop))
+            nc.vector.tensor_tensor(gained[LAST][:, cols], gains_px, normed[:, cols], ALU.mult)
 
         bounds = [sum(CHUNKS[:c]) for c in range(len(CHUNKS) + 1)]
 
@@ -232,7 +237,8 @@ def tile_picked_yspade_none_po_kernel(
         for step in range(len(CHUNKS) + 1):
             if step < len(CHUNKS):
                 if bounds[step] % HALF == 0:
-                    gain_half(bounds[step] // HALF)
+                    gain_quarter(bounds[step])
+                    gain_quarter(bounds[step] + HALF // 2)
                 shift_chunk(step)
             if step >= 1:
                 quantise_chunk(step - 1)

@@ -18,12 +18,14 @@ PACK = 4
 HALF = 512
 TABLE_W = 1376
 EPS = 1e-4
-CHUNKS = (256, 256, 256, 128, 128)
-STORES = {1: 0, 3: 2, 4: 4}
+CHUNKS = (320, 256, 192, 128, 128)
+QUANTISED = (512, 256, 128, 128)
+STORED = (512, 384, 128)
 FLOPS = 2 * K * N * S
 BEFORE_WORDS = 768
-EARLY = 2
-LAST = 3
+EARLY = 0
+FOLDED = 1
+RAW = (2, 3)
 
 
 def tile_picked_yspade_none_po_kernel(
@@ -38,11 +40,9 @@ def tile_picked_yspade_none_po_kernel(
         offs_t = keep.tile([P, S // 16], U16, name="offs_t")
         gam_early = keep.tile([P, TABLE_W], F32, name="gam_early")
         bet_early = keep.tile([P, TABLE_W], F32, name="bet_early")
-        gam_first = keep.tile([P, TABLE_W], F32, name="gam_first")
-        gam_second = keep.tile([P, R], F32, name="gam_second", tag="after_gain")
-        bet_raw = keep.tile([P, 2, R], F32, name="bet_raw")
-        gam_last = keep.tile([P, TABLE_W], F32, name="gam_last")
-        bet_last = keep.tile([P, TABLE_W], F32, name="bet_last")
+        gam_raw = {t: keep.tile([P, TABLE_W], F32, name=f"gam_raw{t}") for t in RAW}
+        gam_folded = keep.tile([P, R], F32, name="gam_folded", tag="after_gain")
+        bet_raw = keep.tile([P, PACK - 1, R], F32, name="bet_raw")
         xw = keep.tile([P, T], U32, name="xw", tag="after_words")
         xs = keep.tile([P, T], U8, name="xs", tag="after_bytes", align_bytes=64)
         w_raw = keep.tile([P, PACK, N], F32, name="w_raw")
@@ -64,20 +64,20 @@ def tile_picked_yspade_none_po_kernel(
             nc.sync.dma_start(xs[q:P:32, :].bitcast(I32), x_scales[0, q:16:4, :].bitcast(I32))
         nc.sync.dma_start(offs_t[:], offs)
         nc.sync.dma_start(xw[:].bitcast(I32), x_words[0].rearrange("p n t -> p (n t)").bitcast(I32))
-        nc.sync.dma_start(gam_last[:, :R], gam_rows[:, LAST, :])
-        nc.sync.dma_start(gam_first[:, :R], gam_rows[:, 0, :])
-        nc.sync.dma_start(bet_raw[:], bet_rows[:, 0:2, :])
-        nc.sync.dma_start(gam_second[:], gam_rows[:, 1, :])
-        nc.sync.dma_start(bet_last[:, :R], bet_rows[:, LAST, :])
+        for t in RAW:
+            nc.sync.dma_start(gam_raw[t][:, :R], gam_rows[:, t, :])
+        nc.sync.dma_start(gam_folded[:], gam_rows[:, FOLDED, :])
+        nc.sync.dma_start(bet_raw[:], bet_rows[:, 1:, :])
 
-        def picks(lo, hi):
-            return lab_t[:, lo // 16 : hi // 16]
+        def picks(cols):
+            return lab_t[:, cols.start // 16 : cols.stop // 16]
 
         halves = [slice(h * HALF, (h + 1) * HALF) for h in range(2)]
-        g_early = keep.tile([P, S], F32, name="g_early")
+        parts = [slice(0, BEFORE_WORDS), slice(BEFORE_WORDS, S)]
+        g_early = keep.tile([P, S], F32, name="g_early", tag="after_centre")
         nc.vector.tensor_copy(g_early[:], gam_early[:].indirect(lab_t[:]))
-        b_early = [keep.tile([P, BEFORE_WORDS], F32, name="b_early0")[:]]
-        nc.vector.tensor_copy(b_early[0], bet_early[:].indirect(picks(0, BEFORE_WORDS)))
+        b_early = [keep.tile([P, BEFORE_WORDS], F32, name="b_early0")]
+        nc.vector.tensor_copy(b_early[0][:], bet_early[:].indirect(picks(parts[0])))
         x_bytes = keep.tile([P, S], U8, name="x_bytes", align_bytes=64)
         nc.vector.tensor_copy(x_bytes[:], xs[:].indirect(offs_t[:]))
 
@@ -89,40 +89,36 @@ def tile_picked_yspade_none_po_kernel(
             out=w_codes[:].bitcast(FP8X4), scales=w_scales[:], in_=w_bf[:].rearrange("p t m j -> p (t m j)")
         )
         x_codes = keep.tile([P, S], U32, name="x_codes", tag="after_quant", align_bytes=64)
-        for h in range(2):
-            nc.vector.tensor_copy(
-                x_codes[:, h * HALF : (h + 1) * HALF], xw[:].indirect(offs_t[:, h * HALF // 16 : (h + 1) * HALF // 16])
-            )
-
-        waiting = keep.tile([P, S - BEFORE_WORDS + HALF], F32, name="waiting", tag="after_words")
-        b_early.append(waiting[:, HALF:])
-        nc.vector.tensor_copy(b_early[1], bet_early[:].indirect(picks(BEFORE_WORDS, S)))
-        g_last = waiting[:, :HALF]
-        nc.vector.tensor_copy(g_last, gam_last[:].indirect(picks(0, HALF)))
+        for cols in halves:
+            nc.vector.tensor_copy(x_codes[:, cols], xw[:].indirect(offs_t[:, cols.start // 16 : cols.stop // 16]))
+        b_early.append(keep.tile([P, S - BEFORE_WORDS], F32, name="b_early1", tag="after_words"))
+        nc.vector.tensor_copy(b_early[1][:], bet_early[:].indirect(picks(parts[1])))
 
         y = psum.tile([P, PACK, S], F32, name="y")
-        for pair in range(2):
-            for h, t in [(h, 2 * pair + 1 - i) for h in range(2) for i in range(2)]:
-                nc.tensor.matmul_mx(
-                    out=y[:, t, h * HALF : (h + 1) * HALF],
-                    lhsT=w_codes[:, t * P : (t + 1) * P].bitcast(FP8X4),
-                    lhsT_scale=w_scales[:, t * P : (t + 1) * P],
-                    rhs=x_codes[:, h * HALF : (h + 1) * HALF].bitcast(FP8X4),
-                    rhs_scale=x_bytes[:, h * HALF : (h + 1) * HALF],
-                    start=True,
-                    stop=True,
-                )
+        for pair in ((RAW[0], FOLDED), (RAW[1], EARLY)):
+            for cols in halves:
+                for t in pair:
+                    nc.tensor.matmul_mx(
+                        out=y[:, t, cols],
+                        lhsT=w_codes[:, t * P : (t + 1) * P].bitcast(FP8X4),
+                        lhsT_scale=w_scales[:, t * P : (t + 1) * P],
+                        rhs=x_codes[:, cols].bitcast(FP8X4),
+                        rhs_scale=x_bytes[:, cols],
+                        start=True,
+                        stop=True,
+                    )
 
         def col(name):
             return keep.tile([P, 1], F32, name=name)
 
         res = keep.tile([P, PACK, S], F32, name="res")
+        gained = keep.tile([P, PACK, S], F32, name="gained")
         out_codes = keep.tile([P, S], U32, name="out_codes", align_bytes=64)
         out_scales = keep.tile([P, S], U8, name="out_scales", align_bytes=64)
         out_rows = out_0.rearrange("(p t) j -> p t j", t=PACK)
         word_rows = out_1[0].rearrange("p n t -> p (n t)").bitcast(I32)
 
-        y_sb = {t: keep.tile([P, S], F32, name=f"y_sb{t}")[:] for t in range(2)}
+        y_sb = {t: keep.tile([P, S], F32, name=f"y_sb{t}")[:] for t in (FOLDED,) + RAW}
         sums = [[col(f"sum{t}{h}") for h in range(2)] for t in range(PACK)]
 
         def copy_out(t, h):
@@ -139,110 +135,80 @@ def tile_picked_yspade_none_po_kernel(
             nc.scalar.activation(rstd[:], squares[:], ACT.Abs_reciprocal_sqrt, scale=1.0 / S, bias=EPS)
             return neg_mean, rstd
 
-        def fold_shift(t, gains, factor):
-            table = keep.tile([P, TABLE_W], F32, name=f"shift{t}")
-            nc.vector.scalar_tensor_tensor(table[:, :R], gains, factor, bet_raw[:, t, :], ALU.mult, ALU.add)
+        def fold_shift(t, gains, factor, tag):
+            table = keep.tile([P, TABLE_W], F32, name=f"shift{t}", tag=tag)
+            nc.vector.scalar_tensor_tensor(table[:, :R], gains, factor, bet_raw[:, t - 1, :], ALU.mult, ALU.add)
             return table
 
-        def product(t, neg_mean, rstd):
-            out = col(f"c{t}")
-            nc.scalar.activation(out[:], neg_mean[:], ACT.Copy, scale=rstd[:])
-            return out
-
         for h in range(2):
-            for t in (1, 0):
-                copy_out(t, h)
+            copy_out(RAW[0], h)
+            copy_out(FOLDED, h)
+        neg_mean, rstd = moments(FOLDED, keep.tile([P, S], BF16, name="junk")[:])
+        gains = keep.tile([P, TABLE_W], F32, name="gains")
+        nc.scalar.activation(gains[:, :R], gam_folded[:], ACT.Copy, scale=rstd[:])
+        for h in range(2):
+            copy_out(RAW[1], h)
 
-        raw_gained = keep.tile([P, S], F32, name="raw_gained")
-        gained = [keep.tile([P, S], F32, name=f"gained{t}") for t in range(PACK)]
-        for cols in halves:
-            nc.vector.tensor_tensor(
-                raw_gained[:, cols], gam_first[:].indirect(picks(cols.start, cols.stop)), y_sb[0][:, cols], ALU.mult
-            )
-        neg_mean1, rstd = moments(1, keep.tile([P, S], BF16, name="junk")[:])
-        gains = keep.tile([P, TABLE_W], F32, name="gains1")
-        nc.scalar.activation(gains[:, :R], gam_second[:], ACT.Copy, scale=rstd[:])
-        shifts1 = fold_shift(1, gains[:, :R], neg_mean1[:])
-        nc.vector.tensor_tensor(gained[1][:], gains[:].indirect(lab_t[:]), y_sb[1], ALU.mult)
+        raw_gained = keep.tile([P, 2, S], F32, name="raw_gained", tag="after_rescale")
+        for i, t in enumerate(RAW):
+            for cols in halves:
+                nc.vector.tensor_tensor(
+                    raw_gained[:, i, cols], gam_raw[t][:].indirect(picks(cols)), y_sb[t][:, cols], ALU.mult
+                )
 
-        late = keep.tile([P, 3, S], F32, name="late", tag="after_gain")
-        junk = late[:, 0, :]
-        y_sb[EARLY] = late[:, 1, :]
-        y_sb[LAST] = late[:, 2, :]
-        neg_mean, rstd = moments(0, junk)
-        factor = product(0, neg_mean, rstd)
-        shifts = fold_shift(0, gam_first[:, :R], factor[:])
-        nc.vector.tensor_tensor(res[:, 1, :], shifts1[:].indirect(lab_t[:]), gained[1][:], ALU.add)
-        nc.sync.dma_start(out_rows[:, 1, :], res[:, 1, :])
-        nc.scalar.activation(gained[0][:], raw_gained[:], ACT.Copy, scale=rstd[:])
-        nc.vector.tensor_tensor(res[:, 0, :], shifts[:].indirect(lab_t[:]), gained[0][:], ALU.add)
-        nc.sync.dma_start(out_rows[:, 0, :], res[:, 0, :])
+        shifts = {FOLDED: fold_shift(FOLDED, gains[:, :R], neg_mean[:], "shift_folded")}
+        nc.vector.tensor_tensor(gained[:, FOLDED, :], gains[:].indirect(lab_t[:]), y_sb[FOLDED], ALU.mult)
+
+        late = keep.tile([P, PACK, S], F32, name="late", tag="after_gain")
+        y_sb[EARLY] = late[:, FOLDED, :]
+
+        nc.vector.tensor_tensor(res[:, FOLDED, :], shifts[FOLDED][:].indirect(lab_t[:]), gained[:, FOLDED, :], ALU.add)
+        nc.sync.dma_start(out_rows[:, FOLDED, :], res[:, FOLDED, :])
 
         for h in range(2):
             copy_out(EARLY, h)
-        neg_mean_early, rstd_early = moments(EARLY, junk)
-        for h in range(2):
-            copy_out(LAST, h)
-        neg_mean, rstd = moments(LAST, junk)
-        factor = product(LAST, neg_mean, rstd)
-        normed = keep.tile([P, S], F32, name="normed")
-        for cols in halves:
-            nc.scalar.activation(normed[:, cols], y_sb[LAST][:, cols], ACT.Identity, scale=rstd[:], bias=factor[:])
-
-        parts = [slice(0, BEFORE_WORDS), slice(BEFORE_WORDS, S)]
+        neg_mean, rstd = moments(EARLY, late[:, EARLY, :])
         for cols in halves:
             nc.vector.scalar_tensor_tensor(
-                gained[EARLY][:, cols], y_sb[EARLY][:, cols], neg_mean_early[:], g_early[:, cols], ALU.add, ALU.mult
+                gained[:, EARLY, cols], y_sb[EARLY][:, cols], neg_mean[:], g_early[:, cols], ALU.add, ALU.mult
             )
-        for cols, shifts_px in reversed(list(zip(parts, b_early))):
+        for cols, shifts_px in zip(parts, b_early):
             nc.vector.scalar_tensor_tensor(
-                res[:, EARLY, cols], gained[EARLY][:, cols], rstd_early[:], shifts_px, ALU.mult, ALU.add
+                res[:, EARLY, cols], gained[:, EARLY, cols], rstd[:], shifts_px[:], ALU.mult, ALU.add
             )
         nc.sync.dma_start(out_rows[:, EARLY, :], res[:, EARLY, :])
 
-        def gain_quarter(lo):
-            cols = slice(lo, lo + HALF // 2)
-            gains_px = g_last[:, cols] if lo < HALF else gam_last[:].indirect(picks(cols.start, cols.stop))
-            nc.vector.tensor_tensor(gained[LAST][:, cols], gains_px, normed[:, cols], ALU.mult)
+        factors = {}
+        for i, t in enumerate(RAW):
+            neg_mean, rstd = moments(t, late[:, t, :])
+            factors[t] = col(f"c{t}")
+            nc.scalar.activation(factors[t][:], neg_mean[:], ACT.Copy, scale=rstd[:])
+            nc.scalar.activation(gained[:, t, :], raw_gained[:, i, :], ACT.Copy, scale=rstd[:])
+        for t, tag in zip(RAW, ("after_rescale", "after_centre")):
+            shifts[t] = fold_shift(t, gam_raw[t][:, :R], factors[t][:], tag)
 
-        bounds = [sum(CHUNKS[:c]) for c in range(len(CHUNKS) + 1)]
+        def runs(widths):
+            return [slice(sum(widths[:c]), sum(widths[: c + 1])) for c in range(len(widths))]
 
-        res_bf = []
-
-        def shift_chunk(c):
-            cols = slice(bounds[c], bounds[c + 1])
-            nc.vector.tensor_tensor(
-                res[:, LAST, cols], bet_last[:].indirect(picks(cols.start, cols.stop)), gained[LAST][:, cols], ALU.add
-            )
-            if c in STORES:
-                run = slice(bounds[STORES[c]], bounds[c + 1])
-                nc.sync.dma_start(out_rows[:, LAST, run], res[:, LAST, run])
-            res_bf.append(keep.tile([P, CHUNKS[c], PACK], BF16, name=f"res_bf{c}", align_bytes=64))
+        res_bf = keep.tile([P, S, PACK], BF16, name="res_bf", align_bytes=64)
+        for cols in runs(CHUNKS):
+            for t in RAW:
+                nc.vector.tensor_tensor(res[:, t, cols], shifts[t][:].indirect(picks(cols)), gained[:, t, cols], ALU.add)
             nc.scalar.copy(
-                res_bf[c][:].rearrange("p (c i) t -> p c t i", i=4),
+                res_bf[:, cols, :].rearrange("p (c i) t -> p c t i", i=4),
                 res[:, :, cols].rearrange("p t (c i) -> p c t i", i=4),
             )
-
-        def quantise_chunk(c):
-            cols = slice(bounds[c], bounds[c + 1])
+        for cols in runs(STORED):
+            nc.sync.dma_start(out_rows[:, RAW[0] :, cols], res[:, RAW[0] :, cols])
+        for cols in runs(QUANTISED):
             nc.vector.quantize_mx(
                 out=out_codes[:, cols].bitcast(FP8X4),
                 scales=out_scales[:, cols],
-                in_=res_bf[c][:].rearrange("p n t -> p (n t)"),
+                in_=res_bf[:, cols, :].rearrange("p n t -> p (n t)"),
             )
-            if c in STORES:
-                run = slice(bounds[STORES[c]], bounds[c + 1])
-                nc.sync.dma_start(word_rows[:, run], out_codes[:, run].bitcast(I32))
-
-        for step in range(len(CHUNKS) + 1):
-            if step < len(CHUNKS):
-                if bounds[step] % HALF == 0:
-                    gain_quarter(bounds[step])
-                    gain_quarter(bounds[step] + HALF // 2)
-                shift_chunk(step)
-            if step >= 1:
-                quantise_chunk(step - 1)
+        for cols in runs(STORED):
+            nc.sync.dma_start(word_rows[:, cols], out_codes[:, cols].bitcast(I32))
 
         for q in range(4):
             queue = nc.sync if q % 2 else nc.scalar
-            queue.dma_start(out_2[0, 4 * q : 4 * q + 4, :].bitcast(I32), out_scales[32 * q : 32 * q + 4, :].bitcast(I32))
+            queue.dma_start(out_2[0, q:16:4, :].bitcast(I32), out_scales[q:P:32, :].bitcast(I32))

@@ -18,9 +18,10 @@ PACK = 4
 HALF = 512
 TABLE_W = 1376
 EPS = 1e-4
-CHUNKS = (320, 256, 192, 128, 128)
+CHUNKS = (128, 192, 192, 192, 192, 128)
 QUANTISED = (512, 256, 128, 128)
-STORED = (512, 384, 128)
+STORED = (320, 384, 320)
+WORDS_STORED = (512, 256, 256)
 FLOPS = 2 * K * N * S
 BEFORE_WORDS = 768
 EARLY = 0
@@ -74,7 +75,7 @@ def tile_picked_yspade_none_po_kernel(
 
         halves = [slice(h * HALF, (h + 1) * HALF) for h in range(2)]
         parts = [slice(0, BEFORE_WORDS), slice(BEFORE_WORDS, S)]
-        g_early = keep.tile([P, S], F32, name="g_early", tag="after_centre")
+        g_early = keep.tile([P, S], F32, name="g_early")
         nc.vector.tensor_copy(g_early[:], gam_early[:].indirect(lab_t[:]))
         b_early = [keep.tile([P, BEFORE_WORDS], F32, name="b_early0")]
         nc.vector.tensor_copy(b_early[0][:], bet_early[:].indirect(picks(parts[0])))
@@ -112,88 +113,120 @@ def tile_picked_yspade_none_po_kernel(
             return keep.tile([P, 1], F32, name=name)
 
         res = keep.tile([P, PACK, S], F32, name="res")
-        gained = keep.tile([P, PACK, S], F32, name="gained")
+        gained_early = keep.tile([P, S], F32, name="gained_early")
+        gained_folded = [keep.tile([P, HALF], F32, name=f"gained_folded{h}", tag=f"after_folded{h}") for h in range(2)]
         out_codes = keep.tile([P, S], U32, name="out_codes", align_bytes=64)
         out_scales = keep.tile([P, S], U8, name="out_scales", align_bytes=64)
         out_rows = out_0.rearrange("(p t) j -> p t j", t=PACK)
         word_rows = out_1[0].rearrange("p n t -> p (n t)").bitcast(I32)
 
         y_sb = {t: keep.tile([P, S], F32, name=f"y_sb{t}")[:] for t in (FOLDED,) + RAW}
-        sums = [[col(f"sum{t}{h}") for h in range(2)] for t in range(PACK)]
+        sums = [keep.tile([P, 2], F32, name=f"sums{t}") for t in range(PACK)]
 
         def copy_out(t, h):
-            nc.scalar.activation(y_sb[t][:, halves[h]], y[:, t, halves[h]], ACT.Copy, accum_out=sums[t][h][:])
+            nc.scalar.activation(y_sb[t][:, halves[h]], y[:, t, halves[h]], ACT.Copy, accum_out=sums[t][:, h : h + 1])
 
-        def moments(t, junk):
-            part_mean = col(f"pm{t}")
-            nc.scalar.activation(part_mean[:], sums[t][0][:], ACT.Copy, scale=-1.0 / S)
+        def minus_mean(t):
+            shares = keep.tile([P, 2], F32, name=f"shares{t}")
             neg_mean = col(f"nm{t}")
-            nc.scalar.activation(neg_mean[:], sums[t][1][:], ACT.Identity, scale=-1.0 / S, bias=part_mean[:])
-            squares = col(f"sq{t}")
-            nc.scalar.activation(junk, y_sb[t], ACT.Square, bias=neg_mean[:], accum_out=squares[:])
-            rstd = col(f"rstd{t}")
-            nc.scalar.activation(rstd[:], squares[:], ACT.Abs_reciprocal_sqrt, scale=1.0 / S, bias=EPS)
-            return neg_mean, rstd
+            nc.scalar.activation(shares[:], sums[t][:], ACT.Copy, scale=-1.0 / S, accum_out=neg_mean[:])
+            return neg_mean
 
-        def fold_shift(t, gains, factor, tag):
-            table = keep.tile([P, TABLE_W], F32, name=f"shift{t}", tag=tag)
+        def square_sum(t, neg_mean, junk, squares):
+            nc.scalar.activation(junk, y_sb[t], ACT.Square, bias=neg_mean[:], accum_out=squares)
+
+        def inverse_std(rstd, squares):
+            nc.scalar.activation(rstd, squares, ACT.Abs_reciprocal_sqrt, scale=1.0 / S, bias=EPS)
+
+        def fold_shift(t, gains, factor):
+            table = keep.tile([P, TABLE_W], F32, name=f"shift{t}", tag="after_shift")
             nc.vector.scalar_tensor_tensor(table[:, :R], gains, factor, bet_raw[:, t - 1, :], ALU.mult, ALU.add)
             return table
 
         for h in range(2):
             copy_out(RAW[0], h)
             copy_out(FOLDED, h)
-        neg_mean, rstd = moments(FOLDED, keep.tile([P, S], BF16, name="junk")[:])
+        neg_mean = {FOLDED: minus_mean(FOLDED)}
+        squares_folded = col("squares_folded")
+        square_sum(FOLDED, neg_mean[FOLDED], keep.tile([P, S], BF16, name="junk")[:], squares_folded[:])
+        rstd_folded = col("rstd_folded")
+        inverse_std(rstd_folded[:], squares_folded[:])
         gains = keep.tile([P, TABLE_W], F32, name="gains")
-        nc.scalar.activation(gains[:, :R], gam_folded[:], ACT.Copy, scale=rstd[:])
+        nc.scalar.activation(gains[:, :R], gam_folded[:], ACT.Copy, scale=rstd_folded[:])
         for h in range(2):
             copy_out(RAW[1], h)
 
-        raw_gained = keep.tile([P, 2, S], F32, name="raw_gained", tag="after_rescale")
+        raw_gained = keep.tile([P, 2, S], F32, name="raw_gained")
         for i, t in enumerate(RAW):
             for cols in halves:
                 nc.vector.tensor_tensor(
                     raw_gained[:, i, cols], gam_raw[t][:].indirect(picks(cols)), y_sb[t][:, cols], ALU.mult
                 )
 
-        shifts = {FOLDED: fold_shift(FOLDED, gains[:, :R], neg_mean[:], "shift_folded")}
-        nc.vector.tensor_tensor(gained[:, FOLDED, :], gains[:].indirect(lab_t[:]), y_sb[FOLDED], ALU.mult)
+        shifts = {FOLDED: fold_shift(FOLDED, gains[:, :R], neg_mean[FOLDED][:])}
+        for h, cols in enumerate(halves):
+            nc.vector.tensor_tensor(
+                gained_folded[h][:], gains[:].indirect(picks(cols)), y_sb[FOLDED][:, cols], ALU.mult
+            )
+        for h, cols in enumerate(halves):
+            nc.vector.tensor_tensor(
+                res[:, FOLDED, cols], shifts[FOLDED][:].indirect(picks(cols)), gained_folded[h][:], ALU.add
+            )
+        nc.sync.dma_start(out_rows[:, FOLDED, :], res[:, FOLDED, :])
 
         late = keep.tile([P, PACK, S], F32, name="late", tag="after_gain")
         y_sb[EARLY] = late[:, FOLDED, :]
 
-        nc.vector.tensor_tensor(res[:, FOLDED, :], shifts[FOLDED][:].indirect(lab_t[:]), gained[:, FOLDED, :], ALU.add)
-        nc.sync.dma_start(out_rows[:, FOLDED, :], res[:, FOLDED, :])
+        squares_raw = keep.tile([P, 2], F32, name="squares_raw")
+        rstd_raw = keep.tile([P, 2], F32, name="rstd_raw")
+        for i, t in enumerate(RAW):
+            neg_mean[t] = minus_mean(t)
+            square_sum(t, neg_mean[t], late[:, t, :], squares_raw[:, i : i + 1])
+        inverse_std(rstd_raw[:], squares_raw[:])
+        offsets = {}
+        for i, t in enumerate(RAW):
+            factor = col(f"factor{t}")
+            nc.scalar.activation(factor[:], neg_mean[t][:], ACT.Copy, scale=rstd_raw[:, i : i + 1])
+            offsets[t] = keep.tile([P, R], F32, name=f"offset{t}")
+            nc.scalar.activation(offsets[t][:], gam_raw[t][:, :R], ACT.Copy, scale=factor[:])
+        for i, t in enumerate(RAW):
+            shifts[t] = keep.tile([P, TABLE_W], F32, name=f"shift{t}", tag="after_folded1" if i == 0 else "after_shift")
+            nc.gpsimd.tensor_tensor(shifts[t][:, :R], offsets[t][:], bet_raw[:, t - 1, :], ALU.add)
 
         for h in range(2):
             copy_out(EARLY, h)
-        neg_mean, rstd = moments(EARLY, late[:, EARLY, :])
+        neg_mean[EARLY] = minus_mean(EARLY)
+        squares_early = keep.tile([P, 1], F32, name="squares_early", tag="after_stats")
+        square_sum(EARLY, neg_mean[EARLY], late[:, EARLY, :], squares_early[:])
+        rstd_early = col("rstd_early")
+        inverse_std(rstd_early[:], squares_early[:])
         for cols in halves:
             nc.vector.scalar_tensor_tensor(
-                gained[:, EARLY, cols], y_sb[EARLY][:, cols], neg_mean[:], g_early[:, cols], ALU.add, ALU.mult
+                gained_early[:, cols], y[:, EARLY, cols], neg_mean[EARLY][:], g_early[:, cols], ALU.add, ALU.mult
             )
-        for cols, shifts_px in zip(parts, b_early):
+        pieces = [
+            (halves[0], b_early[0][:, :HALF]),
+            (slice(HALF, BEFORE_WORDS), b_early[0][:, HALF:]),
+            (parts[1], b_early[1][:]),
+        ]
+        for cols, shifts_px in pieces:
             nc.vector.scalar_tensor_tensor(
-                res[:, EARLY, cols], gained[:, EARLY, cols], rstd[:], shifts_px[:], ALU.mult, ALU.add
+                res[:, EARLY, cols], gained_early[:, cols], rstd_early[:], shifts_px, ALU.mult, ALU.add
             )
         nc.sync.dma_start(out_rows[:, EARLY, :], res[:, EARLY, :])
 
-        factors = {}
-        for i, t in enumerate(RAW):
-            neg_mean, rstd = moments(t, late[:, t, :])
-            factors[t] = col(f"c{t}")
-            nc.scalar.activation(factors[t][:], neg_mean[:], ACT.Copy, scale=rstd[:])
-            nc.scalar.activation(gained[:, t, :], raw_gained[:, i, :], ACT.Copy, scale=rstd[:])
-        for t, tag in zip(RAW, ("after_rescale", "after_centre")):
-            shifts[t] = fold_shift(t, gam_raw[t][:, :R], factors[t][:], tag)
+        rescaled = keep.tile([P, 2, S], F32, name="rescaled", tag="after_stats")
+        for cols in halves:
+            for i in range(2):
+                nc.scalar.activation(rescaled[:, i, cols], raw_gained[:, i, cols], ACT.Copy, scale=rstd_raw[:, i : i + 1])
 
         def runs(widths):
             return [slice(sum(widths[:c]), sum(widths[: c + 1])) for c in range(len(widths))]
 
         res_bf = keep.tile([P, S, PACK], BF16, name="res_bf", align_bytes=64)
         for cols in runs(CHUNKS):
-            for t in RAW:
-                nc.vector.tensor_tensor(res[:, t, cols], shifts[t][:].indirect(picks(cols)), gained[:, t, cols], ALU.add)
+            for i, t in enumerate(RAW):
+                nc.vector.tensor_tensor(res[:, t, cols], shifts[t][:].indirect(picks(cols)), rescaled[:, i, cols], ALU.add)
             nc.scalar.copy(
                 res_bf[:, cols, :].rearrange("p (c i) t -> p c t i", i=4),
                 res[:, :, cols].rearrange("p t (c i) -> p c t i", i=4),
@@ -206,7 +239,7 @@ def tile_picked_yspade_none_po_kernel(
                 scales=out_scales[:, cols],
                 in_=res_bf[:, cols, :].rearrange("p n t -> p (n t)"),
             )
-        for cols in runs(STORED):
+        for cols in runs(WORDS_STORED):
             nc.sync.dma_start(word_rows[:, cols], out_codes[:, cols].bitcast(I32))
 
         for q in range(4):

@@ -17,10 +17,11 @@ P = 128
 PACK = 4
 HALF = 512
 TABLE_W = 1376
+HALF_W = 704
 EPS = 1e-4
 CHUNKS = (128, 192, 192, 192, 192, 128)
 QUANTISED = (512, 256, 128, 128)
-STORED = (320, 384, 320)
+STORED = (320, 384, 192, 128)
 WORDS_STORED = (512, 256, 256)
 FLOPS = 2 * K * N * S
 BEFORE_WORDS = 768
@@ -35,17 +36,22 @@ def tile_picked_yspade_none_po_kernel(
     nc = tc.nc
     with ExitStack() as ctx:
         keep = ctx.enter_context(tc.tile_pool(name="keep", bufs=1))
+        shared = ctx.enter_context(tc.tile_pool(name="shared", bufs=1))
         psum = ctx.enter_context(tc.psum_pool(name="psum", bufs=1))
 
         lab_t = keep.tile([P, S // 16], U16, name="lab_t")
         offs_t = keep.tile([P, S // 16], U16, name="offs_t")
         gam_early = keep.tile([P, TABLE_W], F32, name="gam_early")
         bet_early = keep.tile([P, TABLE_W], F32, name="bet_early")
-        gam_raw = {t: keep.tile([P, TABLE_W], F32, name=f"gam_raw{t}") for t in RAW}
-        gam_folded = keep.tile([P, R], F32, name="gam_folded", tag="after_gain")
-        bet_raw = keep.tile([P, PACK - 1, R], F32, name="bet_raw")
+        xs = shared.tile([P, T], U8, name="xs", offset=4096)
+        gam_raw = {
+            RAW[0]: shared.tile([P, HALF_W], F32, name="gam_first", offset=4096 + 64),
+            RAW[1]: shared.tile([P, HALF_W], F32, name="gam_second", offset=4096 + T - 64),
+        }
+        gam_folded = shared.tile([P, R], F32, name="gam_folded", offset=4096 + 64 + 4 * HALF_W)
+        picked_bytes = keep.tile([P, S], U8, name="picked_bytes", tag="after_moves")
+        bet_raw = keep.tile([P, PACK - 1, R], F32, name="bet_raw", tag="after_moves")
         xw = keep.tile([P, T], U32, name="xw", tag="after_words")
-        xs = keep.tile([P, T], U8, name="xs", tag="after_bytes", align_bytes=64)
         w_raw = keep.tile([P, PACK, N], F32, name="w_raw")
         gam_rows = gam.rearrange("(p t) r -> p t r", t=PACK)
         bet_rows = bet.rearrange("(p t) r -> p t r", t=PACK)
@@ -53,22 +59,20 @@ def tile_picked_yspade_none_po_kernel(
 
         nc.gpsimd.memset(xs[:, : T // 2].bitcast(I32), 0)
         nc.vector.memset(xs[:, T // 2 :].bitcast(I32), 0)
+        x_bytes = keep.tile([P, S], U8, name="x_bytes", align_bytes=64)
+        nc.gpsimd.memset(x_bytes[:].bitcast(I32), 0)
         warm = keep.tile([P, 2], F32, name="warm")
         nc.vector.memset(warm[:, 0:1], 1.0)
         nc.scalar.activation(warm[:, 1:2], warm[:, 0:1], ACT.Abs_reciprocal_sqrt)
 
         nc.sync.dma_start(lab_t[:], lab)
         nc.sync.dma_start(gam_early[:, :R], gam_rows[:, EARLY, :])
-        nc.sync.dma_start(bet_early[:, :R], bet_rows[:, EARLY, :])
-        nc.sync.dma_start(w_raw[:], w_rows)
-        for q in range(4):
-            nc.sync.dma_start(xs[q:P:32, :].bitcast(I32), x_scales[0, q:16:4, :].bitcast(I32))
+        nc.sync.dma_start(w_raw[:, :2, :], w_rows[:, :2, :])
+        nc.sync.dma_start(xs[0:P:8, :].bitcast(I32), x_scales[0].bitcast(I32))
         nc.sync.dma_start(offs_t[:], offs)
+        nc.sync.dma_start(bet_early[:, :R], bet_rows[:, EARLY, :])
+        nc.sync.dma_start(w_raw[:, 2:, :], w_rows[:, 2:, :])
         nc.sync.dma_start(xw[:].bitcast(I32), x_words[0].rearrange("p n t -> p (n t)").bitcast(I32))
-        for t in RAW:
-            nc.sync.dma_start(gam_raw[t][:, :R], gam_rows[:, t, :])
-        nc.sync.dma_start(gam_folded[:], gam_rows[:, FOLDED, :])
-        nc.sync.dma_start(bet_raw[:], bet_rows[:, 1:, :])
 
         def picks(cols):
             return lab_t[:, cols.start // 16 : cols.stop // 16]
@@ -77,14 +81,19 @@ def tile_picked_yspade_none_po_kernel(
         parts = [slice(0, BEFORE_WORDS), slice(BEFORE_WORDS, S)]
         g_early = keep.tile([P, S], F32, name="g_early")
         nc.vector.tensor_copy(g_early[:], gam_early[:].indirect(lab_t[:]))
+        nc.vector.tensor_copy(picked_bytes[:], xs[:].indirect(offs_t[:]))
+        for q in range(4):
+            nc.sync.dma_start(x_bytes[q:P:32, :].bitcast(I32), picked_bytes[8 * q : P : 32, :].bitcast(I32))
+        for t in RAW:
+            nc.sync.dma_start(gam_raw[t][:, :R], gam_rows[:, t, :])
+        nc.sync.dma_start(gam_folded[:], gam_rows[:, FOLDED, :])
+        nc.sync.dma_start(bet_raw[:], bet_rows[:, 1:, :])
         b_early = [keep.tile([P, BEFORE_WORDS], F32, name="b_early0")]
         nc.vector.tensor_copy(b_early[0][:], bet_early[:].indirect(picks(parts[0])))
-        x_bytes = keep.tile([P, S], U8, name="x_bytes", align_bytes=64)
-        nc.vector.tensor_copy(x_bytes[:], xs[:].indirect(offs_t[:]))
 
         w_bf = keep.tile([P, PACK, P, PACK], BF16, name="w_bf", tag="after_quant", align_bytes=64)
         nc.scalar.copy(w_bf[:].rearrange("p t m j -> p m j t"), w_raw[:].rearrange("p j (m t) -> p m j t", t=PACK))
-        w_codes = keep.tile([P, N], U32, name="w_codes", tag="after_bytes", align_bytes=64)
+        w_codes = keep.tile([P, N], U32, name="w_codes", align_bytes=64)
         w_scales = keep.tile([P, N], U8, name="w_scales", align_bytes=64)
         nc.vector.quantize_mx(
             out=w_codes[:].bitcast(FP8X4), scales=w_scales[:], in_=w_bf[:].rearrange("p t m j -> p (t m j)")
@@ -149,7 +158,7 @@ def tile_picked_yspade_none_po_kernel(
         neg_mean = {FOLDED: minus_mean(FOLDED)}
         squares_folded = col("squares_folded")
         square_sum(FOLDED, neg_mean[FOLDED], keep.tile([P, S], BF16, name="junk")[:], squares_folded[:])
-        rstd_folded = col("rstd_folded")
+        rstd_folded = keep.tile([P, 1], F32, name="rstd_folded", tag="after_gain")
         inverse_std(rstd_folded[:], squares_folded[:])
         gains = keep.tile([P, TABLE_W], F32, name="gains")
         nc.scalar.activation(gains[:, :R], gam_folded[:], ACT.Copy, scale=rstd_folded[:])
@@ -190,7 +199,7 @@ def tile_picked_yspade_none_po_kernel(
             offsets[t] = keep.tile([P, R], F32, name=f"offset{t}")
             nc.scalar.activation(offsets[t][:], gam_raw[t][:, :R], ACT.Copy, scale=factor[:])
         for i, t in enumerate(RAW):
-            shifts[t] = keep.tile([P, TABLE_W], F32, name=f"shift{t}", tag="after_folded1" if i == 0 else "after_shift")
+            shifts[t] = keep.tile([P, TABLE_W], F32, name=f"shift{t}", tag="after_folded0" if i == 0 else "after_shift")
             nc.gpsimd.tensor_tensor(shifts[t][:, :R], offsets[t][:], bet_raw[:, t - 1, :], ALU.add)
 
         for h in range(2):

@@ -24,7 +24,8 @@ QUANTISED = (512, 256, 128, 128)
 STORED = (320, 384, 192, 128)
 WORDS_STORED = (512, 256, 256)
 FLOPS = 2 * K * N * S
-BEFORE_WORDS = 768
+BEFORE_WORDS = 512
+AFTER_WORDS = 256
 EARLY = 0
 FOLDED = 1
 RAW = (2, 3)
@@ -78,7 +79,7 @@ def tile_picked_yspade_none_po_kernel(
             return lab_t[:, cols.start // 16 : cols.stop // 16]
 
         halves = [slice(h * HALF, (h + 1) * HALF) for h in range(2)]
-        parts = [slice(0, BEFORE_WORDS), slice(BEFORE_WORDS, S)]
+        parts = [slice(0, BEFORE_WORDS), slice(BEFORE_WORDS, BEFORE_WORDS + AFTER_WORDS), slice(BEFORE_WORDS + AFTER_WORDS, S)]
         g_early = keep.tile([P, S], F32, name="g_early")
         nc.vector.tensor_copy(g_early[:], gam_early[:].indirect(lab_t[:]))
         nc.vector.tensor_copy(picked_bytes[:], xs[:].indirect(offs_t[:]))
@@ -91,17 +92,17 @@ def tile_picked_yspade_none_po_kernel(
         b_early = [keep.tile([P, BEFORE_WORDS], F32, name="b_early0")]
         nc.vector.tensor_copy(b_early[0][:], bet_early[:].indirect(picks(parts[0])))
 
-        w_bf = keep.tile([P, PACK, P, PACK], BF16, name="w_bf", tag="after_quant", align_bytes=64)
+        w_bf = keep.tile([P, PACK, P, PACK], BF16, name="w_bf", align_bytes=64)
         nc.scalar.copy(w_bf[:].rearrange("p t m j -> p m j t"), w_raw[:].rearrange("p j (m t) -> p m j t", t=PACK))
         w_codes = keep.tile([P, N], U32, name="w_codes", align_bytes=64)
         w_scales = keep.tile([P, N], U8, name="w_scales", align_bytes=64)
         nc.vector.quantize_mx(
             out=w_codes[:].bitcast(FP8X4), scales=w_scales[:], in_=w_bf[:].rearrange("p t m j -> p (t m j)")
         )
-        x_codes = keep.tile([P, S], U32, name="x_codes", tag="after_quant", align_bytes=64)
+        x_codes = keep.tile([P, S], U32, name="x_codes", align_bytes=64)
         for cols in halves:
             nc.vector.tensor_copy(x_codes[:, cols], xw[:].indirect(offs_t[:, cols.start // 16 : cols.stop // 16]))
-        b_early.append(keep.tile([P, S - BEFORE_WORDS], F32, name="b_early1", tag="after_words"))
+        b_early.append(keep.tile([P, AFTER_WORDS], F32, name="b_early1", tag="after_words"))
         nc.vector.tensor_copy(b_early[1][:], bet_early[:].indirect(picks(parts[1])))
 
         y = psum.tile([P, PACK, S], F32, name="y")
@@ -213,11 +214,9 @@ def tile_picked_yspade_none_po_kernel(
             nc.vector.scalar_tensor_tensor(
                 gained_early[:, cols], y[:, EARLY, cols], neg_mean[EARLY][:], g_early[:, cols], ALU.add, ALU.mult
             )
-        pieces = [
-            (halves[0], b_early[0][:, :HALF]),
-            (slice(HALF, BEFORE_WORDS), b_early[0][:, HALF:]),
-            (parts[1], b_early[1][:]),
-        ]
+        b_rest = g_early[:, : S - parts[2].start]
+        nc.vector.tensor_copy(b_rest, bet_early[:].indirect(picks(parts[2])))
+        pieces = zip(parts, (b_early[0][:], b_early[1][:], b_rest))
         for cols, shifts_px in pieces:
             nc.vector.scalar_tensor_tensor(
                 res[:, EARLY, cols], gained_early[:, cols], rstd_early[:], shifts_px, ALU.mult, ALU.add

@@ -16,19 +16,22 @@ K, T, S, N, R = 512, 4096, 1024, 512, 256
 P = 128
 PACK = 4
 HALF = 512
+EPS = 1e-4
+FLOPS = 2 * K * N * S
+
+EARLY, FOLDED, RAW = 0, 1, (2, 3)
 TABLE_W = 1376
 HALF_W = 704
-EPS = 1e-4
+BEFORE_WORDS = 256
+AFTER_WORDS = 512
 CHUNKS = (128, 192, 192, 192, 192, 128)
 QUANTISED = (512, 256, 128, 128)
 STORED = (320, 384, 192, 128)
 WORDS_STORED = (512, 256, 256)
-FLOPS = 2 * K * N * S
-BEFORE_WORDS = 512
-AFTER_WORDS = 256
-EARLY = 0
-FOLDED = 1
-RAW = (2, 3)
+
+
+def runs(widths):
+    return [slice(sum(widths[:c]), sum(widths[: c + 1])) for c in range(len(widths))]
 
 
 def tile_picked_yspade_none_po_kernel(
@@ -44,15 +47,12 @@ def tile_picked_yspade_none_po_kernel(
         offs_t = keep.tile([P, S // 16], U16, name="offs_t")
         gam_early = keep.tile([P, TABLE_W], F32, name="gam_early")
         bet_early = keep.tile([P, TABLE_W], F32, name="bet_early")
-        xs = shared.tile([P, T], U8, name="xs", offset=4096)
-        gam_raw = {
-            RAW[0]: shared.tile([P, HALF_W], F32, name="gam_first", offset=4096 + 64),
-            RAW[1]: shared.tile([P, HALF_W], F32, name="gam_second", offset=4096 + T - 64),
-        }
-        gam_folded = shared.tile([P, R], F32, name="gam_folded", offset=4096 + 64 + 4 * HALF_W)
+        xs = shared.tile([P, T], U8, name="xs", offset=0)
+        gam_raw = {t: shared.tile([P, HALF_W], F32, name=f"gam_raw{t}", offset=4 * HALF_W * i) for i, t in enumerate(RAW)}
+        gam_folded = bet_early[:, S : S + R]
         picked_bytes = keep.tile([P, S], U8, name="picked_bytes", tag="after_moves")
-        bet_raw = keep.tile([P, PACK - 1, R], F32, name="bet_raw", tag="after_moves")
-        xw = keep.tile([P, T], U32, name="xw", tag="after_words")
+        bet_late = keep.tile([P, PACK - 1, R], F32, name="bet_late", tag="after_moves")
+        xw = keep.tile([P, T], U32, name="xw")
         w_raw = keep.tile([P, PACK, N], F32, name="w_raw")
         gam_rows = gam.rearrange("(p t) r -> p t r", t=PACK)
         bet_rows = bet.rearrange("(p t) r -> p t r", t=PACK)
@@ -71,15 +71,16 @@ def tile_picked_yspade_none_po_kernel(
         nc.sync.dma_start(w_raw[:, :2, :], w_rows[:, :2, :])
         nc.sync.dma_start(xs[0:P:8, :].bitcast(I32), x_scales[0].bitcast(I32))
         nc.sync.dma_start(offs_t[:], offs)
-        nc.sync.dma_start(bet_early[:, :R], bet_rows[:, EARLY, :])
         nc.sync.dma_start(w_raw[:, 2:, :], w_rows[:, 2:, :])
+        nc.sync.dma_start(bet_early[:, :R], bet_rows[:, EARLY, :])
         nc.sync.dma_start(xw[:].bitcast(I32), x_words[0].rearrange("p n t -> p (n t)").bitcast(I32))
+        nc.sync.dma_start(gam_folded, gam_rows[:, FOLDED, :])
 
         def picks(cols):
             return lab_t[:, cols.start // 16 : cols.stop // 16]
 
-        halves = [slice(h * HALF, (h + 1) * HALF) for h in range(2)]
-        parts = [slice(0, BEFORE_WORDS), slice(BEFORE_WORDS, BEFORE_WORDS + AFTER_WORDS), slice(BEFORE_WORDS + AFTER_WORDS, S)]
+        halves = runs((HALF, HALF))
+        before, after, rest = runs((BEFORE_WORDS, AFTER_WORDS, S - BEFORE_WORDS - AFTER_WORDS))
         g_early = keep.tile([P, S], F32, name="g_early")
         nc.vector.tensor_copy(g_early[:], gam_early[:].indirect(lab_t[:]))
         nc.vector.tensor_copy(picked_bytes[:], xs[:].indirect(offs_t[:]))
@@ -87,10 +88,10 @@ def tile_picked_yspade_none_po_kernel(
             nc.sync.dma_start(x_bytes[q:P:32, :].bitcast(I32), picked_bytes[8 * q : P : 32, :].bitcast(I32))
         for t in RAW:
             nc.sync.dma_start(gam_raw[t][:, :R], gam_rows[:, t, :])
-        nc.sync.dma_start(gam_folded[:], gam_rows[:, FOLDED, :])
-        nc.sync.dma_start(bet_raw[:], bet_rows[:, 1:, :])
-        b_early = [keep.tile([P, BEFORE_WORDS], F32, name="b_early0")]
-        nc.vector.tensor_copy(b_early[0][:], bet_early[:].indirect(picks(parts[0])))
+        nc.sync.dma_start(bet_late[:], bet_rows[:, EARLY + 1 :, :])
+        res = keep.tile([P, PACK, S], F32, name="res")
+        b_early = res[:, RAW[1], :]
+        nc.vector.tensor_copy(b_early[:, before], bet_early[:, :S].indirect(picks(before)))
 
         w_bf = keep.tile([P, PACK, P, PACK], BF16, name="w_bf", align_bytes=64)
         nc.scalar.copy(w_bf[:].rearrange("p t m j -> p m j t"), w_raw[:].rearrange("p j (m t) -> p m j t", t=PACK))
@@ -102,8 +103,7 @@ def tile_picked_yspade_none_po_kernel(
         x_codes = keep.tile([P, S], U32, name="x_codes", align_bytes=64)
         for cols in halves:
             nc.vector.tensor_copy(x_codes[:, cols], xw[:].indirect(offs_t[:, cols.start // 16 : cols.stop // 16]))
-        b_early.append(keep.tile([P, AFTER_WORDS], F32, name="b_early1", tag="after_words"))
-        nc.vector.tensor_copy(b_early[1][:], bet_early[:].indirect(picks(parts[1])))
+        nc.vector.tensor_copy(b_early[:, after], bet_early[:].indirect(picks(after)))
 
         y = psum.tile([P, PACK, S], F32, name="y")
         for pair in ((RAW[0], FOLDED), (RAW[1], EARLY)):
@@ -122,8 +122,7 @@ def tile_picked_yspade_none_po_kernel(
         def col(name):
             return keep.tile([P, 1], F32, name=name)
 
-        res = keep.tile([P, PACK, S], F32, name="res")
-        gained_early = keep.tile([P, S], F32, name="gained_early")
+        gained_early = res[:, RAW[0], :]
         gained_folded = [keep.tile([P, HALF], F32, name=f"gained_folded{h}", tag=f"after_folded{h}") for h in range(2)]
         out_codes = keep.tile([P, S], U32, name="out_codes", align_bytes=64)
         out_scales = keep.tile([P, S], U8, name="out_scales", align_bytes=64)
@@ -131,38 +130,35 @@ def tile_picked_yspade_none_po_kernel(
         word_rows = out_1[0].rearrange("p n t -> p (n t)").bitcast(I32)
 
         y_sb = {t: keep.tile([P, S], F32, name=f"y_sb{t}")[:] for t in (FOLDED,) + RAW}
-        sums = [keep.tile([P, 2], F32, name=f"sums{t}") for t in range(PACK)]
+        sums = [
+            keep.tile([P, 2], F32, name=f"sums{t}", tag="after_mean" if t == EARLY else f"sums{t}") for t in range(PACK)
+        ]
 
         def copy_out(t, h):
             nc.scalar.activation(y_sb[t][:, halves[h]], y[:, t, halves[h]], ACT.Copy, accum_out=sums[t][:, h : h + 1])
 
         def minus_mean(t):
             shares = keep.tile([P, 2], F32, name=f"shares{t}")
-            neg_mean = col(f"nm{t}")
-            nc.scalar.activation(shares[:], sums[t][:], ACT.Copy, scale=-1.0 / S, accum_out=neg_mean[:])
-            return neg_mean
+            total = col(f"neg_mean{t}")
+            nc.scalar.activation(shares[:], sums[t][:], ACT.Copy, scale=-1.0 / S, accum_out=total[:])
+            return total
 
-        def square_sum(t, neg_mean, junk, squares):
-            nc.scalar.activation(junk, y_sb[t], ACT.Square, bias=neg_mean[:], accum_out=squares)
+        def square_sum(t, unused_squares, total):
+            nc.scalar.activation(unused_squares, y_sb[t], ACT.Square, bias=neg_mean[t][:], accum_out=total)
 
         def inverse_std(rstd, squares):
             nc.scalar.activation(rstd, squares, ACT.Abs_reciprocal_sqrt, scale=1.0 / S, bias=EPS)
-
-        def fold_shift(t, gains, factor):
-            table = keep.tile([P, TABLE_W], F32, name=f"shift{t}", tag="after_shift")
-            nc.vector.scalar_tensor_tensor(table[:, :R], gains, factor, bet_raw[:, t - 1, :], ALU.mult, ALU.add)
-            return table
 
         for h in range(2):
             copy_out(RAW[0], h)
             copy_out(FOLDED, h)
         neg_mean = {FOLDED: minus_mean(FOLDED)}
         squares_folded = col("squares_folded")
-        square_sum(FOLDED, neg_mean[FOLDED], keep.tile([P, S], BF16, name="junk")[:], squares_folded[:])
-        rstd_folded = keep.tile([P, 1], F32, name="rstd_folded", tag="after_gain")
+        square_sum(FOLDED, keep.tile([P, S], BF16, name="unused_squares")[:], squares_folded[:])
+        rstd_folded = keep.tile([P, 1], F32, name="rstd_folded", tag="after_gains")
         inverse_std(rstd_folded[:], squares_folded[:])
         gains = keep.tile([P, TABLE_W], F32, name="gains")
-        nc.scalar.activation(gains[:, :R], gam_folded[:], ACT.Copy, scale=rstd_folded[:])
+        nc.scalar.activation(gains[:, :R], gam_folded, ACT.Copy, scale=rstd_folded[:])
         for h in range(2):
             copy_out(RAW[1], h)
 
@@ -173,7 +169,10 @@ def tile_picked_yspade_none_po_kernel(
                     raw_gained[:, i, cols], gam_raw[t][:].indirect(picks(cols)), y_sb[t][:, cols], ALU.mult
                 )
 
-        shifts = {FOLDED: fold_shift(FOLDED, gains[:, :R], neg_mean[FOLDED][:])}
+        shifts = {FOLDED: keep.tile([P, TABLE_W], F32, name="shifts_folded", tag="after_shifts")}
+        nc.vector.scalar_tensor_tensor(
+            shifts[FOLDED][:, :R], gains[:, :R], neg_mean[FOLDED][:], bet_late[:, FOLDED - 1, :], ALU.mult, ALU.add
+        )
         for h, cols in enumerate(halves):
             nc.vector.tensor_tensor(
                 gained_folded[h][:], gains[:].indirect(picks(cols)), y_sb[FOLDED][:, cols], ALU.mult
@@ -184,52 +183,49 @@ def tile_picked_yspade_none_po_kernel(
             )
         nc.sync.dma_start(out_rows[:, FOLDED, :], res[:, FOLDED, :])
 
-        late = keep.tile([P, PACK, S], F32, name="late", tag="after_gain")
+        late = keep.tile([P, PACK, S], F32, name="late", tag="after_gains")
         y_sb[EARLY] = late[:, FOLDED, :]
 
         squares_raw = keep.tile([P, 2], F32, name="squares_raw")
         rstd_raw = keep.tile([P, 2], F32, name="rstd_raw")
         for i, t in enumerate(RAW):
             neg_mean[t] = minus_mean(t)
-            square_sum(t, neg_mean[t], late[:, t, :], squares_raw[:, i : i + 1])
+            square_sum(t, late[:, t, :], squares_raw[:, i : i + 1])
         inverse_std(rstd_raw[:], squares_raw[:])
-        offsets = {}
+        centring = {}
         for i, t in enumerate(RAW):
             factor = col(f"factor{t}")
             nc.scalar.activation(factor[:], neg_mean[t][:], ACT.Copy, scale=rstd_raw[:, i : i + 1])
-            offsets[t] = keep.tile([P, R], F32, name=f"offset{t}")
-            nc.scalar.activation(offsets[t][:], gam_raw[t][:, :R], ACT.Copy, scale=factor[:])
-        for i, t in enumerate(RAW):
-            shifts[t] = keep.tile([P, TABLE_W], F32, name=f"shift{t}", tag="after_folded0" if i == 0 else "after_shift")
-            nc.gpsimd.tensor_tensor(shifts[t][:, :R], offsets[t][:], bet_raw[:, t - 1, :], ALU.add)
+            centring[t] = keep.tile([P, R], F32, name=f"centring{t}")
+            nc.scalar.activation(centring[t][:], gam_raw[t][:, :R], ACT.Copy, scale=factor[:])
+        for t, tag in zip(RAW, ("after_folded0", "after_shifts")):
+            shifts[t] = keep.tile([P, TABLE_W], F32, name=f"shifts{t}", tag=tag)
+            nc.gpsimd.tensor_tensor(shifts[t][:, :R], centring[t][:], bet_late[:, t - 1, :], ALU.add)
 
         for h in range(2):
             copy_out(EARLY, h)
         neg_mean[EARLY] = minus_mean(EARLY)
-        squares_early = keep.tile([P, 1], F32, name="squares_early", tag="after_stats")
-        square_sum(EARLY, neg_mean[EARLY], late[:, EARLY, :], squares_early[:])
+        squares_early = col("squares_early")
+        square_sum(EARLY, late[:, EARLY, :], squares_early[:])
         rstd_early = col("rstd_early")
         inverse_std(rstd_early[:], squares_early[:])
         for cols in halves:
             nc.vector.scalar_tensor_tensor(
                 gained_early[:, cols], y[:, EARLY, cols], neg_mean[EARLY][:], g_early[:, cols], ALU.add, ALU.mult
             )
-        b_rest = g_early[:, : S - parts[2].start]
-        nc.vector.tensor_copy(b_rest, bet_early[:].indirect(picks(parts[2])))
-        pieces = zip(parts, (b_early[0][:], b_early[1][:], b_rest))
-        for cols, shifts_px in pieces:
+        b_rest = g_early[:, : S - rest.start]
+        nc.vector.tensor_copy(b_rest, bet_early[:].indirect(picks(rest)))
+        middle = slice(HALF, rest.start)
+        for cols, shifts_px in ((halves[0], b_early[:, halves[0]]), (middle, b_early[:, middle]), (rest, b_rest)):
             nc.vector.scalar_tensor_tensor(
                 res[:, EARLY, cols], gained_early[:, cols], rstd_early[:], shifts_px, ALU.mult, ALU.add
             )
         nc.sync.dma_start(out_rows[:, EARLY, :], res[:, EARLY, :])
 
-        rescaled = keep.tile([P, 2, S], F32, name="rescaled", tag="after_stats")
+        rescaled = keep.tile([P, 2, S], F32, name="rescaled", tag="after_mean")
         for cols in halves:
             for i in range(2):
                 nc.scalar.activation(rescaled[:, i, cols], raw_gained[:, i, cols], ACT.Copy, scale=rstd_raw[:, i : i + 1])
-
-        def runs(widths):
-            return [slice(sum(widths[:c]), sum(widths[: c + 1])) for c in range(len(widths))]
 
         res_bf = keep.tile([P, S, PACK], BF16, name="res_bf", align_bytes=64)
         for cols in runs(CHUNKS):

@@ -22,7 +22,7 @@ FLOPS = 2 * K * N * S
 EARLY, FOLDED, RAW = 0, 1, (2, 3)
 TABLE_W = 1376
 HALF_W = 704
-BEFORE_WORDS = 256
+BEFORE_WORDS = 512
 AFTER_WORDS = 512
 CHUNKS = (128, 192, 192, 192, 192, 128)
 QUANTISED = (512, 256, 128, 128)
@@ -80,7 +80,7 @@ def tile_picked_yspade_none_po_kernel(
             return lab_t[:, cols.start // 16 : cols.stop // 16]
 
         halves = runs((HALF, HALF))
-        before, after, rest = runs((BEFORE_WORDS, AFTER_WORDS, S - BEFORE_WORDS - AFTER_WORDS))
+        before, after = runs((BEFORE_WORDS, AFTER_WORDS))
         g_early = keep.tile([P, S], F32, name="g_early")
         nc.vector.tensor_copy(g_early[:], gam_early[:].indirect(lab_t[:]))
         nc.vector.tensor_copy(picked_bytes[:], xs[:].indirect(offs_t[:]))
@@ -119,6 +119,8 @@ def tile_picked_yspade_none_po_kernel(
                         stop=True,
                     )
 
+        partial_sums = y[:, RAW[0], :P]
+
         def col(name):
             return keep.tile([P, 1], F32, name=name)
 
@@ -131,7 +133,7 @@ def tile_picked_yspade_none_po_kernel(
 
         y_sb = {t: keep.tile([P, S], F32, name=f"y_sb{t}")[:] for t in (FOLDED,) + RAW}
         sums = [
-            keep.tile([P, 2], F32, name=f"sums{t}", tag="after_mean" if t == EARLY else f"sums{t}") for t in range(PACK)
+            keep.tile([P, 2], F32, name=f"sums{t}", tag=f"sums{t}") for t in range(PACK)
         ]
 
         def copy_out(t, h):
@@ -184,9 +186,9 @@ def tile_picked_yspade_none_po_kernel(
         nc.sync.dma_start(out_rows[:, FOLDED, :], res[:, FOLDED, :])
 
         late = keep.tile([P, PACK, S], F32, name="late", tag="after_gains")
-        y_sb[EARLY] = late[:, FOLDED, :]
 
         squares_raw = keep.tile([P, 2], F32, name="squares_raw")
+        factors = keep.tile([P, 2], F32, name="factors", tag="after_mean")
         rstd_raw = keep.tile([P, 2], F32, name="rstd_raw")
         for i, t in enumerate(RAW):
             neg_mean[t] = minus_mean(t)
@@ -194,31 +196,44 @@ def tile_picked_yspade_none_po_kernel(
         inverse_std(rstd_raw[:], squares_raw[:])
         centring = {}
         for i, t in enumerate(RAW):
-            factor = col(f"factor{t}")
-            nc.scalar.activation(factor[:], neg_mean[t][:], ACT.Copy, scale=rstd_raw[:, i : i + 1])
+            factor = factors[:, i : i + 1]
+            nc.scalar.activation(factor, neg_mean[t][:], ACT.Copy, scale=rstd_raw[:, i : i + 1])
             centring[t] = keep.tile([P, R], F32, name=f"centring{t}")
-            nc.scalar.activation(centring[t][:], gam_raw[t][:, :R], ACT.Copy, scale=factor[:])
+            nc.scalar.activation(centring[t][:], gam_raw[t][:, :R], ACT.Copy, scale=factor)
         for t, tag in zip(RAW, ("after_folded0", "after_shifts")):
             shifts[t] = keep.tile([P, TABLE_W], F32, name=f"shifts{t}", tag=tag)
             nc.gpsimd.tensor_tensor(shifts[t][:, :R], centring[t][:], bet_late[:, t - 1, :], ALU.add)
 
-        for h in range(2):
-            copy_out(EARLY, h)
-        neg_mean[EARLY] = minus_mean(EARLY)
-        squares_early = col("squares_early")
-        square_sum(EARLY, late[:, EARLY, :], squares_early[:])
+        for c, cols in enumerate(runs((P,) * 8)):
+            nc.tensor.matmul_mx(
+                out=partial_sums,
+                lhsT=w_codes[:, EARLY * P : (EARLY + 1) * P].bitcast(FP8X4),
+                lhsT_scale=w_scales[:, EARLY * P : (EARLY + 1) * P],
+                rhs=x_codes[:, cols].bitcast(FP8X4),
+                rhs_scale=x_bytes[:, cols],
+                start=c == 0,
+                stop=c == 7,
+            )
+        neg_mean[EARLY] = col("neg_mean_early")
+        nc.scalar.activation(late[:, FOLDED, :P], partial_sums, ACT.Copy, scale=-1.0 / S, accum_out=neg_mean[EARLY][:])
+        for h, cols in enumerate(halves):
+            nc.scalar.activation(
+                late[:, EARLY, cols], y[:, EARLY, cols], ACT.Square, bias=neg_mean[EARLY][:],
+                accum_out=sums[EARLY][:, h : h + 1],
+            )
+        first_half = col("first_half")
+        nc.scalar.activation(first_half[:], sums[EARLY][:, 0:1], ACT.Identity, scale=1.0 / S, bias=EPS)
         rstd_early = col("rstd_early")
-        inverse_std(rstd_early[:], squares_early[:])
+        nc.scalar.activation(
+            rstd_early[:], sums[EARLY][:, 1:2], ACT.Abs_reciprocal_sqrt, scale=1.0 / S, bias=first_half[:]
+        )
         for cols in halves:
             nc.vector.scalar_tensor_tensor(
                 gained_early[:, cols], y[:, EARLY, cols], neg_mean[EARLY][:], g_early[:, cols], ALU.add, ALU.mult
             )
-        b_rest = g_early[:, : S - rest.start]
-        nc.vector.tensor_copy(b_rest, bet_early[:].indirect(picks(rest)))
-        middle = slice(HALF, rest.start)
-        for cols, shifts_px in ((halves[0], b_early[:, halves[0]]), (middle, b_early[:, middle]), (rest, b_rest)):
+        for cols in halves:
             nc.vector.scalar_tensor_tensor(
-                res[:, EARLY, cols], gained_early[:, cols], rstd_early[:], shifts_px, ALU.mult, ALU.add
+                res[:, EARLY, cols], gained_early[:, cols], rstd_early[:], b_early[:, cols], ALU.mult, ALU.add
             )
         nc.sync.dma_start(out_rows[:, EARLY, :], res[:, EARLY, :])
 

@@ -27,7 +27,7 @@ AFTER_WORDS = 512
 CHUNKS = (128, 192, 192, 192, 192, 128)
 QUANTISED = (512, 256, 128, 128)
 STORED = (320, 384, 192, 128)
-WORDS_STORED = (512, 256, 256)
+WORDS_STORED = (512, 512)
 
 
 def runs(widths):
@@ -262,5 +262,4 @@ def tile_picked_yspade_none_po_kernel(
             nc.sync.dma_start(word_rows[:, cols], out_codes[:, cols].bitcast(I32))
 
         for q in range(4):
-            queue = nc.sync if q % 2 else nc.scalar
-            queue.dma_start(out_2[0, q:16:4, :].bitcast(I32), out_scales[q:P:32, :].bitcast(I32))
+            nc.scalar.dma_start(out_2[0, q:16:4, :].bitcast(I32), out_scales[q:P:32, :].bitcast(I32))

@@ -22,12 +22,9 @@ FLOPS = 2 * K * N * S
 EARLY, FOLDED, RAW = 0, 1, (2, 3)
 TABLE_W = 1376
 HALF_W = 704
-BEFORE_WORDS = 512
-AFTER_WORDS = 512
 CHUNKS = (128, 192, 192, 192, 192, 128)
 QUANTISED = (512, 256, 128, 128)
 STORED = (320, 384, 192, 128)
-WORDS_STORED = (512, 512)
 
 
 def runs(widths):
@@ -80,7 +77,6 @@ def tile_picked_yspade_none_po_kernel(
             return lab_t[:, cols.start // 16 : cols.stop // 16]
 
         halves = runs((HALF, HALF))
-        before, after = runs((BEFORE_WORDS, AFTER_WORDS))
         g_early = keep.tile([P, S], F32, name="g_early")
         nc.vector.tensor_copy(g_early[:], gam_early[:].indirect(lab_t[:]))
         nc.vector.tensor_copy(picked_bytes[:], xs[:].indirect(offs_t[:]))
@@ -91,7 +87,7 @@ def tile_picked_yspade_none_po_kernel(
         nc.sync.dma_start(bet_late[:], bet_rows[:, EARLY + 1 :, :])
         res = keep.tile([P, PACK, S], F32, name="res")
         b_early = res[:, RAW[1], :]
-        nc.vector.tensor_copy(b_early[:, before], bet_early[:, :S].indirect(picks(before)))
+        nc.vector.tensor_copy(b_early[:, halves[0]], bet_early[:, :S].indirect(picks(halves[0])))
 
         w_bf = keep.tile([P, PACK, P, PACK], BF16, name="w_bf", align_bytes=64)
         nc.scalar.copy(w_bf[:].rearrange("p t m j -> p m j t"), w_raw[:].rearrange("p j (m t) -> p m j t", t=PACK))
@@ -103,23 +99,24 @@ def tile_picked_yspade_none_po_kernel(
         x_codes = keep.tile([P, S], U32, name="x_codes", align_bytes=64)
         for cols in halves:
             nc.vector.tensor_copy(x_codes[:, cols], xw[:].indirect(offs_t[:, cols.start // 16 : cols.stop // 16]))
-        nc.vector.tensor_copy(b_early[:, after], bet_early[:].indirect(picks(after)))
+        nc.vector.tensor_copy(b_early[:, halves[1]], bet_early[:].indirect(picks(halves[1])))
+
+        def product(out, t, cols, start, stop):
+            nc.tensor.matmul_mx(
+                out=out,
+                lhsT=w_codes[:, t * P : (t + 1) * P].bitcast(FP8X4),
+                lhsT_scale=w_scales[:, t * P : (t + 1) * P],
+                rhs=x_codes[:, cols].bitcast(FP8X4),
+                rhs_scale=x_bytes[:, cols],
+                start=start,
+                stop=stop,
+            )
 
         y = psum.tile([P, PACK, S], F32, name="y")
         for pair in ((RAW[0], FOLDED), (RAW[1], EARLY)):
             for cols in halves:
                 for t in pair:
-                    nc.tensor.matmul_mx(
-                        out=y[:, t, cols],
-                        lhsT=w_codes[:, t * P : (t + 1) * P].bitcast(FP8X4),
-                        lhsT_scale=w_scales[:, t * P : (t + 1) * P],
-                        rhs=x_codes[:, cols].bitcast(FP8X4),
-                        rhs_scale=x_bytes[:, cols],
-                        start=True,
-                        stop=True,
-                    )
-
-        partial_sums = y[:, RAW[0], :P]
+                    product(y[:, t, cols], t, cols, True, True)
 
         def col(name):
             return keep.tile([P, 1], F32, name=name)
@@ -132,9 +129,7 @@ def tile_picked_yspade_none_po_kernel(
         word_rows = out_1[0].rearrange("p n t -> p (n t)").bitcast(I32)
 
         y_sb = {t: keep.tile([P, S], F32, name=f"y_sb{t}")[:] for t in (FOLDED,) + RAW}
-        sums = [
-            keep.tile([P, 2], F32, name=f"sums{t}", tag=f"sums{t}") for t in range(PACK)
-        ]
+        sums = [keep.tile([P, 2], F32, name=f"sums{t}") for t in range(PACK)]
 
         def copy_out(t, h):
             nc.scalar.activation(y_sb[t][:, halves[h]], y[:, t, halves[h]], ACT.Copy, accum_out=sums[t][:, h : h + 1])
@@ -148,8 +143,8 @@ def tile_picked_yspade_none_po_kernel(
         def square_sum(t, unused_squares, total):
             nc.scalar.activation(unused_squares, y_sb[t], ACT.Square, bias=neg_mean[t][:], accum_out=total)
 
-        def inverse_std(rstd, squares):
-            nc.scalar.activation(rstd, squares, ACT.Abs_reciprocal_sqrt, scale=1.0 / S, bias=EPS)
+        def inverse_std(rstd, squares, bias=EPS):
+            nc.scalar.activation(rstd, squares, ACT.Abs_reciprocal_sqrt, scale=1.0 / S, bias=bias)
 
         for h in range(2):
             copy_out(RAW[0], h)
@@ -188,7 +183,7 @@ def tile_picked_yspade_none_po_kernel(
         late = keep.tile([P, PACK, S], F32, name="late", tag="after_gains")
 
         squares_raw = keep.tile([P, 2], F32, name="squares_raw")
-        factors = keep.tile([P, 2], F32, name="factors", tag="after_mean")
+        factors = keep.tile([P, 2], F32, name="factors", tag="after_centring")
         rstd_raw = keep.tile([P, 2], F32, name="rstd_raw")
         for i, t in enumerate(RAW):
             neg_mean[t] = minus_mean(t)
@@ -204,29 +199,25 @@ def tile_picked_yspade_none_po_kernel(
             shifts[t] = keep.tile([P, TABLE_W], F32, name=f"shifts{t}", tag=tag)
             nc.gpsimd.tensor_tensor(shifts[t][:, :R], centring[t][:], bet_late[:, t - 1, :], ALU.add)
 
-        for c, cols in enumerate(runs((P,) * 8)):
-            nc.tensor.matmul_mx(
-                out=partial_sums,
-                lhsT=w_codes[:, EARLY * P : (EARLY + 1) * P].bitcast(FP8X4),
-                lhsT_scale=w_scales[:, EARLY * P : (EARLY + 1) * P],
-                rhs=x_codes[:, cols].bitcast(FP8X4),
-                rhs_scale=x_bytes[:, cols],
-                start=c == 0,
-                stop=c == 7,
-            )
+        partial_sums = y[:, RAW[0], :P]
+        blocks = runs((P,) * (S // P))
+        for cols in blocks:
+            product(partial_sums, EARLY, cols, cols == blocks[0], cols == blocks[-1])
         neg_mean[EARLY] = col("neg_mean_early")
         nc.scalar.activation(late[:, FOLDED, :P], partial_sums, ACT.Copy, scale=-1.0 / S, accum_out=neg_mean[EARLY][:])
         for h, cols in enumerate(halves):
             nc.scalar.activation(
-                late[:, EARLY, cols], y[:, EARLY, cols], ACT.Square, bias=neg_mean[EARLY][:],
+                late[:, EARLY, cols],
+                y[:, EARLY, cols],
+                ACT.Square,
+                bias=neg_mean[EARLY][:],
                 accum_out=sums[EARLY][:, h : h + 1],
             )
         first_half = col("first_half")
         nc.scalar.activation(first_half[:], sums[EARLY][:, 0:1], ACT.Identity, scale=1.0 / S, bias=EPS)
         rstd_early = col("rstd_early")
-        nc.scalar.activation(
-            rstd_early[:], sums[EARLY][:, 1:2], ACT.Abs_reciprocal_sqrt, scale=1.0 / S, bias=first_half[:]
-        )
+        inverse_std(rstd_early[:], sums[EARLY][:, 1:2], bias=first_half[:])
+
         for cols in halves:
             nc.vector.scalar_tensor_tensor(
                 gained_early[:, cols], y[:, EARLY, cols], neg_mean[EARLY][:], g_early[:, cols], ALU.add, ALU.mult
@@ -237,7 +228,7 @@ def tile_picked_yspade_none_po_kernel(
             )
         nc.sync.dma_start(out_rows[:, EARLY, :], res[:, EARLY, :])
 
-        rescaled = keep.tile([P, 2, S], F32, name="rescaled", tag="after_mean")
+        rescaled = keep.tile([P, 2, S], F32, name="rescaled", tag="after_centring")
         for cols in halves:
             for i in range(2):
                 nc.scalar.activation(rescaled[:, i, cols], raw_gained[:, i, cols], ACT.Copy, scale=rstd_raw[:, i : i + 1])
@@ -258,7 +249,7 @@ def tile_picked_yspade_none_po_kernel(
                 scales=out_scales[:, cols],
                 in_=res_bf[:, cols, :].rearrange("p n t -> p (n t)"),
             )
-        for cols in runs(WORDS_STORED):
+        for cols in halves:
             nc.sync.dma_start(word_rows[:, cols], out_codes[:, cols].bitcast(I32))
 
         for q in range(4):

@@ -63,8 +63,8 @@ def tile_picked_yspade_none_po_kernel(
         nc.vector.memset(warm[:, 0:1], 1.0)
         nc.scalar.activation(warm[:, 1:2], warm[:, 0:1], ACT.Abs_reciprocal_sqrt)
 
-        nc.sync.dma_start(lab_t[:], lab)
         nc.sync.dma_start(gam_early[:, :R], gam_rows[:, EARLY, :])
+        nc.sync.dma_start(lab_t[:], lab)
         nc.sync.dma_start(w_raw[:, :2, :], w_rows[:, :2, :])
         nc.sync.dma_start(xs[0:P:8, :].bitcast(I32), x_scales[0].bitcast(I32))
         nc.sync.dma_start(offs_t[:], offs)

@@ -24,7 +24,8 @@ TABLE_W = 1376
 HALF_W = 704
 CHUNKS = (128, 192, 192, 192, 192, 128)
 QUANTISED = (512, 256, 128, 128)
-STORED = (320, 384, 192, 128)
+STORED = (320, 192, 192, 192, 128)
+WORDS_STORED = (512, 256, 256)
 
 
 def runs(widths):
@@ -249,7 +250,7 @@ def tile_picked_yspade_none_po_kernel(
                 scales=out_scales[:, cols],
                 in_=res_bf[:, cols, :].rearrange("p n t -> p (n t)"),
             )
-        for cols in halves:
+        for cols in runs(WORDS_STORED):
             nc.sync.dma_start(word_rows[:, cols], out_codes[:, cols].bitcast(I32))
 
         for q in range(4):

@@ -19,12 +19,9 @@ HALF = 512
 EPS = 1e-4
 FLOPS = 2 * K * N * S
 
-EARLY, FOLDED, RAW = 0, 1, (2, 3)
-TABLE_W = 1376
-HALF_W = 704
-CHUNKS = (128, 192, 192, 192, 192, 128)
-QUANTISED = (512, 256, 128, 128)
-STORED = (320, 192, 192, 192, 128)
+SCALAR_W = 1040
+VECTOR_W = 1376
+CHUNKS = (256, 256, 256, 128, 128)
 WORDS_STORED = (512, 256, 256)
 
 
@@ -43,13 +40,12 @@ def tile_picked_yspade_none_po_kernel(
 
         lab_t = keep.tile([P, S // 16], U16, name="lab_t")
         offs_t = keep.tile([P, S // 16], U16, name="offs_t")
-        gam_early = keep.tile([P, TABLE_W], F32, name="gam_early")
-        bet_early = keep.tile([P, TABLE_W], F32, name="bet_early")
-        xs = shared.tile([P, T], U8, name="xs", offset=0)
-        gam_raw = {t: shared.tile([P, HALF_W], F32, name=f"gam_raw{t}", offset=4 * HALF_W * i) for i, t in enumerate(RAW)}
-        gam_folded = bet_early[:, S : S + R]
-        picked_bytes = keep.tile([P, S], U8, name="picked_bytes", tag="after_moves")
-        bet_late = keep.tile([P, PACK - 1, R], F32, name="bet_late", tag="after_moves")
+        gam_t = [keep.tile([P, VECTOR_W if t == 3 else SCALAR_W], F32, name=f"gam{t}") for t in range(PACK)]
+        table = 4 * SCALAR_W
+        xs = shared.tile([P, T], U8, name="xs", offset=table - 32)
+        picked_bytes = shared.tile([P, S], U8, name="picked_bytes", offset=3 * table + T - 96)
+        bet_at = (0, table + T - 64, 2 * table + T - 64, 3 * table + T + S - 128)
+        bet_t = [shared.tile([P, SCALAR_W], F32, name=f"bet{t}", offset=bet_at[t]) for t in range(PACK)]
         xw = keep.tile([P, T], U32, name="xw")
         w_raw = keep.tile([P, PACK, N], F32, name="w_raw")
         gam_rows = gam.rearrange("(p t) r -> p t r", t=PACK)
@@ -64,34 +60,34 @@ def tile_picked_yspade_none_po_kernel(
         nc.vector.memset(warm[:, 0:1], 1.0)
         nc.scalar.activation(warm[:, 1:2], warm[:, 0:1], ACT.Abs_reciprocal_sqrt)
 
-        nc.sync.dma_start(gam_early[:, :R], gam_rows[:, EARLY, :])
+        nc.sync.dma_start(gam_t[0][:, :R], gam_rows[:, 0, :])
         nc.sync.dma_start(lab_t[:], lab)
         nc.sync.dma_start(w_raw[:, :2, :], w_rows[:, :2, :])
         nc.sync.dma_start(xs[0:P:8, :].bitcast(I32), x_scales[0].bitcast(I32))
         nc.sync.dma_start(offs_t[:], offs)
+        nc.sync.dma_start(gam_t[1][:, :R], gam_rows[:, 1, :])
         nc.sync.dma_start(w_raw[:, 2:, :], w_rows[:, 2:, :])
-        nc.sync.dma_start(bet_early[:, :R], bet_rows[:, EARLY, :])
+        nc.sync.dma_start(gam_t[2][:, :R], gam_rows[:, 2, :])
+        nc.sync.dma_start(gam_t[3][:, :R], gam_rows[:, 3, :])
         nc.sync.dma_start(xw[:].bitcast(I32), x_words[0].rearrange("p n t -> p (n t)").bitcast(I32))
-        nc.sync.dma_start(gam_folded, gam_rows[:, FOLDED, :])
-
-        def picks(cols):
-            return lab_t[:, cols.start // 16 : cols.stop // 16]
 
         halves = runs((HALF, HALF))
-        g_early = keep.tile([P, S], F32, name="g_early")
-        nc.vector.tensor_copy(g_early[:], gam_early[:].indirect(lab_t[:]))
         nc.vector.tensor_copy(picked_bytes[:], xs[:].indirect(offs_t[:]))
         for q in range(4):
             nc.sync.dma_start(x_bytes[q:P:32, :].bitcast(I32), picked_bytes[8 * q : P : 32, :].bitcast(I32))
-        for t in RAW:
-            nc.sync.dma_start(gam_raw[t][:, :R], gam_rows[:, t, :])
-        nc.sync.dma_start(bet_late[:], bet_rows[:, EARLY + 1 :, :])
-        res = keep.tile([P, PACK, S], F32, name="res")
-        b_early = res[:, RAW[1], :]
-        nc.vector.tensor_copy(b_early[:, halves[0]], bet_early[:, :S].indirect(picks(halves[0])))
+        for t in range(PACK):
+            nc.sync.dma_start(bet_t[t][:, :R], bet_rows[:, t, :])
+
+        gains = [keep.tile([P, S], F32, name=f"gains{t}") for t in range(PACK)]
+        shifts = [keep.tile([P, S], F32, name=f"shifts{t}") for t in range(PACK)]
+        for t in range(3):
+            nc.scalar.activation(gains[t][:], gam_t[t][:].indirect(lab_t[:]), ACT.Copy)
+        for t in range(PACK):
+            nc.scalar.activation(shifts[t][:], bet_t[t][:].indirect(lab_t[:]), ACT.Copy)
 
         w_bf = keep.tile([P, PACK, P, PACK], BF16, name="w_bf", align_bytes=64)
-        nc.scalar.copy(w_bf[:].rearrange("p t m j -> p m j t"), w_raw[:].rearrange("p j (m t) -> p m j t", t=PACK))
+        nc.vector.tensor_copy(w_bf[:].rearrange("p t m j -> p m j t"), w_raw[:].rearrange("p j (m t) -> p m j t", t=PACK))
+        nc.vector.tensor_copy(gains[3][:], gam_t[3][:].indirect(lab_t[:]))
         w_codes = keep.tile([P, N], U32, name="w_codes", align_bytes=64)
         w_scales = keep.tile([P, N], U8, name="w_scales", align_bytes=64)
         nc.vector.quantize_mx(
@@ -100,158 +96,76 @@ def tile_picked_yspade_none_po_kernel(
         x_codes = keep.tile([P, S], U32, name="x_codes", align_bytes=64)
         for cols in halves:
             nc.vector.tensor_copy(x_codes[:, cols], xw[:].indirect(offs_t[:, cols.start // 16 : cols.stop // 16]))
-        nc.vector.tensor_copy(b_early[:, halves[1]], bet_early[:].indirect(picks(halves[1])))
-
-        def product(out, t, cols, start, stop):
-            nc.tensor.matmul_mx(
-                out=out,
-                lhsT=w_codes[:, t * P : (t + 1) * P].bitcast(FP8X4),
-                lhsT_scale=w_scales[:, t * P : (t + 1) * P],
-                rhs=x_codes[:, cols].bitcast(FP8X4),
-                rhs_scale=x_bytes[:, cols],
-                start=start,
-                stop=stop,
-            )
 
         y = psum.tile([P, PACK, S], F32, name="y")
-        for pair in ((RAW[0], FOLDED), (RAW[1], EARLY)):
-            for cols in halves:
-                for t in pair:
-                    product(y[:, t, cols], t, cols, True, True)
+        bank_stats = keep.tile([P, PACK, 2, 6], F32, name="bank_stats")
+        moments = keep.tile([P, PACK, 2], F32, name="moments")
+        banks = [(t, h) for pair in ((0, 1), (2, 3)) for h in range(2) for t in pair]
+        for t, h in banks:
+            nc.tensor.matmul_mx(
+                out=y[:, t, halves[h]],
+                lhsT=w_codes[:, t * P : (t + 1) * P].bitcast(FP8X4),
+                lhsT_scale=w_scales[:, t * P : (t + 1) * P],
+                rhs=x_codes[:, halves[h]].bitcast(FP8X4),
+                rhs_scale=x_bytes[:, halves[h]],
+                start=True,
+                stop=True,
+            )
+        for t, h in banks:
+            nc.vector.bn_stats(bank_stats[:, t, h, :], y[:, t, halves[h]])
+        for t in range(PACK):
+            nc.vector.bn_aggr(moments[:, t, :], bank_stats[:, t, :, :].rearrange("p h s -> p (h s)"))
+        rstd = keep.tile([P, PACK], F32, name="rstd")
+        nc.scalar.activation(rstd[:], moments[:, :, 1], ACT.Abs_reciprocal_sqrt, bias=EPS)
 
-        def col(name):
-            return keep.tile([P, 1], F32, name=name)
-
-        gained_early = res[:, RAW[0], :]
-        gained_folded = [keep.tile([P, HALF], F32, name=f"gained_folded{h}", tag=f"after_folded{h}") for h in range(2)]
-        out_codes = keep.tile([P, S], U32, name="out_codes", align_bytes=64)
-        out_scales = keep.tile([P, S], U8, name="out_scales", align_bytes=64)
+        gained = keep.tile([P, PACK, S], F32, name="gained")
+        res = keep.tile([P, PACK, S], F32, name="res")
         out_rows = out_0.rearrange("(p t) j -> p t j", t=PACK)
         word_rows = out_1[0].rearrange("p n t -> p (n t)").bitcast(I32)
 
-        y_sb = {t: keep.tile([P, S], F32, name=f"y_sb{t}")[:] for t in (FOLDED,) + RAW}
-        sums = [keep.tile([P, 2], F32, name=f"sums{t}") for t in range(PACK)]
+        def gain(t, cols):
+            nc.vector.scalar_tensor_tensor(
+                gained[:, t, cols], y[:, t, cols], moments[:, t, 0:1], gains[t][:, cols], ALU.subtract, ALU.mult
+            )
 
-        def copy_out(t, h):
-            nc.scalar.activation(y_sb[t][:, halves[h]], y[:, t, halves[h]], ACT.Copy, accum_out=sums[t][:, h : h + 1])
+        def shift(t, cols):
+            nc.vector.scalar_tensor_tensor(
+                res[:, t, cols], gained[:, t, cols], rstd[:, t : t + 1], shifts[t][:, cols], ALU.mult, ALU.add
+            )
 
-        def minus_mean(t):
-            shares = keep.tile([P, 2], F32, name=f"shares{t}")
-            total = col(f"neg_mean{t}")
-            nc.scalar.activation(shares[:], sums[t][:], ACT.Copy, scale=-1.0 / S, accum_out=total[:])
-            return total
-
-        def square_sum(t, unused_squares, total):
-            nc.scalar.activation(unused_squares, y_sb[t], ACT.Square, bias=neg_mean[t][:], accum_out=total)
-
-        def inverse_std(rstd, squares, bias=EPS):
-            nc.scalar.activation(rstd, squares, ACT.Abs_reciprocal_sqrt, scale=1.0 / S, bias=bias)
-
-        for h in range(2):
-            copy_out(RAW[0], h)
-            copy_out(FOLDED, h)
-        neg_mean = {FOLDED: minus_mean(FOLDED)}
-        squares_folded = col("squares_folded")
-        square_sum(FOLDED, keep.tile([P, S], BF16, name="unused_squares")[:], squares_folded[:])
-        rstd_folded = keep.tile([P, 1], F32, name="rstd_folded", tag="after_gains")
-        inverse_std(rstd_folded[:], squares_folded[:])
-        gains = keep.tile([P, TABLE_W], F32, name="gains")
-        nc.scalar.activation(gains[:, :R], gam_folded, ACT.Copy, scale=rstd_folded[:])
-        for h in range(2):
-            copy_out(RAW[1], h)
-
-        raw_gained = keep.tile([P, 2, S], F32, name="raw_gained")
-        for i, t in enumerate(RAW):
+        for t in (0, 1):
             for cols in halves:
-                nc.vector.tensor_tensor(
-                    raw_gained[:, i, cols], gam_raw[t][:].indirect(picks(cols)), y_sb[t][:, cols], ALU.mult
-                )
+                gain(t, cols)
+        for t in (0, 1):
+            shift(t, slice(0, S))
+            nc.sync.dma_start(out_rows[:, t, :], res[:, t, :])
 
-        shifts = {FOLDED: keep.tile([P, TABLE_W], F32, name="shifts_folded", tag="after_shifts")}
-        nc.vector.scalar_tensor_tensor(
-            shifts[FOLDED][:, :R], gains[:, :R], neg_mean[FOLDED][:], bet_late[:, FOLDED - 1, :], ALU.mult, ALU.add
-        )
-        for h, cols in enumerate(halves):
-            nc.vector.tensor_tensor(
-                gained_folded[h][:], gains[:].indirect(picks(cols)), y_sb[FOLDED][:, cols], ALU.mult
-            )
-        for h, cols in enumerate(halves):
-            nc.vector.tensor_tensor(
-                res[:, FOLDED, cols], shifts[FOLDED][:].indirect(picks(cols)), gained_folded[h][:], ALU.add
-            )
-        nc.sync.dma_start(out_rows[:, FOLDED, :], res[:, FOLDED, :])
-
-        late = keep.tile([P, PACK, S], F32, name="late", tag="after_gains")
-
-        squares_raw = keep.tile([P, 2], F32, name="squares_raw")
-        factors = keep.tile([P, 2], F32, name="factors", tag="after_centring")
-        rstd_raw = keep.tile([P, 2], F32, name="rstd_raw")
-        for i, t in enumerate(RAW):
-            neg_mean[t] = minus_mean(t)
-            square_sum(t, late[:, t, :], squares_raw[:, i : i + 1])
-        inverse_std(rstd_raw[:], squares_raw[:])
-        centring = {}
-        for i, t in enumerate(RAW):
-            factor = factors[:, i : i + 1]
-            nc.scalar.activation(factor, neg_mean[t][:], ACT.Copy, scale=rstd_raw[:, i : i + 1])
-            centring[t] = keep.tile([P, R], F32, name=f"centring{t}")
-            nc.scalar.activation(centring[t][:], gam_raw[t][:, :R], ACT.Copy, scale=factor)
-        for t, tag in zip(RAW, ("after_folded0", "after_shifts")):
-            shifts[t] = keep.tile([P, TABLE_W], F32, name=f"shifts{t}", tag=tag)
-            nc.gpsimd.tensor_tensor(shifts[t][:, :R], centring[t][:], bet_late[:, t - 1, :], ALU.add)
-
-        partial_sums = y[:, RAW[0], :P]
-        blocks = runs((P,) * (S // P))
-        for cols in blocks:
-            product(partial_sums, EARLY, cols, cols == blocks[0], cols == blocks[-1])
-        neg_mean[EARLY] = col("neg_mean_early")
-        nc.scalar.activation(late[:, FOLDED, :P], partial_sums, ACT.Copy, scale=-1.0 / S, accum_out=neg_mean[EARLY][:])
-        for h, cols in enumerate(halves):
-            nc.scalar.activation(
-                late[:, EARLY, cols],
-                y[:, EARLY, cols],
-                ACT.Square,
-                bias=neg_mean[EARLY][:],
-                accum_out=sums[EARLY][:, h : h + 1],
-            )
-        first_half = col("first_half")
-        nc.scalar.activation(first_half[:], sums[EARLY][:, 0:1], ACT.Identity, scale=1.0 / S, bias=EPS)
-        rstd_early = col("rstd_early")
-        inverse_std(rstd_early[:], sums[EARLY][:, 1:2], bias=first_half[:])
-
-        for cols in halves:
-            nc.vector.scalar_tensor_tensor(
-                gained_early[:, cols], y[:, EARLY, cols], neg_mean[EARLY][:], g_early[:, cols], ALU.add, ALU.mult
-            )
-        for cols in halves:
-            nc.vector.scalar_tensor_tensor(
-                res[:, EARLY, cols], gained_early[:, cols], rstd_early[:], b_early[:, cols], ALU.mult, ALU.add
-            )
-        nc.sync.dma_start(out_rows[:, EARLY, :], res[:, EARLY, :])
-
-        rescaled = keep.tile([P, 2, S], F32, name="rescaled", tag="after_centring")
-        for cols in halves:
-            for i in range(2):
-                nc.scalar.activation(rescaled[:, i, cols], raw_gained[:, i, cols], ACT.Copy, scale=rstd_raw[:, i : i + 1])
-
+        out_codes = keep.tile([P, S], U32, name="out_codes", align_bytes=64)
+        out_scales = keep.tile([P, S], U8, name="out_scales", align_bytes=64)
         res_bf = keep.tile([P, S, PACK], BF16, name="res_bf", align_bytes=64)
-        for cols in runs(CHUNKS):
-            for i, t in enumerate(RAW):
-                nc.vector.tensor_tensor(res[:, t, cols], shifts[t][:].indirect(picks(cols)), rescaled[:, i, cols], ALU.add)
-            nc.scalar.copy(
-                res_bf[:, cols, :].rearrange("p (c i) t -> p c t i", i=4),
-                res[:, :, cols].rearrange("p t (c i) -> p c t i", i=4),
-            )
-        for cols in runs(STORED):
-            nc.sync.dma_start(out_rows[:, RAW[0] :, cols], res[:, RAW[0] :, cols])
-        for cols in runs(QUANTISED):
+
+        def quantise(cols):
             nc.vector.quantize_mx(
                 out=out_codes[:, cols].bitcast(FP8X4),
                 scales=out_scales[:, cols],
                 in_=res_bf[:, cols, :].rearrange("p n t -> p (n t)"),
             )
+
+        chunks = runs(CHUNKS)
+        for c, cols in enumerate(chunks):
+            for t in (2, 3):
+                gain(t, cols)
+            for t in (2, 3):
+                shift(t, cols)
+            nc.scalar.copy(
+                res_bf[:, cols, :].rearrange("p (c i) t -> p c t i", i=4),
+                res[:, :, cols].rearrange("p t (c i) -> p c t i", i=4),
+            )
+            nc.sync.dma_start(out_rows[:, 2:, cols], res[:, 2:, cols])
+            if c > 0:
+                quantise(chunks[c - 1])
+        quantise(chunks[-1])
         for cols in runs(WORDS_STORED):
             nc.sync.dma_start(word_rows[:, cols], out_codes[:, cols].bitcast(I32))
-
         for q in range(4):
             nc.scalar.dma_start(out_2[0, q:16:4, :].bitcast(I32), out_scales[q:P:32, :].bitcast(I32))

@@ -21,6 +21,7 @@ FLOPS = 2 * K * N * S
 
 SCALAR_W = 1040
 VECTOR_W = 1376
+SHARED = 384
 CHUNKS = (256, 256, 256, 128, 128)
 WORDS_STORED = (512, 256, 256)
 
@@ -45,7 +46,8 @@ def tile_picked_yspade_none_po_kernel(
         xs = shared.tile([P, T], U8, name="xs", offset=table - 32)
         picked_bytes = shared.tile([P, S], U8, name="picked_bytes", offset=3 * table + T - 96)
         bet_at = (0, table + T - 64, 2 * table + T - 64, 3 * table + T + S - 128)
-        bet_t = [shared.tile([P, SCALAR_W], F32, name=f"bet{t}", offset=bet_at[t]) for t in range(PACK)]
+        bet_t = [keep.tile([P, SCALAR_W], F32, name="bet0")]
+        bet_t += [shared.tile([P, SCALAR_W], F32, name=f"bet{t}", offset=bet_at[t - 1]) for t in range(1, PACK)]
         xw = keep.tile([P, T], U32, name="xw")
         w_raw = keep.tile([P, PACK, N], F32, name="w_raw")
         gam_rows = gam.rearrange("(p t) r -> p t r", t=PACK)
@@ -59,35 +61,44 @@ def tile_picked_yspade_none_po_kernel(
         warm = keep.tile([P, 2], F32, name="warm")
         nc.vector.memset(warm[:, 0:1], 1.0)
         nc.scalar.activation(warm[:, 1:2], warm[:, 0:1], ACT.Abs_reciprocal_sqrt)
+        eps = keep.tile([P, 1], F32, name="eps", tag="after_rstd")
+        nc.vector.tensor_scalar(eps[:], warm[:, 0:1], EPS, None, ALU.mult)
 
-        nc.sync.dma_start(gam_t[0][:, :R], gam_rows[:, 0, :])
+        nc.sync.dma_start(gam_t[3][:, :R], gam_rows[:, 3, :])
         nc.sync.dma_start(lab_t[:], lab)
+        nc.sync.dma_start(gam_t[0][:, :R], gam_rows[:, 0, :])
         nc.sync.dma_start(w_raw[:, :2, :], w_rows[:, :2, :])
         nc.sync.dma_start(xs[0:P:8, :].bitcast(I32), x_scales[0].bitcast(I32))
         nc.sync.dma_start(offs_t[:], offs)
         nc.sync.dma_start(gam_t[1][:, :R], gam_rows[:, 1, :])
         nc.sync.dma_start(w_raw[:, 2:, :], w_rows[:, 2:, :])
         nc.sync.dma_start(gam_t[2][:, :R], gam_rows[:, 2, :])
-        nc.sync.dma_start(gam_t[3][:, :R], gam_rows[:, 3, :])
+        nc.sync.dma_start(bet_t[0][:, :R], bet_rows[:, 0, :])
         nc.sync.dma_start(xw[:].bitcast(I32), x_words[0].rearrange("p n t -> p (n t)").bitcast(I32))
 
+        def picks(cols):
+            return lab_t[:, cols.start // 16 : cols.stop // 16]
+
         halves = runs((HALF, HALF))
+        gains = [keep.tile([P, S], F32, name=f"gains{t}") for t in range(PACK)]
+        nc.vector.tensor_copy(gains[3][:], gam_t[3][:].indirect(lab_t[:]))
         nc.vector.tensor_copy(picked_bytes[:], xs[:].indirect(offs_t[:]))
         for q in range(4):
             nc.sync.dma_start(x_bytes[q:P:32, :].bitcast(I32), picked_bytes[8 * q : P : 32, :].bitcast(I32))
-        for t in range(PACK):
+        for t in range(1, PACK):
             nc.sync.dma_start(bet_t[t][:, :R], bet_rows[:, t, :])
 
-        gains = [keep.tile([P, S], F32, name=f"gains{t}") for t in range(PACK)]
-        shifts = [keep.tile([P, S], F32, name=f"shifts{t}") for t in range(PACK)]
-        for t in range(3):
+        shifts = [keep.tile([P, S], F32, name=f"shifts{t}") for t in range(3)]
+        on_scalar, on_vector = runs((S - SHARED, SHARED))
+        for t in range(2):
             nc.scalar.activation(gains[t][:], gam_t[t][:].indirect(lab_t[:]), ACT.Copy)
-        for t in range(PACK):
+        nc.scalar.activation(gains[2][:, on_scalar], gam_t[2][:].indirect(picks(on_scalar)), ACT.Copy)
+        for t in range(3):
             nc.scalar.activation(shifts[t][:], bet_t[t][:].indirect(lab_t[:]), ACT.Copy)
 
         w_bf = keep.tile([P, PACK, P, PACK], BF16, name="w_bf", align_bytes=64)
         nc.vector.tensor_copy(w_bf[:].rearrange("p t m j -> p m j t"), w_raw[:].rearrange("p j (m t) -> p m j t", t=PACK))
-        nc.vector.tensor_copy(gains[3][:], gam_t[3][:].indirect(lab_t[:]))
+        nc.vector.tensor_copy(gains[2][:, on_vector], gam_t[2][:].indirect(picks(on_vector)))
         w_codes = keep.tile([P, N], U32, name="w_codes", align_bytes=64)
         w_scales = keep.tile([P, N], U8, name="w_scales", align_bytes=64)
         nc.vector.quantize_mx(
@@ -98,25 +109,46 @@ def tile_picked_yspade_none_po_kernel(
             nc.vector.tensor_copy(x_codes[:, cols], xw[:].indirect(offs_t[:, cols.start // 16 : cols.stop // 16]))
 
         y = psum.tile([P, PACK, S], F32, name="y")
-        bank_stats = keep.tile([P, PACK, 2, 6], F32, name="bank_stats")
+        bank_stats = keep.tile([P, 3, 2, 6], F32, name="bank_stats")
         moments = keep.tile([P, PACK, 2], F32, name="moments")
-        banks = [(t, h) for pair in ((0, 1), (2, 3)) for h in range(2) for t in pair]
-        for t, h in banks:
+
+        def product(out, t, cols, start=True, stop=True):
             nc.tensor.matmul_mx(
-                out=y[:, t, halves[h]],
+                out=out,
                 lhsT=w_codes[:, t * P : (t + 1) * P].bitcast(FP8X4),
                 lhsT_scale=w_scales[:, t * P : (t + 1) * P],
-                rhs=x_codes[:, halves[h]].bitcast(FP8X4),
-                rhs_scale=x_bytes[:, halves[h]],
-                start=True,
-                stop=True,
+                rhs=x_codes[:, cols].bitcast(FP8X4),
+                rhs_scale=x_bytes[:, cols],
+                start=start,
+                stop=stop,
             )
+
+        banks = [(0, 0), (1, 0), (0, 1), (1, 1), (2, 0), (2, 1)]
+        for t, h in banks + [(3, 0)]:
+            product(y[:, t, halves[h]], t, halves[h])
         for t, h in banks:
             nc.vector.bn_stats(bank_stats[:, t, h, :], y[:, t, halves[h]])
-        for t in range(PACK):
+        for t in range(3):
             nc.vector.bn_aggr(moments[:, t, :], bank_stats[:, t, :, :].rearrange("p h s -> p (h s)"))
+
+        partial_sums = y[:, 3, HALF : HALF + P]
+        blocks = runs((P,) * (S // P))
+        for cols in blocks:
+            product(partial_sums, 3, cols, cols == blocks[0], cols == blocks[-1])
+        unused = keep.tile([P, S], BF16, name="unused")
+        nc.scalar.activation(unused[:, :P], partial_sums, ACT.Copy, scale=1.0 / S, accum_out=moments[:, 3, 0:1])
+        product(y[:, 3, halves[1]], 3, halves[1])
+        squares = keep.tile([P, 2], F32, name="squares")
+        for h, cols in enumerate(halves):
+            nc.scalar.activation(
+                unused[:, cols], y[:, 3, cols], ACT.Square, scale=-1.0, bias=moments[:, 3, 0:1], accum_out=squares[:, h : h + 1]
+            )
+        shares = keep.tile([P, 2], F32, name="shares")
+        nc.scalar.activation(shares[:], squares[:], ACT.Copy, scale=1.0 / S, accum_out=moments[:, 3, 1:2])
         rstd = keep.tile([P, PACK], F32, name="rstd")
-        nc.scalar.activation(rstd[:], moments[:, :, 1], ACT.Abs_reciprocal_sqrt, bias=EPS)
+        nc.scalar.activation(rstd[:], moments[:, :, 1], ACT.Abs_reciprocal_sqrt, bias=eps[:])
+        shifts.append(keep.tile([P, S], F32, name="shifts3", tag="after_rstd"))
+        nc.scalar.activation(shifts[3][:], bet_t[3][:].indirect(lab_t[:]), ACT.Copy)
 
         gained = keep.tile([P, PACK, S], F32, name="gained")
         res = keep.tile([P, PACK, S], F32, name="res")

@@ -21,8 +21,10 @@ FLOPS = 2 * K * N * S
 
 SCALAR_W = 1040
 VECTOR_W = 1376
-SHARED = 384
-CHUNKS = (256, 256, 256, 128, 128)
+SHARED = 512
+BEFORE_CHAIN = 768
+ON_SCALAR = 3
+CHUNKS = (256, 256, 256, 256)
 WORDS_STORED = (512, 256, 256)
 
 
@@ -61,8 +63,9 @@ def tile_picked_yspade_none_po_kernel(
         warm = keep.tile([P, 2], F32, name="warm")
         nc.vector.memset(warm[:, 0:1], 1.0)
         nc.scalar.activation(warm[:, 1:2], warm[:, 0:1], ACT.Abs_reciprocal_sqrt)
-        eps = keep.tile([P, 1], F32, name="eps", tag="after_rstd")
-        nc.vector.tensor_scalar(eps[:], warm[:, 0:1], EPS, None, ALU.mult)
+        eps = [keep.tile([P, 1], F32, name=f"eps{i}", tag=f"after_rstd{i}") for i in range(2)]
+        for column in eps:
+            nc.vector.tensor_scalar(column[:], warm[:, 0:1], EPS, None, ALU.mult)
 
         nc.sync.dma_start(gam_t[3][:, :R], gam_rows[:, 3, :])
         nc.sync.dma_start(lab_t[:], lab)
@@ -93,8 +96,9 @@ def tile_picked_yspade_none_po_kernel(
         for t in range(2):
             nc.scalar.activation(gains[t][:], gam_t[t][:].indirect(lab_t[:]), ACT.Copy)
         nc.scalar.activation(gains[2][:, on_scalar], gam_t[2][:].indirect(picks(on_scalar)), ACT.Copy)
-        for t in range(3):
+        for t in range(2):
             nc.scalar.activation(shifts[t][:], bet_t[t][:].indirect(lab_t[:]), ACT.Copy)
+        nc.scalar.activation(shifts[2][:, :BEFORE_CHAIN], bet_t[2][:].indirect(picks(slice(0, BEFORE_CHAIN))), ACT.Copy)
 
         w_bf = keep.tile([P, PACK, P, PACK], BF16, name="w_bf", align_bytes=64)
         nc.vector.tensor_copy(w_bf[:].rearrange("p t m j -> p m j t"), w_raw[:].rearrange("p j (m t) -> p m j t", t=PACK))
@@ -109,7 +113,6 @@ def tile_picked_yspade_none_po_kernel(
             nc.vector.tensor_copy(x_codes[:, cols], xw[:].indirect(offs_t[:, cols.start // 16 : cols.stop // 16]))
 
         y = psum.tile([P, PACK, S], F32, name="y")
-        bank_stats = keep.tile([P, 3, 2, 6], F32, name="bank_stats")
         moments = keep.tile([P, PACK, 2], F32, name="moments")
 
         def product(out, t, cols, start=True, stop=True):
@@ -123,54 +126,98 @@ def tile_picked_yspade_none_po_kernel(
                 stop=stop,
             )
 
-        banks = [(0, 0), (1, 0), (0, 1), (1, 1), (2, 0), (2, 1)]
-        for t, h in banks + [(3, 0)]:
-            product(y[:, t, halves[h]], t, halves[h])
-        for t, h in banks:
-            nc.vector.bn_stats(bank_stats[:, t, h, :], y[:, t, halves[h]])
-        for t in range(3):
-            nc.vector.bn_aggr(moments[:, t, :], bank_stats[:, t, :, :].rearrange("p h s -> p (h s)"))
-
-        partial_sums = y[:, 3, HALF : HALF + P]
+        partial_sums = y[:, 2, HALF : HALF + P]
         blocks = runs((P,) * (S // P))
-        for cols in blocks:
-            product(partial_sums, 3, cols, cols == blocks[0], cols == blocks[-1])
-        unused = keep.tile([P, S], BF16, name="unused")
-        nc.scalar.activation(unused[:, :P], partial_sums, ACT.Copy, scale=1.0 / S, accum_out=moments[:, 3, 0:1])
-        product(y[:, 3, halves[1]], 3, halves[1])
-        squares = keep.tile([P, 2], F32, name="squares")
+
+        def bank(t, h):
+            product(y[:, t, halves[h]], t, halves[h])
+
+        def statistics(tiles):
+            bank_stats = keep.tile([P, 2, 2, 6], F32, name="bank_stats")
+            for h in range(2):
+                for i, t in enumerate(tiles):
+                    nc.vector.bn_stats(bank_stats[:, i, h, :], y[:, t, halves[h]])
+            for i, t in enumerate(tiles):
+                nc.vector.bn_aggr(moments[:, t, :], bank_stats[:, i, :, :].rearrange("p h s -> p (h s)"))
+
+        for h in range(2):
+            bank(0, h)
+            bank(1, h)
+            for cols in blocks[4 * h : 4 * h + 4]:
+                product(partial_sums, 2, cols, cols == blocks[0], cols == blocks[-1])
+        for t, h in ((2, 0), (3, 0), (3, 1)):
+            bank(t, h)
+        statistics((0, 1))
+        rstd = keep.tile([P, PACK], F32, name="rstd")
+        nc.scalar.activation(rstd[:, :2], moments[:, :2, 1], ACT.Abs_reciprocal_sqrt, bias=eps[0][:])
+
+        unused = keep.tile([P, S], BF16, name="unused", tag="after_rstd0")
+        nc.scalar.activation(unused[:, :P], partial_sums, ACT.Copy, scale=1.0 / S, accum_out=moments[:, 2, 0:1])
+        bank(2, 1)
+        squares = keep.tile([P, 2], F32, name="squares", tag="after_squares")
         for h, cols in enumerate(halves):
             nc.scalar.activation(
-                unused[:, cols], y[:, 3, cols], ACT.Square, scale=-1.0, bias=moments[:, 3, 0:1], accum_out=squares[:, h : h + 1]
+                unused[:, cols], y[:, 2, cols], ACT.Square, scale=-1.0, bias=moments[:, 2, 0:1], accum_out=squares[:, h : h + 1]
             )
         shares = keep.tile([P, 2], F32, name="shares")
-        nc.scalar.activation(shares[:], squares[:], ACT.Copy, scale=1.0 / S, accum_out=moments[:, 3, 1:2])
-        rstd = keep.tile([P, PACK], F32, name="rstd")
-        nc.scalar.activation(rstd[:], moments[:, :, 1], ACT.Abs_reciprocal_sqrt, bias=eps[:])
-        shifts.append(keep.tile([P, S], F32, name="shifts3", tag="after_rstd"))
-        nc.scalar.activation(shifts[3][:], bet_t[3][:].indirect(lab_t[:]), ACT.Copy)
+        nc.scalar.activation(shares[:], squares[:], ACT.Copy, scale=1.0 / S, accum_out=moments[:, 2, 1:2])
+        middle = keep.tile([P, S - BEFORE_CHAIN + HALF], F32, name="middle", tag="after_squares")
+        nc.scalar.activation(middle[:, :HALF], bet_t[3][:].indirect(picks(halves[0])), ACT.Copy)
+        nc.scalar.activation(middle[:, HALF:], bet_t[2][:].indirect(picks(slice(BEFORE_CHAIN, S))), ACT.Copy)
 
-        gained = keep.tile([P, PACK, S], F32, name="gained")
-        res = keep.tile([P, PACK, S], F32, name="res")
+        res_halves = [keep.tile([P, PACK, HALF], F32, name=f"res{h}") for h in range(2)]
+
+        def res(tiles, cols):
+            h = cols.start // HALF
+            return res_halves[h][:, tiles, cols.start - h * HALF : cols.stop - h * HALF]
+
+        gained = [keep.tile([P, S], F32, name=f"gained{t}") for t in range(PACK)]
         out_rows = out_0.rearrange("(p t) j -> p t j", t=PACK)
         word_rows = out_1[0].rearrange("p n t -> p (n t)").bitcast(I32)
 
         def gain(t, cols):
             nc.vector.scalar_tensor_tensor(
-                gained[:, t, cols], y[:, t, cols], moments[:, t, 0:1], gains[t][:, cols], ALU.subtract, ALU.mult
+                gained[t][:, cols], y[:, t, cols], moments[:, t, 0:1], gains[t][:, cols], ALU.subtract, ALU.mult
             )
+
+        def looked_up(t, cols):
+            if t == 3:
+                return middle[:, cols] if cols.stop <= HALF else last[:, cols.start - HALF : cols.stop - HALF]
+            if t == 2 and cols.start >= BEFORE_CHAIN:
+                return middle[:, HALF + cols.start - BEFORE_CHAIN : HALF + cols.stop - BEFORE_CHAIN]
+            return shifts[t][:, cols]
 
         def shift(t, cols):
             nc.vector.scalar_tensor_tensor(
-                res[:, t, cols], gained[:, t, cols], rstd[:, t : t + 1], shifts[t][:, cols], ALU.mult, ALU.add
+                res(t, cols), gained[t][:, cols], rstd[:, t : t + 1], looked_up(t, cols), ALU.mult, ALU.add
             )
 
-        for t in (0, 1):
+        on_gpsimd = ((0, halves[0]), (0, halves[1]), (1, halves[1]))
+        for t, cols in on_gpsimd + ((1, halves[0]),):
+            gain(t, cols)
+        scaled = keep.tile([P, 2, S], F32, name="scaled")
+
+        def scale(t, cols):
+            nc.gpsimd.tensor_scalar(scaled[:, t, cols], gained[t][:, cols], rstd[:, t : t + 1], 0.0, ALU.mult, ALU.add)
+
+        def add(t, cols):
+            nc.gpsimd.tensor_tensor(res(t, cols), scaled[:, t, cols], shifts[t][:, cols], ALU.add)
+            if t == 0:
+                nc.sync.dma_start(out_rows[:, t, cols], res(t, cols))
+
+        scale(*on_gpsimd[0])
+        for this, following in zip(on_gpsimd, on_gpsimd[1:]):
+            scale(*following)
+            add(*this)
+        add(*on_gpsimd[-1])
+
+        statistics((3,))
+        nc.scalar.activation(rstd[:, 2:], moments[:, 2:, 1], ACT.Abs_reciprocal_sqrt, bias=eps[1][:])
+        last = keep.tile([P, HALF], F32, name="last", tag="after_rstd1")
+        nc.scalar.activation(last[:], bet_t[3][:].indirect(picks(halves[1])), ACT.Copy)
+        for t in (2, 3):
             for cols in halves:
                 gain(t, cols)
-        for t in (0, 1):
-            shift(t, slice(0, S))
-            nc.sync.dma_start(out_rows[:, t, :], res[:, t, :])
 
         out_codes = keep.tile([P, S], U32, name="out_codes", align_bytes=64)
         out_scales = keep.tile([P, S], U8, name="out_scales", align_bytes=64)
@@ -185,15 +232,15 @@ def tile_picked_yspade_none_po_kernel(
 
         chunks = runs(CHUNKS)
         for c, cols in enumerate(chunks):
-            for t in (2, 3):
-                gain(t, cols)
-            for t in (2, 3):
+            first = 1 if cols.stop <= HALF else 2
+            for t in range(first, PACK):
                 shift(t, cols)
-            nc.scalar.copy(
+            copy = nc.scalar.copy if c < ON_SCALAR else nc.vector.tensor_copy
+            copy(
                 res_bf[:, cols, :].rearrange("p (c i) t -> p c t i", i=4),
-                res[:, :, cols].rearrange("p t (c i) -> p c t i", i=4),
+                res(slice(0, PACK), cols).rearrange("p t (c i) -> p c t i", i=4),
             )
-            nc.sync.dma_start(out_rows[:, 2:, cols], res[:, 2:, cols])
+            nc.sync.dma_start(out_rows[:, 1:, cols], res(slice(1, PACK), cols))
             if c > 0:
                 quantise(chunks[c - 1])
         quantise(chunks[-1])

@@ -21,10 +21,9 @@ FLOPS = 2 * K * N * S
 
 SCALAR_W = 1040
 VECTOR_W = 1376
-SHARED = 512
-BEFORE_CHAIN = 768
-ON_SCALAR = 3
-CHUNKS = (256, 256, 256, 256)
+BEFORE_CHAIN = 512
+ON_SCALAR = 4
+CHUNKS = (256, 256, 256, 128, 128)
 WORDS_STORED = (512, 256, 256)
 
 
@@ -92,17 +91,14 @@ def tile_picked_yspade_none_po_kernel(
             nc.sync.dma_start(bet_t[t][:, :R], bet_rows[:, t, :])
 
         shifts = [keep.tile([P, S], F32, name=f"shifts{t}") for t in range(3)]
-        on_scalar, on_vector = runs((S - SHARED, SHARED))
-        for t in range(2):
+        for t in range(3):
             nc.scalar.activation(gains[t][:], gam_t[t][:].indirect(lab_t[:]), ACT.Copy)
-        nc.scalar.activation(gains[2][:, on_scalar], gam_t[2][:].indirect(picks(on_scalar)), ACT.Copy)
         for t in range(2):
             nc.scalar.activation(shifts[t][:], bet_t[t][:].indirect(lab_t[:]), ACT.Copy)
         nc.scalar.activation(shifts[2][:, :BEFORE_CHAIN], bet_t[2][:].indirect(picks(slice(0, BEFORE_CHAIN))), ACT.Copy)
 
         w_bf = keep.tile([P, PACK, P, PACK], BF16, name="w_bf", align_bytes=64)
         nc.vector.tensor_copy(w_bf[:].rearrange("p t m j -> p m j t"), w_raw[:].rearrange("p j (m t) -> p m j t", t=PACK))
-        nc.vector.tensor_copy(gains[2][:, on_vector], gam_t[2][:].indirect(picks(on_vector)))
         w_codes = keep.tile([P, N], U32, name="w_codes", align_bytes=64)
         w_scales = keep.tile([P, N], U8, name="w_scales", align_bytes=64)
         nc.vector.quantize_mx(
@@ -192,8 +188,8 @@ def tile_picked_yspade_none_po_kernel(
                 res(t, cols), gained[t][:, cols], rstd[:, t : t + 1], looked_up(t, cols), ALU.mult, ALU.add
             )
 
-        on_gpsimd = ((0, halves[0]), (0, halves[1]), (1, halves[1]))
-        for t, cols in on_gpsimd + ((1, halves[0]),):
+        on_gpsimd = ((0, halves[0]), (0, halves[1]))
+        for t, cols in on_gpsimd + ((1, halves[0]), (1, halves[1])):
             gain(t, cols)
         scaled = keep.tile([P, 2, S], F32, name="scaled")
 
@@ -232,8 +228,7 @@ def tile_picked_yspade_none_po_kernel(
 
         chunks = runs(CHUNKS)
         for c, cols in enumerate(chunks):
-            first = 1 if cols.stop <= HALF else 2
-            for t in range(first, PACK):
+            for t in range(1, PACK):
                 shift(t, cols)
             copy = nc.scalar.copy if c < ON_SCALAR else nc.vector.tensor_copy
             copy(

@@ -21,7 +21,8 @@ FLOPS = 2 * K * N * S
 
 SCALAR_W = 1040
 VECTOR_W = 1376
-BEFORE_CHAIN = 512
+THIRD_SHIFTS = (512, 256, 256)
+SHARED = 256
 ON_SCALAR = 4
 CHUNKS = (256, 256, 256, 128, 128)
 WORDS_STORED = (512, 256, 256)
@@ -91,14 +92,17 @@ def tile_picked_yspade_none_po_kernel(
             nc.sync.dma_start(bet_t[t][:, :R], bet_rows[:, t, :])
 
         shifts = [keep.tile([P, S], F32, name=f"shifts{t}") for t in range(3)]
-        for t in range(3):
+        on_scalar, on_vector = runs((S - SHARED, SHARED))
+        for t in range(2):
             nc.scalar.activation(gains[t][:], gam_t[t][:].indirect(lab_t[:]), ACT.Copy)
+        nc.scalar.activation(gains[2][:, on_scalar], gam_t[2][:].indirect(picks(on_scalar)), ACT.Copy)
         for t in range(2):
             nc.scalar.activation(shifts[t][:], bet_t[t][:].indirect(lab_t[:]), ACT.Copy)
-        nc.scalar.activation(shifts[2][:, :BEFORE_CHAIN], bet_t[2][:].indirect(picks(slice(0, BEFORE_CHAIN))), ACT.Copy)
+        nc.scalar.activation(shifts[2][:, : THIRD_SHIFTS[0]], bet_t[2][:].indirect(picks(slice(0, THIRD_SHIFTS[0]))), ACT.Copy)
 
         w_bf = keep.tile([P, PACK, P, PACK], BF16, name="w_bf", align_bytes=64)
         nc.vector.tensor_copy(w_bf[:].rearrange("p t m j -> p m j t"), w_raw[:].rearrange("p j (m t) -> p m j t", t=PACK))
+        nc.vector.tensor_copy(gains[2][:, on_vector], gam_t[2][:].indirect(picks(on_vector)))
         w_codes = keep.tile([P, N], U32, name="w_codes", align_bytes=64)
         w_scales = keep.tile([P, N], U8, name="w_scales", align_bytes=64)
         nc.vector.quantize_mx(
@@ -128,26 +132,32 @@ def tile_picked_yspade_none_po_kernel(
         def bank(t, h):
             product(y[:, t, halves[h]], t, halves[h])
 
-        def statistics(tiles):
-            bank_stats = keep.tile([P, 2, 2, 6], F32, name="bank_stats")
-            for h in range(2):
-                for i, t in enumerate(tiles):
-                    nc.vector.bn_stats(bank_stats[:, i, h, :], y[:, t, halves[h]])
-            for i, t in enumerate(tiles):
-                nc.vector.bn_aggr(moments[:, t, :], bank_stats[:, i, :, :].rearrange("p h s -> p (h s)"))
+        bank_stats = keep.tile([P, PACK, 2, 6], F32, name="bank_stats")
 
-        for h in range(2):
-            bank(0, h)
-            bank(1, h)
-            for cols in blocks[4 * h : 4 * h + 4]:
-                product(partial_sums, 2, cols, cols == blocks[0], cols == blocks[-1])
-        for t, h in ((2, 0), (3, 0), (3, 1)):
+        def statistics(t, h):
+            nc.vector.bn_stats(bank_stats[:, t, h, :], y[:, t, halves[h]])
+
+        def aggregate(t):
+            nc.vector.bn_aggr(moments[:, t, :], bank_stats[:, t, :, :].rearrange("p h s -> p (h s)"))
+
+        for t, h in ((0, 0), (1, 0), (0, 1), (1, 1), (3, 0), (3, 1)):
             bank(t, h)
-        statistics((0, 1))
+        for cols in blocks:
+            product(partial_sums, 2, cols, cols == blocks[0], cols == blocks[-1])
+        bank(2, 0)
+        for t, h in ((0, 0), (0, 1), (1, 0)):
+            statistics(t, h)
+        aggregate(0)
+        statistics(1, 1)
+        statistics(3, 0)
+        aggregate(1)
         rstd = keep.tile([P, PACK], F32, name="rstd")
-        nc.scalar.activation(rstd[:, :2], moments[:, :2, 1], ACT.Abs_reciprocal_sqrt, bias=eps[0][:])
+        nc.scalar.activation(rstd[:, :1], moments[:, :1, 1], ACT.Abs_reciprocal_sqrt, bias=eps[0][:])
 
-        unused = keep.tile([P, S], BF16, name="unused", tag="after_rstd0")
+        first, second, third = runs(THIRD_SHIFTS)
+        after_first = keep.tile([P, S + THIRD_SHIFTS[1]], F32, name="after_first", tag="after_rstd0")
+        unused = after_first[:, :S]
+        nc.scalar.activation(after_first[:, S:], bet_t[2][:].indirect(picks(second)), ACT.Copy)
         nc.scalar.activation(unused[:, :P], partial_sums, ACT.Copy, scale=1.0 / S, accum_out=moments[:, 2, 0:1])
         bank(2, 1)
         squares = keep.tile([P, 2], F32, name="squares", tag="after_squares")
@@ -157,9 +167,8 @@ def tile_picked_yspade_none_po_kernel(
             )
         shares = keep.tile([P, 2], F32, name="shares")
         nc.scalar.activation(shares[:], squares[:], ACT.Copy, scale=1.0 / S, accum_out=moments[:, 2, 1:2])
-        middle = keep.tile([P, S - BEFORE_CHAIN + HALF], F32, name="middle", tag="after_squares")
-        nc.scalar.activation(middle[:, :HALF], bet_t[3][:].indirect(picks(halves[0])), ACT.Copy)
-        nc.scalar.activation(middle[:, HALF:], bet_t[2][:].indirect(picks(slice(BEFORE_CHAIN, S))), ACT.Copy)
+        middle = keep.tile([P, HALF], F32, name="middle", tag="after_squares")
+        nc.scalar.activation(middle[:], bet_t[3][:].indirect(picks(halves[0])), ACT.Copy)
 
         res_halves = [keep.tile([P, PACK, HALF], F32, name=f"res{h}") for h in range(2)]
 
@@ -179,8 +188,10 @@ def tile_picked_yspade_none_po_kernel(
         def looked_up(t, cols):
             if t == 3:
                 return middle[:, cols] if cols.stop <= HALF else last[:, cols.start - HALF : cols.stop - HALF]
-            if t == 2 and cols.start >= BEFORE_CHAIN:
-                return middle[:, HALF + cols.start - BEFORE_CHAIN : HALF + cols.stop - BEFORE_CHAIN]
+            if t == 2 and cols.start >= third.start:
+                return last[:, HALF + cols.start - third.start : HALF + cols.stop - third.start]
+            if t == 2 and cols.start >= second.start:
+                return after_first[:, S + cols.start - second.start : S + cols.stop - second.start]
             return shifts[t][:, cols]
 
         def shift(t, cols):
@@ -188,32 +199,26 @@ def tile_picked_yspade_none_po_kernel(
                 res(t, cols), gained[t][:, cols], rstd[:, t : t + 1], looked_up(t, cols), ALU.mult, ALU.add
             )
 
-        on_gpsimd = ((0, halves[0]), (0, halves[1]))
-        for t, cols in on_gpsimd + ((1, halves[0]), (1, halves[1])):
-            gain(t, cols)
-        scaled = keep.tile([P, 2, S], F32, name="scaled")
+        scaled = keep.tile([P, S], F32, name="scaled")
+        for cols in halves:
+            nc.gpsimd.tensor_scalar(scaled[:, cols], gains[0][:, cols], rstd[:, 0:1], 0.0, ALU.mult, ALU.add)
+        for cols in halves:
+            nc.vector.scalar_tensor_tensor(
+                gained[0][:, cols], y[:, 0, cols], moments[:, 0, 0:1], scaled[:, cols], ALU.subtract, ALU.mult
+            )
+        for cols in halves:
+            nc.gpsimd.tensor_tensor(res(0, cols), gained[0][:, cols], shifts[0][:, cols], ALU.add)
+            nc.sync.dma_start(out_rows[:, 0, cols], res(0, cols))
 
-        def scale(t, cols):
-            nc.gpsimd.tensor_scalar(scaled[:, t, cols], gained[t][:, cols], rstd[:, t : t + 1], 0.0, ALU.mult, ALU.add)
-
-        def add(t, cols):
-            nc.gpsimd.tensor_tensor(res(t, cols), scaled[:, t, cols], shifts[t][:, cols], ALU.add)
-            if t == 0:
-                nc.sync.dma_start(out_rows[:, t, cols], res(t, cols))
-
-        scale(*on_gpsimd[0])
-        for this, following in zip(on_gpsimd, on_gpsimd[1:]):
-            scale(*following)
-            add(*this)
-        add(*on_gpsimd[-1])
-
-        statistics((3,))
-        nc.scalar.activation(rstd[:, 2:], moments[:, 2:, 1], ACT.Abs_reciprocal_sqrt, bias=eps[1][:])
-        last = keep.tile([P, HALF], F32, name="last", tag="after_rstd1")
-        nc.scalar.activation(last[:], bet_t[3][:].indirect(picks(halves[1])), ACT.Copy)
-        for t in (2, 3):
-            for cols in halves:
-                gain(t, cols)
+        statistics(3, 1)
+        gain(1, halves[0])
+        aggregate(3)
+        gain(1, halves[1])
+        gain(2, halves[0])
+        nc.scalar.activation(rstd[:, 1:], moments[:, 1:, 1], ACT.Abs_reciprocal_sqrt, bias=eps[1][:])
+        last = keep.tile([P, HALF + THIRD_SHIFTS[2]], F32, name="last", tag="after_rstd1")
+        nc.scalar.activation(last[:, :HALF], bet_t[3][:].indirect(picks(halves[1])), ACT.Copy)
+        nc.scalar.activation(last[:, HALF:], bet_t[2][:].indirect(picks(third)), ACT.Copy)
 
         out_codes = keep.tile([P, S], U32, name="out_codes", align_bytes=64)
         out_scales = keep.tile([P, S], U8, name="out_scales", align_bytes=64)
@@ -228,6 +233,8 @@ def tile_picked_yspade_none_po_kernel(
 
         chunks = runs(CHUNKS)
         for c, cols in enumerate(chunks):
+            for t in range(3 if cols.stop <= HALF else 2, PACK):
+                gain(t, cols)
             for t in range(1, PACK):
                 shift(t, cols)
             copy = nc.scalar.copy if c < ON_SCALAR else nc.vector.tensor_copy

@@ -23,6 +23,7 @@ SCALAR_W = 1040
 VECTOR_W = 1376
 THIRD_SHIFTS = (512, 256, 256)
 SHARED = 256
+STORED = 256
 ON_SCALAR = 4
 CHUNKS = (256, 256, 256, 128, 128)
 WORDS_STORED = (512, 256, 256)
@@ -231,21 +232,42 @@ def tile_picked_yspade_none_po_kernel(
                 in_=res_bf[:, cols, :].rearrange("p n t -> p (n t)"),
             )
 
-        chunks = runs(CHUNKS)
-        for c, cols in enumerate(chunks):
-            for t in range(3 if cols.stop <= HALF else 2, PACK):
-                gain(t, cols)
-            for t in range(1, PACK):
+        def finish_second(half):
+            shift(1, half)
+            nc.sync.dma_start(out_rows[:, 1, half], res(1, half))
+
+        def finish(c):
+            cols = chunks[c]
+            for t in (2, 3):
                 shift(t, cols)
             copy = nc.scalar.copy if c < ON_SCALAR else nc.vector.tensor_copy
             copy(
                 res_bf[:, cols, :].rearrange("p (c i) t -> p c t i", i=4),
                 res(slice(0, PACK), cols).rearrange("p t (c i) -> p c t i", i=4),
             )
-            nc.sync.dma_start(out_rows[:, 1:, cols], res(slice(1, PACK), cols))
-            if c > 0:
-                quantise(chunks[c - 1])
-        quantise(chunks[-1])
+            if cols.stop % STORED == 0:
+                stored = slice(cols.stop - STORED, cols.stop)
+                nc.sync.dma_start(out_rows[:, 2:, stored], res(slice(2, PACK), stored))
+
+        chunks = runs(CHUNKS)
+        quarters = runs((S // 4,) * 4)
+        gain(3, halves[0])
+        finish_second(halves[0])
+        finish(0)
+        gain(2, quarters[2])
+        finish(1)
+        gain(3, quarters[2])
+        finish_second(halves[1])
+        quantise(chunks[0])
+        finish(2)
+        for t in (2, 3):
+            gain(t, quarters[3])
+        quantise(chunks[1])
+        finish(3)
+        quantise(chunks[2])
+        finish(4)
+        for cols in chunks[3:]:
+            quantise(cols)
         for cols in runs(WORDS_STORED):
             nc.sync.dma_start(word_rows[:, cols], out_codes[:, cols].bitcast(I32))
         for q in range(4):

@@ -22,7 +22,7 @@ FLOPS = 2 * K * N * S
 SCALAR_W = 1040
 VECTOR_W = 1376
 THIRD_SHIFTS = (512, 256, 256)
-SHARED = 256
+SHARED = 384
 STORED = 256
 ON_SCALAR = 4
 CHUNKS = (256, 256, 256, 128, 128)
@@ -44,7 +44,8 @@ def tile_picked_yspade_none_po_kernel(
 
         lab_t = keep.tile([P, S // 16], U16, name="lab_t")
         offs_t = keep.tile([P, S // 16], U16, name="offs_t")
-        gam_t = [keep.tile([P, VECTOR_W if t == 3 else SCALAR_W], F32, name=f"gam{t}") for t in range(PACK)]
+        gam_pairs = [keep.tile([P, R + VECTOR_W], F32, name=f"gam_pair{i}") for i in range(2)]
+        gam_last = keep.tile([P, SCALAR_W], F32, name="gam_last")
         table = 4 * SCALAR_W
         xs = shared.tile([P, T], U8, name="xs", offset=table - 32)
         picked_bytes = shared.tile([P, S], U8, name="picked_bytes", offset=3 * table + T - 96)
@@ -53,7 +54,7 @@ def tile_picked_yspade_none_po_kernel(
         bet_t += [shared.tile([P, SCALAR_W], F32, name=f"bet{t}", offset=bet_at[t - 1]) for t in range(1, PACK)]
         xw = keep.tile([P, T], U32, name="xw")
         w_raw = keep.tile([P, PACK, N], F32, name="w_raw")
-        gam_rows = gam.rearrange("(p t) r -> p t r", t=PACK)
+        gam_rows = gam.rearrange("(p i t) r -> p i (t r)", i=2, t=2)
         bet_rows = bet.rearrange("(p t) r -> p t r", t=PACK)
         w_rows = w1.rearrange("(p j) n -> p j n", j=PACK)
 
@@ -68,15 +69,13 @@ def tile_picked_yspade_none_po_kernel(
         for column in eps:
             nc.vector.tensor_scalar(column[:], warm[:, 0:1], EPS, None, ALU.mult)
 
-        nc.sync.dma_start(gam_t[3][:, :R], gam_rows[:, 3, :])
+        nc.sync.dma_start(gam_pairs[0][:, : 2 * R], gam_rows[:, 0, :])
         nc.sync.dma_start(lab_t[:], lab)
-        nc.sync.dma_start(gam_t[0][:, :R], gam_rows[:, 0, :])
         nc.sync.dma_start(w_raw[:, :2, :], w_rows[:, :2, :])
         nc.sync.dma_start(xs[0:P:8, :].bitcast(I32), x_scales[0].bitcast(I32))
         nc.sync.dma_start(offs_t[:], offs)
-        nc.sync.dma_start(gam_t[1][:, :R], gam_rows[:, 1, :])
+        nc.sync.dma_start(gam_pairs[1][:, : 2 * R], gam_rows[:, 1, :])
         nc.sync.dma_start(w_raw[:, 2:, :], w_rows[:, 2:, :])
-        nc.sync.dma_start(gam_t[2][:, :R], gam_rows[:, 2, :])
         nc.sync.dma_start(bet_t[0][:, :R], bet_rows[:, 0, :])
         nc.sync.dma_start(xw[:].bitcast(I32), x_words[0].rearrange("p n t -> p (n t)").bitcast(I32))
 
@@ -85,25 +84,27 @@ def tile_picked_yspade_none_po_kernel(
 
         halves = runs((HALF, HALF))
         gains = [keep.tile([P, S], F32, name=f"gains{t}") for t in range(PACK)]
-        nc.vector.tensor_copy(gains[3][:], gam_t[3][:].indirect(lab_t[:]))
+        nc.vector.tensor_copy(gains[1][:], gam_pairs[0][:, R:].indirect(lab_t[:]))
         nc.vector.tensor_copy(picked_bytes[:], xs[:].indirect(offs_t[:]))
+        nc.sync.dma_start(bet_t[1][:, :R], bet_rows[:, 1, :])
         for q in range(4):
             nc.sync.dma_start(x_bytes[q:P:32, :].bitcast(I32), picked_bytes[8 * q : P : 32, :].bitcast(I32))
-        for t in range(1, PACK):
+        for t in range(2, PACK):
             nc.sync.dma_start(bet_t[t][:, :R], bet_rows[:, t, :])
 
         shifts = [keep.tile([P, S], F32, name=f"shifts{t}") for t in range(3)]
         on_scalar, on_vector = runs((S - SHARED, SHARED))
-        for t in range(2):
-            nc.scalar.activation(gains[t][:], gam_t[t][:].indirect(lab_t[:]), ACT.Copy)
-        nc.scalar.activation(gains[2][:, on_scalar], gam_t[2][:].indirect(picks(on_scalar)), ACT.Copy)
+        nc.gpsimd.tensor_copy(gam_last[:, :R], gam_pairs[1][:, R : 2 * R])
+        for i in range(2):
+            nc.scalar.activation(gains[2 * i][:], gam_pairs[i][:].indirect(lab_t[:]), ACT.Copy)
+        nc.scalar.activation(gains[3][:, on_scalar], gam_last[:].indirect(picks(on_scalar)), ACT.Copy)
         for t in range(2):
             nc.scalar.activation(shifts[t][:], bet_t[t][:].indirect(lab_t[:]), ACT.Copy)
         nc.scalar.activation(shifts[2][:, : THIRD_SHIFTS[0]], bet_t[2][:].indirect(picks(slice(0, THIRD_SHIFTS[0]))), ACT.Copy)
 
         w_bf = keep.tile([P, PACK, P, PACK], BF16, name="w_bf", align_bytes=64)
         nc.vector.tensor_copy(w_bf[:].rearrange("p t m j -> p m j t"), w_raw[:].rearrange("p j (m t) -> p m j t", t=PACK))
-        nc.vector.tensor_copy(gains[2][:, on_vector], gam_t[2][:].indirect(picks(on_vector)))
+        nc.vector.tensor_copy(gains[3][:, on_vector], gam_last[:].indirect(picks(on_vector)))
         w_codes = keep.tile([P, N], U32, name="w_codes", align_bytes=64)
         w_scales = keep.tile([P, N], U8, name="w_scales", align_bytes=64)
         nc.vector.quantize_mx(
@@ -133,22 +134,25 @@ def tile_picked_yspade_none_po_kernel(
         def bank(t, h):
             product(y[:, t, halves[h]], t, halves[h])
 
-        bank_stats = keep.tile([P, PACK, 2, 6], F32, name="bank_stats")
+        bank_stats = keep.tile([P, PACK, 3, 6], F32, name="bank_stats")
 
         def statistics(t, h):
             nc.vector.bn_stats(bank_stats[:, t, h, :], y[:, t, halves[h]])
 
         def aggregate(t):
-            nc.vector.bn_aggr(moments[:, t, :], bank_stats[:, t, :, :].rearrange("p h s -> p (h s)"))
+            pieces = 3 if t == 1 else 2
+            nc.vector.bn_aggr(moments[:, t, :], bank_stats[:, t, :pieces, :].rearrange("p h s -> p (h s)"))
 
         for t, h in ((0, 0), (1, 0), (0, 1), (1, 1), (3, 0), (3, 1)):
             bank(t, h)
         for cols in blocks:
             product(partial_sums, 2, cols, cols == blocks[0], cols == blocks[-1])
         bank(2, 0)
-        for t, h in ((0, 0), (0, 1), (1, 0)):
-            statistics(t, h)
+        for h in range(2):
+            statistics(0, h)
+        nc.vector.bn_stats(bank_stats[:, 1, 0, :], y[:, 1, : HALF // 2])
         aggregate(0)
+        nc.vector.bn_stats(bank_stats[:, 1, 2, :], y[:, 1, HALF // 2 : HALF])
         statistics(1, 1)
         statistics(3, 0)
         aggregate(1)

@@ -27,6 +27,7 @@ STORED = 256
 ON_SCALAR = 4
 CHUNKS = (256, 256, 256, 128, 128)
 WORDS_STORED = (512, 256, 256)
+WORDS_GATHERED = (512, 256, 256)
 
 
 def runs(widths):
@@ -111,7 +112,7 @@ def tile_picked_yspade_none_po_kernel(
             out=w_codes[:].bitcast(FP8X4), scales=w_scales[:], in_=w_bf[:].rearrange("p t m j -> p (t m j)")
         )
         x_codes = keep.tile([P, S], U32, name="x_codes", align_bytes=64)
-        for cols in halves:
+        for cols in runs(WORDS_GATHERED):
             nc.vector.tensor_copy(x_codes[:, cols], xw[:].indirect(offs_t[:, cols.start // 16 : cols.stop // 16]))
 
         y = psum.tile([P, PACK, S], F32, name="y")
@@ -136,14 +137,24 @@ def tile_picked_yspade_none_po_kernel(
 
         bank_stats = keep.tile([P, PACK, 3, 6], F32, name="bank_stats")
 
+        scaled_tile = keep.tile([P, 16 + S], F32, name="scaled_tile")
+        scaled = scaled_tile[:, 16:]
+        last_stats = scaled_tile[:, 4:22]
+
         def statistics(t, h):
-            nc.vector.bn_stats(bank_stats[:, t, h, :], y[:, t, halves[h]])
+            out = last_stats[:, 6 * h : 6 * h + 6] if t == 3 else bank_stats[:, t, h, :]
+            nc.vector.bn_stats(out, y[:, t, halves[h]])
 
         def aggregate(t):
             pieces = 3 if t == 1 else 2
-            nc.vector.bn_aggr(moments[:, t, :], bank_stats[:, t, :pieces, :].rearrange("p h s -> p (h s)"))
+            stats = last_stats if t == 3 else bank_stats[:, t, :pieces, :].rearrange("p h s -> p (h s)")
+            nc.vector.bn_aggr(moments[:, t, :], stats)
 
-        for t, h in ((0, 0), (1, 0), (0, 1), (1, 1), (3, 0), (3, 1)):
+        bank(0, 0)
+        bank(1, 0)
+        for cols in runs(WORDS_GATHERED)[1:]:
+            product(y[:, 0, cols], 0, cols)
+        for t, h in ((1, 1), (3, 0), (3, 1)):
             bank(t, h)
         for cols in blocks:
             product(partial_sums, 2, cols, cols == blocks[0], cols == blocks[-1])
@@ -156,6 +167,7 @@ def tile_picked_yspade_none_po_kernel(
         statistics(1, 1)
         statistics(3, 0)
         aggregate(1)
+        nc.vector.bn_stats(last_stats[:, 6:12], y[:, 3, HALF : HALF + HALF // 2])
         rstd = keep.tile([P, PACK], F32, name="rstd")
         nc.scalar.activation(rstd[:, :1], moments[:, :1, 1], ACT.Abs_reciprocal_sqrt, bias=eps[0][:])
 
@@ -204,21 +216,21 @@ def tile_picked_yspade_none_po_kernel(
                 res(t, cols), gained[t][:, cols], rstd[:, t : t + 1], looked_up(t, cols), ALU.mult, ALU.add
             )
 
-        scaled = keep.tile([P, S], F32, name="scaled")
         for cols in halves:
             nc.gpsimd.tensor_scalar(scaled[:, cols], gains[0][:, cols], rstd[:, 0:1], 0.0, ALU.mult, ALU.add)
         for cols in halves:
             nc.vector.scalar_tensor_tensor(
                 gained[0][:, cols], y[:, 0, cols], moments[:, 0, 0:1], scaled[:, cols], ALU.subtract, ALU.mult
             )
+            if cols == halves[0]:
+                gain(1, halves[0])
         for cols in halves:
             nc.gpsimd.tensor_tensor(res(0, cols), gained[0][:, cols], shifts[0][:, cols], ALU.add)
             nc.sync.dma_start(out_rows[:, 0, cols], res(0, cols))
 
-        statistics(3, 1)
-        gain(1, halves[0])
-        aggregate(3)
+        nc.vector.bn_stats(last_stats[:, 12:], y[:, 3, HALF + HALF // 2 :])
         gain(1, halves[1])
+        aggregate(3)
         gain(2, halves[0])
         nc.scalar.activation(rstd[:, 1:], moments[:, 1:, 1], ACT.Abs_reciprocal_sqrt, bias=eps[1][:])
         last = keep.tile([P, HALF + THIRD_SHIFTS[2]], F32, name="last", tag="after_rstd1")

from contextlib import ExitStack

import concourse.mybir as mybir

F32 = mybir.dt.float32
BF16 = mybir.dt.bfloat16
U32 = mybir.dt.uint32
I32 = mybir.dt.int32
U16 = mybir.dt.uint16
U8 = mybir.dt.uint8
FP8X4 = mybir.dt.float8_e4m3fn_x4
ACT = mybir.ActivationFunctionType
ALU = mybir.AluOpType

K, T, S, N, R = 512, 4096, 1024, 512, 256
P = 128
PACK = 4
HALF = 512
EPS = 1e-4
FLOPS = 2 * K * N * S

SCALAR_W = 1040
VECTOR_W = 1376
THIRD_SHIFTS = (512, 256, 256)
SHARED = 384
STORED = 256
ON_SCALAR = 4
CHUNKS = (256, 256, 256, 128, 128)
WORDS_STORED = (512, 256, 256)
WORDS_GATHERED = (512, 256, 256)


def runs(widths):
    return [slice(sum(widths[:c]), sum(widths[: c + 1])) for c in range(len(widths))]


def tile_picked_yspade_none_po_kernel(
    tc, x_words, x_scales, w1, gam, bet, offs, lab, out_0, out_1, out_2
):
    nc = tc.nc
    with ExitStack() as ctx:
        keep = ctx.enter_context(tc.tile_pool(name="keep", bufs=1))
        shared = ctx.enter_context(tc.tile_pool(name="shared", bufs=1))
        psum = ctx.enter_context(tc.psum_pool(name="psum", bufs=1))

        lab_t = keep.tile([P, S // 16], U16, name="lab_t")
        offs_t = keep.tile([P, S // 16], U16, name="offs_t")
        gam_pairs = [keep.tile([P, R + VECTOR_W], F32, name=f"gam_pair{i}") for i in range(2)]
        gam_last = keep.tile([P, SCALAR_W], F32, name="gam_last")
        table = 4 * SCALAR_W
        xs = shared.tile([P, T], U8, name="xs", offset=table - 32)
        picked_bytes = shared.tile([P, S], U8, name="picked_bytes", offset=3 * table + T - 96)
        bet_at = (0, table + T - 64, 2 * table + T - 64, 3 * table + T + S - 128)
        bet_t = [keep.tile([P, SCALAR_W], F32, name="bet0")]
        bet_t += [shared.tile([P, SCALAR_W], F32, name=f"bet{t}", offset=bet_at[t - 1]) for t in range(1, PACK)]
        xw = keep.tile([P, T], U32, name="xw")
        w_raw = keep.tile([P, PACK, N], F32, name="w_raw")
        gam_rows = gam.rearrange("(p i t) r -> p i (t r)", i=2, t=2)
        bet_rows = bet.rearrange("(p t) r -> p t r", t=PACK)
        w_rows = w1.rearrange("(p j) n -> p j n", j=PACK)

        nc.gpsimd.memset(xs[:, : T // 2].bitcast(I32), 0)
        nc.vector.memset(xs[:, T // 2 :].bitcast(I32), 0)
        x_bytes = keep.tile([P, S], U8, name="x_bytes", align_bytes=64)
        nc.gpsimd.memset(x_bytes[:].bitcast(I32), 0)
        warm = keep.tile([P, 2], F32, name="warm")
        nc.vector.memset(warm[:, 0:1], 1.0)
        nc.scalar.activation(warm[:, 1:2], warm[:, 0:1], ACT.Abs_reciprocal_sqrt)
        eps = [keep.tile([P, 1], F32, name=f"eps{i}", tag=f"after_rstd{i}") for i in range(2)]
        for column in eps:
            nc.vector.tensor_scalar(column[:], warm[:, 0:1], EPS, None, ALU.mult)

        nc.sync.dma_start(gam_pairs[0][:, : 2 * R], gam_rows[:, 0, :])
        nc.sync.dma_start(lab_t[:], lab)
        nc.sync.dma_start(w_raw[:, :2, :], w_rows[:, :2, :])
        nc.sync.dma_start(xs[0:P:8, :].bitcast(I32), x_scales[0].bitcast(I32))
        nc.sync.dma_start(offs_t[:], offs)
        nc.sync.dma_start(gam_pairs[1][:, : 2 * R], gam_rows[:, 1, :])
        nc.sync.dma_start(w_raw[:, 2:, :], w_rows[:, 2:, :])
        nc.sync.dma_start(bet_t[0][:, :R], bet_rows[:, 0, :])
        nc.sync.dma_start(xw[:].bitcast(I32), x_words[0].rearrange("p n t -> p (n t)").bitcast(I32))

        def picks(cols):
            return lab_t[:, cols.start // 16 : cols.stop // 16]

        halves = runs((HALF, HALF))
        gains = [keep.tile([P, S], F32, name=f"gains{t}") for t in range(PACK)]
        nc.vector.tensor_copy(gains[1][:], gam_pairs[0][:, R:].indirect(lab_t[:]))
        nc.vector.tensor_copy(picked_bytes[:], xs[:].indirect(offs_t[:]))
        nc.sync.dma_start(bet_t[1][:, :R], bet_rows[:, 1, :])
        for q in range(4):
            nc.sync.dma_start(x_bytes[q:P:32, :].bitcast(I32), picked_bytes[8 * q : P : 32, :].bitcast(I32))
        for t in range(2, PACK):
            nc.sync.dma_start(bet_t[t][:, :R], bet_rows[:, t, :])

        shifts = [keep.tile([P, S], F32, name=f"shifts{t}") for t in range(3)]
        on_scalar, on_vector = runs((S - SHARED, SHARED))
        nc.gpsimd.tensor_copy(gam_last[:, :R], gam_pairs[1][:, R : 2 * R])
        for i in range(2):
            nc.scalar.activation(gains[2 * i][:], gam_pairs[i][:].indirect(lab_t[:]), ACT.Copy)
        nc.scalar.activation(gains[3][:, on_scalar], gam_last[:].indirect(picks(on_scalar)), ACT.Copy)
        for t in range(2):
            nc.scalar.activation(shifts[t][:], bet_t[t][:].indirect(lab_t[:]), ACT.Copy)
        nc.scalar.activation(shifts[2][:, : THIRD_SHIFTS[0]], bet_t[2][:].indirect(picks(slice(0, THIRD_SHIFTS[0]))), ACT.Copy)

        w_bf = keep.tile([P, PACK, P, PACK], BF16, name="w_bf", align_bytes=64)
        nc.vector.tensor_copy(w_bf[:].rearrange("p t m j -> p m j t"), w_raw[:].rearrange("p j (m t) -> p m j t", t=PACK))
        nc.vector.tensor_copy(gains[3][:, on_vector], gam_last[:].indirect(picks(on_vector)))
        w_codes = keep.tile([P, N], U32, name="w_codes", align_bytes=64)
        w_scales = keep.tile([P, N], U8, name="w_scales", align_bytes=64)
        nc.vector.quantize_mx(
            out=w_codes[:].bitcast(FP8X4), scales=w_scales[:], in_=w_bf[:].rearrange("p t m j -> p (t m j)")
        )
        x_codes = keep.tile([P, S], U32, name="x_codes", align_bytes=64)
        for cols in runs(WORDS_GATHERED):
            nc.vector.tensor_copy(x_codes[:, cols], xw[:].indirect(offs_t[:, cols.start // 16 : cols.stop // 16]))

        y = psum.tile([P, PACK, S], F32, name="y")
        moments = keep.tile([P, PACK, 2], F32, name="moments")

        def product(out, t, cols, start=True, stop=True):
            nc.tensor.matmul_mx(
                out=out,
                lhsT=w_codes[:, t * P : (t + 1) * P].bitcast(FP8X4),
                lhsT_scale=w_scales[:, t * P : (t + 1) * P],
                rhs=x_codes[:, cols].bitcast(FP8X4),
                rhs_scale=x_bytes[:, cols],
                start=start,
                stop=stop,
            )

        partial_sums = y[:, 2, HALF : HALF + P]
        blocks = runs((P,) * (S // P))

        def bank(t, h):
            product(y[:, t, halves[h]], t, halves[h])

        bank_stats = keep.tile([P, PACK, 3, 6], F32, name="bank_stats")

        scaled_tile = keep.tile([P, 16 + S], F32, name="scaled_tile")
        scaled = scaled_tile[:, 16:]
        last_stats = scaled_tile[:, 4:22]

        def statistics(t, h):
            out = last_stats[:, 6 * h : 6 * h + 6] if t == 3 else bank_stats[:, t, h, :]
            nc.vector.bn_stats(out, y[:, t, halves[h]])

        def aggregate(t):
            pieces = 3 if t == 1 else 2
            stats = last_stats if t == 3 else bank_stats[:, t, :pieces, :].rearrange("p h s -> p (h s)")
            nc.vector.bn_aggr(moments[:, t, :], stats)

        bank(0, 0)
        bank(1, 0)
        for cols in runs(WORDS_GATHERED)[1:]:
            product(y[:, 0, cols], 0, cols)
        for t, h in ((1, 1), (3, 0), (3, 1)):
            bank(t, h)
        for cols in blocks:
            product(partial_sums, 2, cols, cols == blocks[0], cols == blocks[-1])
        bank(2, 0)
        for h in range(2):
            statistics(0, h)
        nc.vector.bn_stats(bank_stats[:, 1, 0, :], y[:, 1, : HALF // 2])
        aggregate(0)
        nc.vector.bn_stats(bank_stats[:, 1, 2, :], y[:, 1, HALF // 2 : HALF])
        statistics(1, 1)
        statistics(3, 0)
        aggregate(1)
        nc.vector.bn_stats(last_stats[:, 6:12], y[:, 3, HALF : HALF + HALF // 2])
        rstd = keep.tile([P, PACK], F32, name="rstd")
        nc.scalar.activation(rstd[:, :1], moments[:, :1, 1], ACT.Abs_reciprocal_sqrt, bias=eps[0][:])

        first, second, third = runs(THIRD_SHIFTS)
        after_first = keep.tile([P, S + THIRD_SHIFTS[1]], F32, name="after_first", tag="after_rstd0")
        unused = after_first[:, :S]
        nc.scalar.activation(after_first[:, S:], bet_t[2][:].indirect(picks(second)), ACT.Copy)
        nc.scalar.activation(unused[:, :P], partial_sums, ACT.Copy, scale=1.0 / S, accum_out=moments[:, 2, 0:1])
        bank(2, 1)
        squares = keep.tile([P, 2], F32, name="squares", tag="after_squares")
        for h, cols in enumerate(halves):
            nc.scalar.activation(
                unused[:, cols], y[:, 2, cols], ACT.Square, scale=-1.0, bias=moments[:, 2, 0:1], accum_out=squares[:, h : h + 1]
            )
        shares = keep.tile([P, 2], F32, name="shares")
        nc.scalar.activation(shares[:], squares[:], ACT.Copy, scale=1.0 / S, accum_out=moments[:, 2, 1:2])
        middle = keep.tile([P, HALF], F32, name="middle", tag="after_squares")
        nc.scalar.activation(middle[:], bet_t[3][:].indirect(picks(halves[0])), ACT.Copy)

        res_halves = [keep.tile([P, PACK, HALF], F32, name=f"res{h}") for h in range(2)]

        def res(tiles, cols):
            h = cols.start // HALF
            return res_halves[h][:, tiles, cols.start - h * HALF : cols.stop - h * HALF]

        gained = [keep.tile([P, S], F32, name=f"gained{t}") for t in range(PACK)]
        out_rows = out_0.rearrange("(p t) j -> p t j", t=PACK)
        word_rows = out_1[0].rearrange("p n t -> p (n t)").bitcast(I32)

        def gain(t, cols):
            nc.vector.scalar_tensor_tensor(
                gained[t][:, cols], y[:, t, cols], moments[:, t, 0:1], gains[t][:, cols], ALU.subtract, ALU.mult
            )

        def looked_up(t, cols):
            if t == 3:
                return middle[:, cols] if cols.stop <= HALF else last[:, cols.start - HALF : cols.stop - HALF]
            if t == 2 and cols.start >= third.start:
                return last[:, HALF + cols.start - third.start : HALF + cols.stop - third.start]
            if t == 2 and cols.start >= second.start:
                return after_first[:, S + cols.start - second.start : S + cols.stop - second.start]
            return shifts[t][:, cols]

        def shift(t, cols):
            nc.vector.scalar_tensor_tensor(
                res(t, cols), gained[t][:, cols], rstd[:, t : t + 1], looked_up(t, cols), ALU.mult, ALU.add
            )

        for cols in halves:
            nc.gpsimd.tensor_scalar(scaled[:, cols], gains[0][:, cols], rstd[:, 0:1], 0.0, ALU.mult, ALU.add)
        for cols in halves:
            nc.vector.scalar_tensor_tensor(
                gained[0][:, cols], y[:, 0, cols], moments[:, 0, 0:1], scaled[:, cols], ALU.subtract, ALU.mult
            )
            if cols == halves[0]:
                gain(1, halves[0])
        for cols in halves:
            nc.gpsimd.tensor_tensor(res(0, cols), gained[0][:, cols], shifts[0][:, cols], ALU.add)
            nc.sync.dma_start(out_rows[:, 0, cols], res(0, cols))

        nc.vector.bn_stats(last_stats[:, 12:], y[:, 3, HALF + HALF // 2 :])
        gain(1, halves[1])
        aggregate(3)
        gain(2, halves[0])
        nc.scalar.activation(rstd[:, 1:], moments[:, 1:, 1], ACT.Abs_reciprocal_sqrt, bias=eps[1][:])
        last = keep.tile([P, HALF + THIRD_SHIFTS[2]], F32, name="last", tag="after_rstd1")
        nc.scalar.activation(last[:, :HALF], bet_t[3][:].indirect(picks(halves[1])), ACT.Copy)
        nc.scalar.activation(last[:, HALF:], bet_t[2][:].indirect(picks(third)), ACT.Copy)

        out_codes = keep.tile([P, S], U32, name="out_codes", align_bytes=64)
        out_scales = keep.tile([P, S], U8, name="out_scales", align_bytes=64)
        res_bf = keep.tile([P, S, PACK], BF16, name="res_bf", align_bytes=64)

        def quantise(cols):
            nc.vector.quantize_mx(
                out=out_codes[:, cols].bitcast(FP8X4),
                scales=out_scales[:, cols],
                in_=res_bf[:, cols, :].rearrange("p n t -> p (n t)"),
            )

        def finish_second(half):
            shift(1, half)
            nc.sync.dma_start(out_rows[:, 1, half], res(1, half))

        def finish(c):
            cols = chunks[c]
            for t in (2, 3):
                shift(t, cols)
            copy = nc.scalar.copy if c < ON_SCALAR else nc.vector.tensor_copy
            copy(
                res_bf[:, cols, :].rearrange("p (c i) t -> p c t i", i=4),
                res(slice(0, PACK), cols).rearrange("p t (c i) -> p c t i", i=4),
            )
            if cols.stop % STORED == 0:
                stored = slice(cols.stop - STORED, cols.stop)
                nc.sync.dma_start(out_rows[:, 2:, stored], res(slice(2, PACK), stored))

        chunks = runs(CHUNKS)
        quarters = runs((S // 4,) * 4)
        gain(3, halves[0])
        finish_second(halves[0])
        finish(0)
        gain(2, quarters[2])
        finish(1)
        gain(3, quarters[2])
        finish_second(halves[1])
        quantise(chunks[0])
        finish(2)
        for t in (2, 3):
            gain(t, quarters[3])
        quantise(chunks[1])
        finish(3)
        quantise(chunks[2])
        finish(4)
        for cols in chunks[3:]:
            quantise(cols)
        for cols in runs(WORDS_STORED):
            nc.sync.dma_start(word_rows[:, cols], out_codes[:, cols].bitcast(I32))
        for q in range(4):
            nc.scalar.dma_start(out_2[0, q:16:4, :].bitcast(I32), out_scales[q:P:32, :].bitcast(I32))
